import numpy as np, ml_dtypes
CORES = [6,15,38,47]
N = 4
BF = ml_dtypes.bfloat16
def gentries(a):
    return np.ascontiguousarray(a.reshape(8, 16, -1).transpose(0, 2, 1)).reshape(8, -1)
def gtable(e):
    e = np.asarray(e); return np.ascontiguousarray(e.reshape(8, -1, 16).transpose(0, 2, 1)).reshape(128, -1).astype(np.int32)
V, S, L, M, C, A, B = 2560, 2048, 3, 4, 128, 6, 20
W = V + C * M
def parts(rng):
    c = rng.integers(0, 16, (N, 8, 12, V)); o = np.argsort(rng.random((N, 8, 1, V)), axis=-1)
    i = np.minimum((V * rng.random((N, 8, 2, V)) ** 1.5).astype(np.int64), V - 1)
    t = np.take_along_axis(np.broadcast_to(o, (N, 8, 2, V)), i, 3)
    t = np.where(rng.random(t.shape) < 0.04, np.arange(V), t)
    n = np.exp2(9 * rng.random((N, 8, 2, V))).astype(np.int64) - 1
    s = rng.integers(0, V, (N, 8, S)); x = rng.integers(0, 16, (N, 8, 12, S))
    e = np.where(np.argsort(rng.random((N, 8, 12)), axis=-1) % 2 == 1, 1, -1)
    return c, t, n, s, x, e
def pack(c, t, n, s, x, e):
    return {"recs": np.concatenate([c, t, n], axis=2).reshape(N, 128, V).astype(np.int32), "st0": np.stack([gtable(a) for a in s]),
            "cx0": np.concatenate([x, np.zeros((N, 8, 4, S), np.int64)], axis=2).reshape(N, 128, S).astype(np.float32).astype(BF),
            "sg": np.concatenate([e, np.zeros((N, 8, 4), np.int64)], axis=2).reshape(N, 128, 1).astype(np.int32)}
def setup_inputs(rng):
    return pack(*parts(rng))
def setup_inputs_full(rng):
    c, t, n, s, x, e = parts(rng); n = rng.integers(400, 501, n.shape); h = V // M
    for g in range(8):
        base = rng.permutation(V)
        for r in range(N):
            for m in range(M):
                blk = rng.permutation(base[m * h:(m + 1) * h])
                t[r, g][:, blk] = np.roll(blk, -1)
                s[r, g, m * C:(m + 1) * C] = blk[:C] if g % 2 == 0 else rng.permutation(blk)[:C]
    return pack(c, t, n, s, x, e)
def setup_inputs_meet(rng):
    c, t, n, s, x, e = parts(rng); n = n // 4 + 60
    hub = np.stack([rng.permutation(V)[:24] for g in range(8)])
    t = np.where(rng.random(t.shape) < 0.85, hub[np.arange(8)[None, :, None, None], rng.integers(0, 24, t.shape)], t)
    for r in range(N):
        for g in range(8): t[r, g][:, hub[g, :6]] = hub[g, :6]
    s[:, 0] = s[:, 0, :1].copy(); x[:, 0] = x[:, 0, :, :1].copy(); t[:, 1] = np.arange(V)
    for r in range(N):
        o = rng.permutation(V); h = o[L * C]
        t[r, 4][:, o[:(L - 1) * C]] = o[C:L * C]; t[r, 4][:, o[(L - 1) * C:L * C]] = h
        n[r, 4][:, h] = rng.integers(400, 501, 2); s[r, 4, :C] = rng.permutation(o[:C])
    return pack(c, t, n, s, x, e)
def setup_inputs_ties(rng):
    c, t, n, s, x, e = parts(rng); c[:, ::2] = c[:, ::2] & 1; x[:, ::2] = x[:, ::2] & 1
    a = A - 2 + rng.integers(0, 4, (N, 8, V)); b = A - 2 + rng.integers(0, 4, (N, 8, V))
    b = np.where(rng.random((N, 8, V)) < 0.6, A + B - a + rng.integers(-3, 4, (N, 8, V)), b)
    turn = rng.random((N, 8, V)) < 0.5
    n = np.stack([np.where(turn, b, a), np.where(turn, a, b)], axis=2)
    o = np.argsort(rng.random((N, 8, 1, V)), axis=-1)[..., :3 * C]
    t = np.take_along_axis(np.broadcast_to(o, (N, 8, 2, 3 * C)), rng.integers(0, 3 * C, t.shape), 3)
    return pack(c, t, n, s, x, e)
def setup_inputs_ahead(rng):
    c, t, n, s, x, e = parts(rng); n = rng.integers(300, 401, n.shape); n[1::2] = 0
    t[:, 2] = np.where(rng.random((N, 2, V)) < 0.5, (V - 1) * rng.integers(0, 2, (N, 2, V)), t[:, 2])
    s[:, 3] = (V - 1) * rng.integers(0, 2, (N, S))
    return pack(c, t, n, s, x, e)
def setup_inputs_spread(rng):
    c, t, n, s, x, e = parts(rng)
    c = np.minimum((np.exp2(4 * rng.random((N, 8, 1, V))) * rng.random((N, 8, 12, V))).astype(np.int64), 15); c[rng.random(c.shape) < 0.02] = 15
    x = np.minimum((np.exp2(4 * rng.random((N, 8, 1, S))) * rng.random((N, 8, 12, S))).astype(np.int64), 15)
    t = np.minimum((V * rng.random(t.shape) ** np.exp2(rng.integers(-1, 3, (N, 8, 1, 1)))).astype(np.int64), V - 1)
    n = np.minimum(np.exp2(12 * rng.random(n.shape)).astype(np.int64), 4095); n[rng.random(n.shape) < 0.1] = 0; n[rng.random(n.shape) < 0.01] = 4095
    e = np.where(rng.random(e.shape) < 0.5, 1, -1); e[:, 1] = 1; e[:, 6] = -1
    for g, a in ((2, 1), (5, -1)): e[:, g] = np.where(np.argsort(rng.random((N, 12)), axis=-1) < 10, a, -a)
    for g in (1, 2, 5, 6):
        c[:, g] = np.where(rng.random((N, 1, V)) < 0.5, rng.integers(14, 16, (N, 12, V)), c[:, g])
        x[:, g] = np.where(rng.random((N, 1, S)) < 0.5, rng.integers(14, 16, (N, 12, S)), x[:, g])
    n[:, 3] = rng.integers(4000, 4096, (N, 2, V))
    return pack(c, t, n, s, x, e)
def check_inputs(d):
    bad = []
    a = np.asarray(d["recs"]).reshape(-1, 8, 16, V)
    for k, i, j, hi in (("statistics", 0, 12, 15), ("transitions", 12, 14, V - 1), ("counts", 14, 16, 4095)):
        if np.min(a[:, :, i:j]) < 0 or np.max(a[:, :, i:j]) > hi: bad.append("range of the " + k)
    if np.min(d["st0"]) < 0 or np.max(d["st0"]) > V - 1: bad.append("range of st0")
    x = np.asarray(d["cx0"]).astype(np.float32).reshape(-1, 8, 16, S)
    if not np.all((x >= 0) & (x <= 15) & (x == np.floor(x))): bad.append("cx0 holds whole numbers from 0 to 15")
    if np.any(x[:, :, 12:] != 0): bad.append("rows of 0 of cx0")
    e = np.asarray(d["sg"]).reshape(-1, 8, 16)
    if not np.all(np.abs(e[:, :, :12]) == 1): bad.append("sg holds 1 and -1")
    if np.any(e[:, :, 12:] != 0): bad.append("rows of 0 of sg")
    return bad
def reference(recs, st0, cx0, sg):
    p = np.zeros((N, 8, 16, W), np.int64); p[..., :V] = recs.astype(np.int64).reshape(N, 8, 16, V)
    s = np.stack([gentries(a) for a in st0]).astype(np.int64)
    x = cx0.astype(np.float32).astype(np.int64).reshape(N, 8, 16, S)[:, :, :12].copy()
    e = sg.astype(np.int64).reshape(N, 8, 16, 1)[:, :, :12]
    free = np.full((N, 8), V, np.int64)
    for v in range(M):
        for q in range(N):
            r = (q - v) % N
            for step in range(L):
                rec = np.take_along_axis(p[q], s[r][:, None, :], 2)
                b = (np.sum(e[q] * rec[:, :12] * x[r], axis=1) > 0).astype(np.int64)
                x[r] = (x[r] + rec[:, :12]) >> 1
                old = s[r].copy(); s[r] = np.where(b == 1, rec[:, 13], rec[:, 12])
            lo = C * v
            for g in range(8):
                pg = p[q, g]; so = old[g, lo:lo + C]; bo = b[g, lo:lo + C]; sn = s[r, g, lo:lo + C].copy()
                w = np.sort(np.unique(so, return_index=True)[1])
                pg[14 + bo[w], so[w]] += 1
                w = w[np.sort(np.unique(sn[w], return_index=True)[1])]
                n = pg[14 + bo[w], so[w]]
                ok = (sn[w] != so[w]) & (n >= A) & (pg[14, sn[w]] + pg[15, sn[w]] - n >= B)
                w = w[ok]; k = len(w); new = free[q, g] + np.arange(k)
                t = pg[:, sn[w]]
                pg[:12, new] = (t[:12] + x[r, g][:, lo + w]) >> 1
                pg[12:14, new] = t[12:14]
                pg[14:16, new] = t[14:16] >> 1
                pg[14:16, sn[w]] = t[14:16] - (t[14:16] >> 1)
                pg[12 + bo[w], so[w]] = new
                s[r, g, lo + w] = new; free[q, g] += k
    yx = np.zeros((N, 8, 16, S), np.float32); yx[:, :, :12] = x
    return {"yp": p.reshape(N, 128, W).astype(np.float32), "ys": np.stack([gtable(a) for a in s]).astype(np.float32), "yx": yx.reshape(N, 128, S).astype(BF)}

@@ -1,0 +1,532 @@
+import numpy as np
+from concourse.mybir import AluOpType as ALU, ActivationFunctionType as ACT
+
+V0, NS, NV, WD_ = 2560, 2048, 4, 3200
+DUMMY = 3072
+CH = [(0, 512), (512, 512), (1024, 1024)]
+POS = [0, 2, 4, 5, 1, 3, 6, 7, 8, 9, 10, 11, 12, 13, 14, 15]
+RUNS = [[(0, 0, 1), (1, 2, 1), (2, 4, 2)], [(4, 1, 1), (5, 3, 1), (6, 6, 2)], [(8, 8, 4)], [(12, 12, 4)]]
+MAGIC = 12582912.0
+BIG = 4096.0
+OFF = 1536.0
+
+
+def _sb(cols, dtype):
+    return ("sbuf", [128] + (cols if isinstance(cols, list) else [cols]), dtype)
+
+
+SCRATCH = {}
+for _d, _l in (("int32", dict(R=V0, STI=128, SGI=4, PC=12)),
+               ("uint16", dict(L1=128, L2=128, IX1=16, IX2=16)),
+               ("float16", dict(Z0=[68, 4], Z1=[68, 4], Z2=[34, 8], EYH=128)),
+               ("bfloat16", dict(W=WD_, ID=WD_, YB=1024, XS=NS, CG=NS, PR=NS, SN=256, SEL=1024,
+                                 NSEL=512, TRI=1024, BE=256, S1=128, S2=128, SW=128, SD=128, WV=32, G8=8, M2=128, M3=128, MW=132, MT=512,
+                                 OB=128, TB=128, WB=128, ONE=32, CP=16, G1=128, G2=128, NB=128, KP=128, WT=128, WDN=128, YY=128, FL=256,
+                                 E1=1024, E2=1024)),
+               ("float32", dict(CN=WD_, THC=128, IO=256, COL=32, R16=16, HM=16, IG=128, IR=128, M1=128, M4=128, WN=256, THR=256,
+                                DUM=8, ST=16, MD=8, A2=16, NE=8, FT=16, OO=32, FR=40, GS=128, GT=128, GM=128, MB=128,
+                                H0=128, HF=128, YS=128, OT=512, ON=512))):
+    for _n, _c in _l.items():
+        SCRATCH[_n] = _sb(_c, _d)
+for _v in range(NV + 1):
+    SCRATCH["X%d" % _v] = _sb(NS, "bfloat16")
+    SCRATCH["S%d_" % _v] = _sb(128, "uint16")
+for _v in range(NV):
+    SCRATCH["U%d" % _v] = _sb(128, "uint16")
+for _n in ("PS0", "PS1", "PS2", "PS3", "PVa", "PVb"):
+    SCRATCH[_n] = ("psum", [128, 512], "float32")
+for _n in ("PD0", "PD1"):
+    SCRATCH[_n] = ("psum", [128, 4, 128], "float32")
+
+SEMAPHORES = (["qV", "qA", "qP", "qG", "sent", "outs", "stat", "lsg", "lst"] + ["lr%d" % i for i in range(5)] + ["lx%d" % i for i in range(4)]
+              + ["ax%d_%d" % (v, p) for v in range(1, NV + 1) for p in range(4)] + ["as%d_%d" % (v, c) for v in range(1, NV + 1) for c in range(3)])
+
+PAR = {"round_v": 0.0, "cyc": 0.001, "pec": 0.0005, "gat": 1.56, "sca": 3.8, "hop": 0.12, "lx": 5.0, "ls": 3.5, "tries": 1500, "jit": 0.5}
+
+
+def build(T, topo, core, nxt):
+    ops = []
+    CYC, PEC, GAT, SCA = PAR["cyc"], PAR["pec"], PAR["gat"], PAR["sca"]
+
+    def op(q, cost, rd, wr, fn, sem=None, n=1, lat=0.0):
+        bank = "a" if any(k in ("pv0", "pv1", "pvt") for k in wr) else None
+        ops.append({"q": q, "cost": cost, "rd": rd, "wr": wr, "fn": fn, "sem": sem, "n": n, "lat": lat, "bank": bank})
+
+    def vc(n, k=1.0):
+        return 0.05 + max(64, n * k) * CYC
+
+    def ts(out, in0, s1, s2, o0, o1, n, rd, wr, k=1.0):
+        if o1 is None:
+            op("V", vc(n, k), rd, wr, lambda g: g.vector.tensor_scalar(out, in0, s1, None, o0))
+        else:
+            op("V", vc(n, k), rd, wr, lambda g: g.vector.tensor_scalar(out, in0, s1, s2, o0, o1))
+
+    def tt(out, a, b, o, n, rd, wr, k=1.0):
+        op("V", vc(n, k), rd, wr, lambda g: g.vector.tensor_tensor(out, a, b, o))
+
+    def cp(out, a, n, rd, wr, k=1.0):
+        op("V", vc(n, k), rd, wr, lambda g: g.vector.tensor_copy(out, a))
+
+    def ac(out, a, f, bias, scale, n, rd, wr, k=1.0):
+        op("A", 0.02 + vc(n, k), rd, wr, lambda g: g.scalar.activation(out, a, f, bias=bias, scale=scale))
+
+    def gat(out, a, n, rd, wr):
+        op("A", 0.02 + vc(n, GAT), rd, wr, lambda g: g.scalar.activation(out, a, ACT.Copy))
+
+    def mm(lst, cyc, rd, wr):
+        def fn(g):
+            r = None
+            for (o, l, rh, st, sp) in lst:
+                r = g.tensor.matmul(o, l, rh, st, sp)
+            return r
+        op("P", 0.05 + cyc * PEC, rd, wr, fn)
+
+    def dma(q, pairs, sem, rd, wr, lat):
+        def fn(g):
+            e = g.sync if q == "S" else g.scalar
+            for (o, i) in pairs:
+                e.dma_start(o, i).then_inc(T.sem[sem], 16)
+        op(q, 0.06 * len(pairs), rd, wr, fn, sem=sem, n=16 * len(pairs), lat=lat)
+
+    rid, pid = topo.addr(nxt)[0], topo.addr(nxt)[1]
+    mask = topo.mask(core, nxt)
+    neng = len(topo.engines(core, nxt))
+
+    def send(dst, src, sem, rd, wr, lat):
+        op("G", 0.5, rd, wr, lambda g: g.remote_dma(dst, src, T.sem[sem], T.sem.sent, pid, rid, mask), sem=sem, n=neng, lat=lat)
+
+    def iota(out, pat, base, cm, n, wr, flag=True):
+        if flag:
+            op("G", 0.15 + 2 * n * CYC, [], wr, lambda g: g.iota(out, pat, base, cm, allow_small_or_imprecise_dtypes=True))
+        else:
+            op("G", 0.15 + 2 * n * CYC, [], wr, lambda g: g.iota(out, pat, base, cm))
+
+    def ms(out, val, n, wr):
+        iota(out, [[0, n]], int(val), 0, n, wr)
+
+    def sel(B, pat, o, fill, base, cm, n, k):
+        op("G", 0.2 + 2 * n * CYC, [k], [k], lambda g: g.affine_select(B, B, pat, o, fill, base, cm))
+
+    C = lambda i: T.COL[:, i:i + 1]
+    SL = lambda v: T["S%d_" % v]
+    for c in range(5):
+        dma("S" if c % 2 == 0 else "A", [(T.R[:, 512 * c:512 * c + 512], T.recs[:, 512 * c:512 * c + 512])], "lr%d" % c, [], ["R%d" % c], 2.2 + 0.9 * c)
+    dma("A", [(T.SGI[:, 0:1], T.sg[:])], "lsg", [], ["SGI"], 2.0)
+    dma("S", [(T.STI[:], T.st0[:])], "lst", [], ["STI"], 3.0)
+    for p in range(4):
+        dma("S", [(T.XS[:, 128 * a:128 * (a + k)], T.cx0[:, 128 * b:128 * (b + k)]) for (a, b, k) in RUNS[p]], "lx%d" % p, [], ["XS%d" % p], 5.5 + 0.5 * p)
+    iota(T.PC[:, 0:1], [[0, 1]], 0, 1, 1, ["PC0"], False)
+    iota(T.IO[:], [[1, 256]], 0, 0, 256, ["IO"])
+    iota(T.IG[:], [[1, 8], [0, 16]], 0, 0, 128, ["IG"])
+    iota(T.IR[:], [[0, 8], [1, 16]], 0, 0, 128, ["IR"])
+    iota(T.MD[:], [[16, 8]], DUMMY - int(OFF), 0, 8, ["MD"])
+    for (B, pat, n, f, k) in ((T.SEL, [[-16, 8], [0, 128]], 1024, 1.0, "SEL"), (T.NSEL, [[0, 4], [-16, 8], [0, 16]], 512, -1.0, "NSEL")):
+        ms(B[:], 0, n, [k])
+        for r in (12, 14):
+            sel(B[:], pat, ALU.not_equal, f, -r, 1, n, k)
+    ms(T.TRI[:], 0, 1024, ["TRI"])
+    sel(T.TRI[:], [[16, 8], [0, 8], [1, 16]], ALU.is_gt, 0.5, 0, -1, 1024, "TRI")
+    for h, f in ((0, BIG), (1, -BIG)):
+        ms(T.BE[:, 128 * h:128 * h + 128], 0, 128, ["BE%d" % h])
+        sel(T.BE[:, 128 * h:128 * h + 128], [[-1, 128]], ALU.not_equal, f, 0, 1, 128, "BE%d" % h)
+    ms(T.CN[:, V0:WD_], 0, 640, ["CN5"])
+    ms(T.ONE[:, 0:2], BIG, 2, ["ONEa"])
+    ms(T.ONE[:, 2:4], 1, 2, ["ONEb"])
+    ms(T.ONE[:, 8:16], -OFF / 16, 8, ["ONEc"])
+    ms(T.CP[:], 0, 16, ["CP"])
+    ms(T.FR[:, 0:1], V0 - BIG, 1, ["FR0"])
+    op("V", vc(64), [], ["THCa"], lambda g: g.vector.memset(T.THC[:, 0:64], 0.125))
+    op("V", vc(64), [], ["THCb"], lambda g: g.vector.memset(T.THC[:, 64:128], -0.125))
+    ts(T.PC[:, 4:5], T.PC[:, 0:1], 4, None, ALU.arith_shift_right, None, 1, ["PC0"], ["PC4"])
+    ts(T.PC[:, 8:9], T.PC[:, 0:1], 15, None, ALU.bitwise_and, None, 1, ["PC0"], ["PC8"])
+    (P_, G_, R_, LT12, LT14, GE14, GE12, CH_, C1, CW, CA, CB, CR, E_, M1213, M1214, SIG, TAU, ODD, FW, FW2, PP2, PM2, NO13, NO15, PO13) = range(26)
+    k_ = lambda *a: ["c%d" % i for i in a]
+    r16 = lambda i: T.R16[:, i:i + 1]
+    IO = T.IO[:, 0:128]
+    MT = lambda i: T.MT[:, 128 * i:128 * i + 128]
+    cp(C(P_), T.PC[:, 0:1], 1, ["PC0"], k_(P_))
+    cp(C(G_), T.PC[:, 4:5], 1, ["PC4"], k_(G_))
+    cp(C(R_), T.PC[:, 8:9], 1, ["PC8"], k_(R_))
+    cp(C(E_), T.SGI[:, 0:1], 1, ["SGI"], k_(E_))
+    ts(C(LT14), C(R_), 14.0, None, ALU.is_lt, None, 1, k_(R_), k_(LT14))
+    ts(T.M1[:], IO, C(P_), C(LT14), ALU.is_equal, ALU.mult, 128, ["IO"] + k_(P_, LT14), ["M1"])
+    ts(T.R16[:], T.IO[:, 0:16], C(R_), None, ALU.is_equal, None, 16, ["IO"] + k_(R_), ["R16"])
+    tt(C(M1213), r16(12), r16(13), ALU.add, 1, ["R16"], k_(M1213))
+    ts(C(NO13), C(M1213), -OFF, None, ALU.mult, None, 1, k_(M1213), k_(NO13))
+    ts(C(PP2), C(P_), 2.0, None, ALU.add, None, 1, k_(P_), k_(PP2))
+    ts(MT(0), IO, C(PP2), C(M1213), ALU.is_equal, ALU.mult, 128, ["IO"] + k_(PP2, M1213), ["MT0"])
+    ts(MT(1), IO, C(P_), C(M1213), ALU.is_equal, ALU.mult, 128, ["IO"] + k_(P_, M1213), ["MT1"])
+    tt(T.M2[:], MT(0), MT(1), ALU.subtract, 128, ["MT0", "MT1"], ["M2"])
+    ts(C(LT12), C(R_), 12.0, None, ALU.is_lt, None, 1, k_(R_), k_(LT12))
+    ts(C(GE14), C(R_), 14.0, None, ALU.is_ge, None, 1, k_(R_), k_(GE14))
+    ts(C(NO15), C(R_), 14.0, -OFF, ALU.is_ge, ALU.mult, 1, k_(R_), k_(NO15))
+    ts(C(GE12), C(R_), 12.0, None, ALU.is_ge, None, 1, k_(R_), k_(GE12))
+    ts(C(CH_), C(R_), 12.0, 0.5, ALU.is_lt, ALU.mult, 1, k_(R_), k_(CH_))
+    ts(C(C1), C(GE12), 1.0 / 128, C(CH_), ALU.mult, ALU.add, 1, k_(GE12, CH_), k_(C1))
+    tt(C(CW), C(CH_), C(GE12), ALU.add, 1, k_(CH_, GE12), k_(CW))
+    ts(C(CA), r16(12), -0.5, None, ALU.mult, None, 1, ["R16"], k_(CA))
+    ts(C(CB), r16(13), -1.0 / 512, C(CA), ALU.mult, ALU.add, 1, ["R16"] + k_(CA), k_(CB))
+    ts(C(CR), C(LT12), 0.75, 127.0, ALU.mult, ALU.add, 1, k_(LT12), k_(CR))
+    tt(C(M1214), r16(12), r16(14), ALU.add, 1, ["R16"], k_(M1214))
+    tt(C(ODD), r16(13), r16(15), ALU.add, 1, ["R16"], k_(ODD))
+    tt(C(SIG), C(ODD), C(M1214), ALU.subtract, 1, k_(ODD, M1214), k_(SIG))
+    ts(C(TAU), C(M1214), -0.25, C(LT12), ALU.mult, ALU.add, 1, k_(M1214, LT12), k_(TAU))
+    ts(T.EYH[:], IO, C(P_), None, ALU.is_equal, None, 128, ["IO"] + k_(P_), ["EYH"])
+    ts(T.S2[:], IO, C(P_), C(CH_), ALU.is_equal, ALU.mult, 128, ["IO"] + k_(P_, CH_), ["S2"])
+    ts(T.SW[:], IO, C(P_), C(CW), ALU.is_equal, ALU.mult, 128, ["IO"] + k_(P_, CW), ["SW"])
+    ts(T.OB[:], T.IG[:], C(G_), None, ALU.is_equal, None, 128, ["IG"] + k_(G_), ["OB"])
+    ts(T.G2[:], T.IR[:], 12.0, None, ALU.is_lt, None, 128, ["IR"], ["G2"])
+    tt(T.KP[:], T.G2[:], T.OB[:], ALU.mult, 128, ["G2", "OB"], ["KP"])
+    ts(MT(2), T.KP[:], C(CA), None, ALU.mult, None, 128, ["KP"] + k_(CA), ["MT2"], 0.5)
+    ts(MT(3), IO, C(P_), C(C1), ALU.is_equal, ALU.mult, 128, ["IO"] + k_(P_, C1), ["MT3"])
+    tt(T.S1[:], MT(2), MT(3), ALU.add, 128, ["MT2", "MT3"], ["S1"])
+    ts(T.YY[:], T.KP[:], C(CB), None, ALU.mult, None, 128, ["KP"] + k_(CB), ["YY"], 0.5)
+    tt(T.SD[:], T.YY[:], T.S2[:], ALU.add, 128, ["YY", "S2"], ["SD"])
+    ts(T.G8[:], T.IO[:, 0:8], C(G_), None, ALU.is_equal, None, 8, ["IO"] + k_(G_), ["G8"])
+    for kind, col, f in ((0, E_, 1.0), (1, E_, -1.0), (2, ODD, 1.0), (3, M1214, 1.0)):
+        ts(T.WV[:, 8 * kind:8 * kind + 8], T.G8[:], C(col), f, ALU.mult, ALU.mult, 8, ["G8"] + k_(col), ["WV%d" % kind])
+    WVK = ["WV%d" % i for i in range(4)]
+    for c in range(3):
+        cp(T["Z%d" % c][:], T.CN[:, V0:V0 + 272], 272, ["CN5"], ["Z%d" % c])
+    ac(T.W[:, V0:WD_], T.CN[:, V0:WD_], ACT.Identity, C(NO15), 1.0, 640, ["CN5"] + k_(NO15), ["W5"])
+    ts(T.OO[:, 0:16], T.IO[:, 0:16], 256.0, C(GE14), ALU.mult, ALU.mult, 16, ["IO"] + k_(GE14), ["OOa", "OOb"])
+    ts(T.HM[:], T.OO[:, 0:16], C(NO15), None, ALU.add, None, 16, ["OOa", "OOb"] + k_(NO15), ["HM"])
+    for a in range(13):
+        w = min(256, WD_ - 256 * a)
+        ac(T.ID[:, 256 * a:256 * a + w], T.IO[:, 0:w], ACT.Identity, T.HM[:, a:a + 1], C(M1213), w, ["IO", "HM"] + k_(M1213), ["ID%d" % a])
+    IDK = ["ID%d" % a for a in range(13)]
+    ts(T.WB[:], T.IG[:], C(G_), C(E_), ALU.is_equal, ALU.mult, 128, ["IG"] + k_(G_, E_), ["WB"])
+    ts(T.G1[:], T.IR[:], C(R_), None, ALU.is_gt, None, 128, ["IR"] + k_(R_), ["G1"])
+    tt(T.TB[:], T.G1[:], T.OB[:], ALU.mult, 128, ["G1", "OB"], ["TB"])
+    ts(T.WN[:, 0:128], T.IG[:], C(G_), C(GE14), ALU.is_equal, ALU.mult, 128, ["IG"] + k_(G_, GE14), ["WNa"])
+    ac(T.WN[:, 128:256], T.WN[:, 0:128], ACT.Copy, 0.0, -1.0, 128, ["WNa"], ["WNb"])
+    ts(T.GS[:], T.IR[:], C(R_), 65536.0, ALU.not_equal, ALU.mult, 128, ["IR"] + k_(R_), ["GS"])
+    ac(T.THR[:, 0:128], T.GS[:], ACT.Identity, 5.0, -1.0, 128, ["GS"], ["THRa"])
+    ac(T.THR[:, 128:256], T.GS[:], ACT.Identity, 21.0, -1.0, 128, ["GS"], ["THRb"])
+    ts(T.DUM[:], T.MD[:], C(R_), None, ALU.add, None, 8, ["MD"] + k_(R_), ["DUM"])
+    for c in range(5):
+        sl = slice(512 * c, 512 * c + 512)
+        yb = T.YB[:, 512 * (c % 2):512 * (c % 2) + 512]
+        ps = "PS%d" % (c % 4)
+        cp(T.CN[:, sl], T.R[:, sl], 512, ["R%d" % c], ["CN%d" % c])
+        ac(yb, T.CN[:, sl], ACT.Identity, C(NO13), 1.0, 512, ["CN%d" % c] + k_(NO13), ["YB%d" % (c % 2)])
+        mm([(T[ps][:], T.M1[:], T.CN[:, sl], True, False), (T[ps][:], T.M2[:], yb, False, True)], 2560,
+           ["M1", "M2", "CN%d" % c, "YB%d" % (c % 2)], [ps])
+        if c % 2 == 0:
+            ts(T.W[:, sl], T[ps][:], C(NO13), None, ALU.add, None, 512, k_(NO13), [ps, "W%d" % c])
+        else:
+            ac(T.W[:, sl], T[ps][:], ACT.Identity, C(NO13), 1.0, 512, k_(NO13), [ps, "W%d" % c])
+    WK = ["W%d" % c for c in range(6)]
+    CK = ["CN%d" % c for c in range(6)]
+    dma("S", [(T.yp[16 * g:16 * g + 12, 0:V0], T.CN[16 * g:16 * g + 12, 0:V0]) for g in range(8)], "stat", CK[:5], ["ypa"], 6.0)
+    xk = lambda v, p: "X%d_%d" % (v, p)
+    for p in range(4):
+        ts(T.X0[:, 512 * p:512 * p + 512], T.XS[:, 512 * p:512 * p + 512], 128.0, None, ALU.add, None, 512, ["XS%d" % p], [xk(0, p)], 0.5)
+        for (a, b, k) in RUNS[p]:
+            cp(SL(0)[:, 8 * a:8 * (a + k)], T.STI[:, 8 * b:8 * (b + k)], 8 * k, ["STI"], ["S0_%d" % min(p, 2)])
+    Wwin, Cwin, Iwin = T.W[:, 0:WD_], T.CN[:, 0:WD_], T.ID[:, 0:WD_]
+    acc = [0.5]
+
+    def walk(v, c, step):
+        j0, n = CH[c]
+        nb = n // 128
+        H = 16 // nb
+        X = T["X%d" % v]
+        src, sk = [(SL(v), "S%d_%d" % (v, c)), (T.L1, "L1_%d" % c), (T.L2, "L2_%d" % c)][step]
+        dst, dk = [(T.L1, "L1_%d" % c), (T.L2, "L2_%d" % c), (T["U%d" % v], "U%d_%d" % (v, c))][step]
+        pcs = list(range(j0 // 512, (j0 + n) // 512))
+        pv, Z = "pv%d" % c, T["Z%d" % c]
+        PV, b0 = (T.PVa, 160 * c) if c < 2 else (T.PVb, 0)
+        for p in pcs:
+            sl, ps = slice(512 * p, 512 * p + 512), "PS%d" % p
+            mm([(T[ps][:], T.S1[:], X[:, sl], True, True)], 512, ["S1", xk(v, p)], [ps])
+            gat(T.CG[:, sl], Wwin.indirect(src[:, 32 * p:32 * p + 32]), 512, WK + [sk], ["CG%d" % p])
+            tt(T.PR[:, sl], T.CG[:, sl], T[ps][:], ALU.mult, 512, ["CG%d" % p], [ps, "PR%d" % p])
+        mm([(PV[:, b0 + i:b0 + 32 * nb:nb], T.PR[:, j0 + i:j0 + n:nb], T.WV[:], True, True) for i in range(nb)], 64 * nb,
+           WVK + ["PR%d" % p for p in pcs], [pv])
+        sn = T.SN[:, j0 // 8:j0 // 8 + 16 * nb]
+        tt(sn, PV[:, b0:b0 + 16 * nb], T.THC[:, 64 - 8 * nb:64 + 8 * nb], ALU.is_gt, 16 * nb, ["THCa", "THCb"], [pv, "SN%d" % c])
+        tt(Z[:, H:17 * H:H, :], sn, PV[:, b0 + 16 * nb:b0 + 32 * nb], ALU.mult, 16 * nb, ["SN%d" % c], [pv, "Z%d" % c])
+        lo = PV[:, b0 + 32 * nb:b0 + 40 * nb]
+        mm([(lo, Z[:, H * (1 + 8 * hl) - h:H * (9 + 8 * hl) - h, :], T.EYH[:, h:128:H], hl == 0 and h == 0, hl == 1 and h == H - 1)
+            for hl in range(2) for h in range(H)], 128 * H, ["EYH", "Z%d" % c], [pv])
+        ts(dst[:, j0 // 16:(j0 + n) // 16], lo, OFF, None, ALU.add, None, 8 * nb, [], [pv, dk])
+        if c == v % 2 and step > 0:
+            o8 = b0 + 32 * nb + 8 * (POS.index(v) % 4)
+            ac(T.ST[:, 8 * step - 8:8 * step], PV[:, o8:o8 + 8], ACT.Copy, 0.0, 1.0, 8, [], [pv, "STs" if step == 1 else "STt"])
+        for p in pcs:
+            sl, ps = slice(512 * p, 512 * p + 512), "PS%d" % p
+            mm([(T[ps][:], T.S1[:], X[:, sl], True, False), (T[ps][:], T.S2[:], T.CG[:, sl], False, True)], 1024,
+               ["S1", "S2", "CG%d" % p, xk(v, p)], [ps])
+            acc[0] += PAR["round_v"]
+            if acc[0] >= 0.999:
+                acc[0] -= 1.0
+                ts(X[:, sl], T[ps][:], C(CR), None, ALU.add, None, 512, k_(CR), [ps, xk(v, p)])
+            else:
+                ac(X[:, sl], T[ps][:], ACT.Identity, C(CR), 1.0, 512, k_(CR), [ps, xk(v, p)])
+            if step == 2:
+                if v < NV - 1:
+                    send(T["X%d" % (v + 1)][:, sl], X[:, sl], "ax%d_%d" % (v + 1, p), [xk(v, p)], [xk(v + 1, p)], PAR["lx"])
+                else:
+                    ts(T.XS[:, sl], X[:, sl], -128.0, None, ALU.add, None, 512, [xk(v, p)], ["XS%d" % p], 0.5)
+                    send(T["X%d" % (v + 1)][:, sl], T.XS[:, sl], "ax%d_%d" % (v + 1, p), ["XS%d" % p], [xk(v + 1, p)], PAR["lx"])
+
+    def send_list(v, c):
+        j0, n = CH[c]
+        cs = slice(j0 // 16, (j0 + n) // 16)
+        send(SL(v + 1)[:, cs], T["U%d" % v][:, cs], "as%d_%d" % (v + 1, c), ["U%d_%d" % (v, c)], ["S%d_%d" % (v + 1, c)], PAR["ls"])
+
+    def equalities(G, gk, E, ek):
+        for h in (1, 0):
+            PD = T["PD%d" % h]
+            mm([(PD[:], G[:], T.NSEL[:], True, False)] +
+               [(PD[:, :, 16 * q:16 * q + 16], T.SEL[:, 128 * q:128 * q + 128], G[:, 64 * h:64 * h + 64], False, q == 7) for q in range(8)],
+               1024, ["SEL", "NSEL", gk], ["PD%d" % h])
+            tt(E[:, 512 * h:512 * h + 512], PD[:], T.TRI[:, 512 * h:512 * h + 512], ALU.is_equal, 512, ["TRI"], ["PD%d" % h, ek + str(h)])
+
+    def train(v):
+        c = v % 2
+        pos = POS.index(v)
+        p = pos // 4
+        tc = slice(128 * pos, 128 * pos + 128)
+        lc = slice(8 * pos, 8 * pos + 8)
+        sL, sk = T.L2[:, lc], "L2_%d" % c
+        tL, tk = T["U%d" % v][:, lc], "U%d_%d" % (v, c)
+        pv, ps = "pvt", "PS%d" % p
+        PV, PS = T.PVa, T[ps]
+        o8 = 160 * c + 128 + 8 * (pos % 4)
+        gat(T.G1[:], Iwin.indirect(sL), 128, IDK + [sk], ["G1"])
+        gat(T.GS[:], Cwin.indirect(sL), 128, CK + [sk], ["GS"])
+        equalities(T.G1, "G1", T.E1, "E1")
+        mm([(PV[:, 448:456], T.OB[:], T.ONE[:, 8:16], True, False)] +
+           [(PV[:, 448 + k:449 + k], T.E1[:, 128 * k:128 * k + 128], T.ONE[:, 0:1], False, k == 7) for k in range(8)], 576,
+           ["E10", "E11", "ONEa", "ONEc", "OB"], [pv])
+        tt(T.MD[:], PV[:, 448:456], T.DUM[:], ALU.min, 8, ["DUM"], [pv, "MD"])
+        tt(T.A2[:, 0:8], T.MD[:], T.ST[:, 0:8], ALU.max, 8, ["MD", "STs"], ["A2s"])
+        ts(T.IX1[:, 0:8], T.A2[:, 0:8], OFF, None, ALU.add, None, 8, ["A2s"], ["IXs"])
+        tt(T.A2[:, 8:16], PV[:, o8:o8 + 8], T.MD[:], ALU.max, 8, ["MD"], ["pv%d" % c, "A2t"])
+        ts(T.IX1[:, 8:16], T.A2[:, 8:16], OFF, None, ALU.add, None, 8, ["A2t"], ["IXt"])
+        tt(T.NE[:], T.A2[:, 0:8], T.A2[:, 8:16], ALU.not_equal, 8, ["A2s", "A2t"], ["NE"])
+        mm([(T.PD0[:, 0, :], T.WB[:], T.PR[:, tc], True, True)], 128, ["WB", "PR%d" % p], ["PD0"])
+        ts(T.MB[:], T.PD0[:, 0, :], C(SIG), C(TAU), ALU.mult, ALU.is_gt, 128, k_(SIG, TAU), ["PD0", "MB"])
+        ac(T.NB[:], T.MB[:], ACT.Identity, 1.0, -1.0, 128, ["MB"], ["NB"])
+        tt(Cwin.indirect(T.IX1[:, 0:8]), T.GS[:], T.MB[:], ALU.add, 128, ["IXs", "GS", "MB"], CK, SCA)
+        tt(T.GM[:], T.GS[:], T.MB[:], ALU.mult, 128, ["GS", "MB"], ["GM"], 2.0)
+        tt(T.KP[:], T.CG[:, tc], T.NB[:], ALU.mult, 128, ["CG%d" % p, "NB"], ["KP"])
+        gat(T.G2[:], Iwin.indirect(T.IX1[:, 8:16]), 128, IDK + ["IXt"], ["G2"])
+        equalities(T.G2, "G2", T.E2, "E2")
+        gat(T.GT[:], Cwin.indirect(tL), 128, CK + [tk], ["GT"])
+        gat(T.WT[:], Wwin.indirect(tL), 128, WK + [tk], ["WT"])
+        mm([(PS[:, 128:256], T.GM[:], T.WN[:, 0:128], True, True), (PS[:, 256:384], T.GM[:], T.WN[:, 128:256], True, False),
+            (PS[:, 256:384], T.GT[:], T.WN[:, 0:128], False, True)], 1536, ["GM", "GT", "WNa", "WNb"], [ps])
+        tt(T.FL[:], PS[:, 128:384], T.THR[:], ALU.is_lt, 256, ["THRa", "THRb"], [ps, "FL"])
+        mm([(PS[:, 384:512], T.SW[:], T.WT[:], True, False), (PS[:, 384:512], T.SD[:], T["X%d" % v][:, tc], False, True)], 256,
+           ["SW", "SD", "WT", xk(v, p)], [ps])
+        ts(T.WDN[:], PS[:, 384:512], MAGIC, MAGIC, ALU.add, ALU.subtract, 128, [], [ps, "WDN"])
+        mm([(PV[:, 464:472], T.FL[:, 0:128], T.G8[:], True, False), (PV[:, 464:472], T.FL[:, 128:256], T.G8[:], False, False)] +
+           [(PV[:, 464 + k:465 + k], T.E2[:, 128 * k:128 * k + 128], T.ONE[:, 2:3], False, k == 7) for k in range(8)], 640,
+           ["FL", "G8", "E20", "E21", "ONEb"], [pv])
+        tt(T.CP[:, 0:8], PV[:, 464:472], T.NE[:], ALU.is_lt, 8, ["NE"], [pv, "CP"])
+        fr, f2, fa, fb = (T.FR[:, 8 * v + i:8 * v + i + 1] for i in range(4))
+        fk = "FR%d" % v
+        ac(f2, fr, ACT.Identity, 2 * BIG, 1.0, 1, [fk], [fk + "b"])
+        ac(fa, fr, ACT.Identity, OFF, -1.0, 1, [fk], [fk + "c"])
+        ac(fb, fr, ACT.Identity, OFF - 2 * BIG, -1.0, 1, [fk], [fk + "d"])
+        ac(T.FT[:, 0:8], T.ST[:, 8:16], ACT.Identity, fa, 1.0, 8, ["STt", fk + "c"], ["FTa"])
+        ac(T.FT[:, 8:16], T.DUM[:], ACT.Identity, fb, 1.0, 8, ["DUM", fk + "d"], ["FTb"])
+
+        def ranks(o, h):
+            return ([(PV[:, o:o + 9], T.TB[:], T.CP[:, 0:9], True, False), (PV[:, o:o + 8], T.BE[:, 128 * h:128 * h + 128], T.CP[:, 0:8], False, False)] +
+                    [(PV[:, o + a:o + 9], T.OB[:], T.CP[:, 0:9 - a], False, a == 8) for a in range(1, 9)])
+        mm(ranks(472, 0), 640, ["TB", "OB", "BE0", "CP"], [pv])
+        tt(T.OO[:, 0:8], PV[:, 472:480], T.FT[:, 0:8], ALU.max, 8, ["FTa"], [pv, "OOa"])
+        ts(tL, T.OO[:, 0:8], fr, None, ALU.add, None, 8, ["OOa", fk], [tk])
+        send_list(v, c)
+        tt(T.YY[:], Iwin.indirect(tL), T.MB[:], ALU.mult, 128, IDK + [tk, "MB"], ["YY"], GAT)
+        tt(Wwin.indirect(T.IX1[:, 0:8]), T.YY[:], T.KP[:], ALU.add, 128, ["IXs", "YY", "KP"], WK, SCA)
+        mm(ranks(484, 1) + [(PV[:, 496:504], T.BE[:, 128:256], T.CP[:, 0:8], True, True)], 704, ["TB", "OB", "BE1", "CP"], [pv])
+        tt(T.OO[:, 8:16], PV[:, 484:492], T.FT[:, 8:16], ALU.min, 8, ["FTb"], [pv, "OOb"])
+        ts(T.IX2[:, 8:16], T.OO[:, 8:16], f2, None, ALU.add, None, 8, ["OOb", fk + "b"], ["IXd"])
+        cp(Wwin.indirect(T.IX2[:, 8:16]), T.WDN[:], 128, ["IXd", "WDN"], WK, SCA)
+        tt(T.OO[:, 16:24], PV[:, 496:504], T.DUM[:], ALU.add, 8, ["DUM"], [pv, "OOc"])
+        if v < NV - 1:
+            ac(T.FR[:, 8 * v + 8:8 * v + 9], PV[:, 492:493], ACT.Identity, fr, 1.0, 1, [fk], [pv, "FR%d" % (v + 1)])
+        tt(T.OO[:, 24:32], T.OO[:, 16:24], T.ST[:, 8:16], ALU.max, 8, ["OOc", "STt"], ["OOd"])
+        ts(T.IX2[:, 0:8], T.OO[:, 24:32], OFF, None, ALU.add, None, 8, ["OOd"], ["IXu"])
+        ac(T.H0[:], T.GT[:], ACT.Identity, -0.25, 0.5, 128, ["GT"], ["H0"])
+        ts(T.HF[:], T.H0[:], MAGIC, MAGIC, ALU.add, ALU.subtract, 128, ["H0"], ["HF"])
+        cp(Cwin.indirect(T.IX2[:, 8:16]), T.HF[:], 128, ["IXd", "HF"], CK, SCA)
+        tt(Cwin.indirect(T.IX2[:, 0:8]), T.GT[:], T.HF[:], ALU.subtract, 128, ["IXu", "GT", "HF"], CK, SCA)
+
+    for v in range(NV):
+        for c in (v % 2, 1 - v % 2, 2):
+            for step in range(3):
+                walk(v, c, step)
+            if c != v % 2:
+                send_list(v, c)
+        train(v)
+        if v == 0:
+            ts(C(FW), C(ODD), 64.0, 4.0, ALU.mult, ALU.add, 1, k_(ODD), k_(FW))
+            ts(C(FW2), C(G_), 5.0, C(FW), ALU.mult, ALU.add, 1, k_(G_, FW), k_(FW2))
+            ts(T.MW[:], T.IO[:, 0:132], C(FW2), C(GE12), ALU.is_equal, ALU.mult, 132, ["IO"] + k_(FW2, GE12), ["MW"])
+            ts(C(PM2), C(P_), -2.0, None, ALU.add, None, 1, k_(P_), k_(PM2))
+            ts(C(PO13), C(M1213), OFF, None, ALU.mult, None, 1, k_(M1213), k_(PO13))
+            ts(MT(0), IO, C(PM2), C(GE14), ALU.is_equal, ALU.mult, 128, ["IO"] + k_(PM2, GE14), ["MT0"])
+            tt(T.M3[:], MT(0), T.M1[:], ALU.add, 128, ["MT0", "M1"], ["M3"])
+            ts(T.M4[:], IO, C(P_), C(GE14), ALU.is_equal, ALU.mult, 128, ["IO"] + k_(P_, GE14), ["M4"])
+    mm([(T.PD0[:], T.MW[:, 4 - c:132 - c], T.W[:, 512 * c:512 * c + 512], c == 0, c == 4) for c in range(5)], 2560, ["MW"] + WK, ["PD0"])
+    ac(T.OT[:], T.PD0[:], ACT.Identity, OFF, 1.0, 512, [], ["PD0", "OT"])
+    dma("S", [(T.yp[12:128:16, 0:V0], T.OT[0:40, :]), (T.yp[13:128:16, 0:V0], T.OT[64:104, :])], "outs", ["OT"], ["ypb"], 2.5)
+    dma("S", [(T.yp[14:128:16, 0:V0], T.CN[14:128:16, 0:V0]), (T.yp[15:128:16, 0:V0], T.CN[15:128:16, 0:V0])], "outs", CK, ["ypc"], 2.5)
+    mm([(T.PD1[:], T.M3[:], T.W[:, V0:V0 + 512], True, False), (T.PD1[:], T.M4[:], T.CN[:, V0:V0 + 512], False, True)], 2560,
+       ["M3", "M4"] + WK + CK, ["PD1"])
+    ts(T.ON[:], T.PD1[:], C(PO13), None, ALU.add, None, 512, k_(PO13), ["PD1", "ON"])
+    dma("S", [(T.yp[:, V0:V0 + 512], T.ON[:])], "outs", ["ON"], ["ypd"], 3.0)
+    for p in range(4):
+        dma("S", [(T.yx[:, 128 * b:128 * (b + k)], T["X%d" % NV][:, 128 * a:128 * (a + k)]) for (a, b, k) in RUNS[p]], "outs",
+            [xk(NV, p)], ["yx%d" % p], 3.0)
+        for (a, b, k) in RUNS[p]:
+            cp(T.YS[:, 8 * b:8 * (b + k)], SL(NV)[:, 8 * a:8 * (a + k)], 8 * k, ["S%d_%d" % (NV, min(p, 2))], ["YS%d" % b])
+    dma("A", [(T.ys[:], T.YS[:])], "outs", ["YS%d" % b for r in RUNS for (a, b, k) in r], ["ys"], 2.5)
+    return ops, neng
+
+
+def depend(ops):
+    lastw, readers, deps = {}, {}, []
+    for i, o in enumerate(ops):
+        d = set()
+        for k in o["rd"]:
+            if k in lastw:
+                d.add(lastw[k])
+        for k in o["wr"]:
+            if k in lastw:
+                d.add(lastw[k])
+            d.update(readers.get(k, []))
+        d.discard(i)
+        deps.append(sorted(d))
+        for k in o["rd"]:
+            readers.setdefault(k, []).append(i)
+        for k in o["wr"]:
+            lastw[k] = i
+            readers[k] = []
+    return deps
+
+
+def place(ops, before, seq, back):
+    HOP = PAR["hop"]
+    busy, at, fin = {}, {}, {}
+    for i in seq:
+        o = ops[i]
+        t = max([fin[j] + HOP for j in before[i]] + [0.0]) + (o["lat"] if back else 0.0)
+        res = [(o["q"], o["cost"])] + ([(o["bank"], o["cost"] + HOP)] if o["bank"] else [])
+        moved = True
+        while moved:
+            moved = False
+            for (r, d) in res:
+                l = busy.setdefault(r, [])
+                k = len(l)
+                while k > 0 and l[k - 1][1] > t + 1e-9:
+                    k -= 1
+                while k < len(l) and l[k][0] < t + d - 1e-9:
+                    if l[k][1] > t + 1e-9:
+                        t = l[k][1]
+                        moved = True
+                    k += 1
+        for (r, d) in res:
+            l = busy[r]
+            k = len(l)
+            while k > 0 and l[k - 1][0] > t:
+                k -= 1
+            l.insert(k, (t, t + d))
+        at[i] = t
+        fin[i] = t + o["cost"] + (0.0 if back else o["lat"])
+    return at, fin
+
+
+PLANS = {}
+
+
+def plan(ops):
+    if "best" not in PLANS:
+        n = len(ops)
+        deps = depend(ops)
+        succ = [[] for _ in range(n)]
+        for i in range(n):
+            for j in deps[i]:
+                succ[j].append(i)
+        rng = np.random.default_rng(7)
+        prio = [0.0] * n
+        for i in range(n - 1, -1, -1):
+            prio[i] = ops[i]["cost"] + ops[i]["lat"] + PAR["hop"] + max([prio[j] for j in succ[i]] + [0.0])
+        seq = sorted(range(n), key=lambda i: (-prio[i], i))
+        best = None
+        for k in range(PAR["tries"]):
+            at, fin = place(ops, deps, seq, False)
+            end = max(fin.values())
+            if best is None or end < best[0]:
+                best = (end, at, fin)
+            elif k % 4 == 3:
+                at, fin = best[1], best[2]
+            key = {}
+            for i in range(n):
+                key[i] = max([fin[i] + PAR["jit"] * float(rng.random())] + [key[j] + 1e-6 for j in deps[i]])
+            atb, finb = place(ops, succ, sorted(range(n), key=lambda i: -key[i]), True)
+            key = {}
+            for i in range(n - 1, -1, -1):
+                key[i] = max([finb[i] + PAR["jit"] * float(rng.random())] + [key[j] + 1e-6 for j in succ[i]])
+            seq = sorted(range(n), key=lambda i: -key[i])
+        at = best[1]
+        order = sorted(range(n), key=lambda i: (at[i], i))
+        last = {}
+        for i in order:
+            b = ops[i]["bank"]
+            if b:
+                if b in last and ops[last[b]]["q"] != ops[i]["q"]:
+                    deps[i] = sorted(set(deps[i] + [last[b]]))
+                last[b] = i
+        PLANS["best"] = (order, deps, best[0], at)
+    return PLANS["best"]
+
+
+def rank_program(g, core, T, topo):
+    rank = T.rank_of(core)
+    if rank is None:
+        return
+    nxt = T.cores[(rank + 1) % len(T.cores)]
+    assert topo.may_write(core, nxt)
+    ops, neng = build(T, topo, core, nxt)
+    order, deps = plan(ops)[:2]
+    spot = {i: k for k, i in enumerate(order)}
+    eng = {"V": g.vector, "A": g.scalar, "P": g.tensor, "G": g, "S": g.sync}
+    count, token, clock = {}, {}, {}
+    known = {q: {} for q in eng}
+    nsent = 0
+    for i in order:
+        o = ops[i]
+        q = o["q"]
+        kn = known[q]
+        need = {}
+        for j in deps[i]:
+            s, val = token[j]
+            if kn.get(s, 0) < val and need.get(s, (0, 0))[0] < val:
+                need[s] = (val, j)
+        for s, (val, j) in sorted(need.items(), key=lambda e: -spot[e[1][1]]):
+            if kn.get(s, 0) < val:
+                eng[q].wait_ge(T.sem[s], val)
+                kn[s] = val
+                for s2, v2 in clock[j].items():
+                    if kn.get(s2, 0) < v2:
+                        kn[s2] = v2
+        r = o["fn"](g)
+        s = o["sem"] or "q" + q
+        count[s] = count.get(s, 0) + o["n"]
+        if o["sem"] is None:
+            r.then_inc(T.sem[s], 1)
+        token[i] = (s, count[s])
+        remote = o["sem"] is not None and q == "G"
+        nsent += 1 if remote else 0
+        clock[i] = {} if remote else dict(kn)
+    for s in sorted(count):
+        if max(known[q].get(s, 0) for q in known) < count[s]:
+            g.wait_ge(T.sem[s], count[s])
+    g.wait_ge(T.sem.sent, nsent * neng)

@@ -3,9 +3,9 @@ from concourse.mybir import AluOpType as ALU, ActivationFunctionType as ACT
 
 V0, NS, NV, WD_ = 2560, 2048, 4, 3200
 DUMMY = 3072
-CH = [(0, 512), (512, 512), (1024, 1024)]
-POS = [0, 2, 4, 5, 1, 3, 6, 7, 8, 9, 10, 11, 12, 13, 14, 15]
-RUNS = [[(0, 0, 1), (1, 2, 1), (2, 4, 2)], [(4, 1, 1), (5, 3, 1), (6, 6, 2)], [(8, 8, 4)], [(12, 12, 4)]]
+CH = [(0, 1024), (1024, 1024)]
+POS = [0, 2, 4, 5, 8, 9, 10, 11, 1, 3, 6, 7, 12, 13, 14, 15]
+RUNS = [[(0, 0, 1), (1, 2, 1), (2, 4, 2)], [(4, 8, 4)], [(8, 1, 1), (9, 3, 1), (10, 6, 2)], [(12, 12, 4)]]
 MAGIC = 12582912.0
 BIG = 4096.0
 OFF = 1536.0
@@ -18,10 +18,10 @@ def _sb(cols, dtype):
 SCRATCH = {}
 for _d, _l in (("int32", dict(R=V0, STI=128, SGI=4, PC=12)),
                ("uint16", dict(L1=128, L2=128, IX1=16, IX2=16)),
-               ("float16", dict(Z0=[68, 4], Z1=[68, 4], Z2=[34, 8], EYH=128)),
-               ("bfloat16", dict(W=WD_, ID=WD_, YB=1024, XS=NS, CG=NS, PR=NS, SN=256, SEL=1024,
+               ("float16", dict(Z0=[34, 8], Z1=[34, 8], EYH=128)),
+               ("bfloat16", dict(W=WD_, ID=WD_, YB=1024, XS=NS, CG=NS, PR=NS, SN=256, ZZ=1024, SEL=1024,
                                  NSEL=512, TRI=1024, BE=256, S1=128, S2=128, SW=128, SD=128, WV=32, G8=8, M2=128, M3=128, MW=132, MT=512,
-                                 OB=128, TB=128, WB=128, ONE=32, CP=16, G1=128, G2=128, NB=128, KP=128, WT=128, WDN=128, YY=128, FL=256,
+                                 OB=128, TB=128, WB=128, ONE=32, CP=16, CX=16, G1=128, G2=128, NB=128, KP=128, WT=128, WDN=128, YY=128, FL=256,
                                  E1=1024, E2=1024)),
                ("float32", dict(CN=WD_, THC=128, IO=256, COL=32, R16=16, HM=16, IG=128, IR=128, M1=128, M4=128, WN=256, THR=256,
                                 DUM=8, ST=16, MD=8, A2=16, NE=8, FT=16, OO=32, FR=40, GS=128, GT=128, GM=128, MB=128,
@@ -39,21 +39,22 @@ for _n in ("PD0", "PD1"):
     SCRATCH[_n] = ("psum", [128, 4, 128], "float32")
 
 SEMAPHORES = (["qV", "qA", "qP", "qG", "sent", "outs", "stat", "lsg", "lst"] + ["lr%d" % i for i in range(5)] + ["lx%d" % i for i in range(4)]
-              + ["ax%d_%d" % (v, p) for v in range(1, NV + 1) for p in range(4)] + ["as%d_%d" % (v, c) for v in range(1, NV + 1) for c in range(3)])
+              + ["ax%d_%d" % (v, p) for v in range(1, NV + 1) for p in range(4)] + ["as%d_%d" % (v, c) for v in range(1, NV + 1) for c in range(2)])
 
-PAR = {"round_v": 0.0, "cyc": 0.001, "pec": 0.0005, "gat": 1.56, "sca": 3.8, "hop": 0.12, "lx": 5.0, "ls": 3.5, "tries": 1500, "jit": 0.5}
+PAR = {"round_v": 0.0, "cyc": 0.00087, "pec": 0.00044, "gat": 1.56, "sca": 3.8, "hop": 0.18, "ov": 0.02, "lx": 1.0, "ls": 0.4, "lat": 2.2,
+       "split": 10, "mmo": 0.007, "tries": 9000, "jit": 0.5, "tol": 2.5}
 
 
 def build(T, topo, core, nxt):
     ops = []
     CYC, PEC, GAT, SCA = PAR["cyc"], PAR["pec"], PAR["gat"], PAR["sca"]
 
-    def op(q, cost, rd, wr, fn, sem=None, n=1, lat=0.0):
-        bank = "a" if any(k in ("pv0", "pv1", "pvt") for k in wr) else None
-        ops.append({"q": q, "cost": cost, "rd": rd, "wr": wr, "fn": fn, "sem": sem, "n": n, "lat": lat, "bank": bank})
+    def op(q, cost, rd, wr, fn, sem=None, n=1, lat=0.0, link=0.0):
+        bank = "a" if any(k in ("pv0", "pvt") for k in wr) else None
+        ops.append({"q": q, "cost": cost, "rd": rd, "wr": wr, "fn": fn, "sem": sem, "n": n, "lat": lat, "bank": bank, "link": link})
 
     def vc(n, k=1.0):
-        return 0.05 + max(64, n * k) * CYC
+        return PAR["ov"] + max(64, n * k) * CYC
 
     def ts(out, in0, s1, s2, o0, o1, n, rd, wr, k=1.0):
         if o1 is None:
@@ -79,7 +80,7 @@ def build(T, topo, core, nxt):
             for (o, l, rh, st, sp) in lst:
                 r = g.tensor.matmul(o, l, rh, st, sp)
             return r
-        op("P", 0.05 + cyc * PEC, rd, wr, fn)
+        op("P", PAR["mmo"] * len(lst) + cyc * PEC, rd, wr, fn)
 
     def dma(q, pairs, sem, rd, wr, lat):
         def fn(g):
@@ -92,8 +93,9 @@ def build(T, topo, core, nxt):
     mask = topo.mask(core, nxt)
     neng = len(topo.engines(core, nxt))
 
-    def send(dst, src, sem, rd, wr, lat):
-        op("G", 0.5, rd, wr, lambda g: g.remote_dma(dst, src, T.sem[sem], T.sem.sent, pid, rid, mask), sem=sem, n=neng, lat=lat)
+    def send(dst, src, sem, rd, wr, link):
+        op("G", 0.5, rd, wr, lambda g: g.remote_dma(dst, src, T.sem[sem], T.sem.sent, pid, rid, mask), sem=sem, n=neng,
+           lat=PAR["lat"] + link, link=link)
 
     def iota(out, pat, base, cm, n, wr, flag=True):
         if flag:
@@ -104,8 +106,9 @@ def build(T, topo, core, nxt):
     def ms(out, val, n, wr):
         iota(out, [[0, n]], int(val), 0, n, wr)
 
-    def sel(B, pat, o, fill, base, cm, n, k):
-        op("G", 0.2 + 2 * n * CYC, [k], [k], lambda g: g.affine_select(B, B, pat, o, fill, base, cm))
+    def sel(B, pat, o, fill, base, cm, n, k, zero=None):
+        src = B if zero is None else zero
+        op("G", 0.2 + 2 * n * CYC, [k, "ZZ"], [k], lambda g: g.affine_select(B, src, pat, o, fill, base, cm))
 
     C = lambda i: T.COL[:, i:i + 1]
     SL = lambda v: T["S%d_" % v]
@@ -120,19 +123,18 @@ def build(T, topo, core, nxt):
     iota(T.IG[:], [[1, 8], [0, 16]], 0, 0, 128, ["IG"])
     iota(T.IR[:], [[0, 8], [1, 16]], 0, 0, 128, ["IR"])
     iota(T.MD[:], [[16, 8]], DUMMY - int(OFF), 0, 8, ["MD"])
+    op("V", vc(512), [], ["ZZ"], lambda g: g.vector.memset(T.ZZ[:], 0.0))
     for (B, pat, n, f, k) in ((T.SEL, [[-16, 8], [0, 128]], 1024, 1.0, "SEL"), (T.NSEL, [[0, 4], [-16, 8], [0, 16]], 512, -1.0, "NSEL")):
-        ms(B[:], 0, n, [k])
         for r in (12, 14):
-            sel(B[:], pat, ALU.not_equal, f, -r, 1, n, k)
-    ms(T.TRI[:], 0, 1024, ["TRI"])
-    sel(T.TRI[:], [[16, 8], [0, 8], [1, 16]], ALU.is_gt, 0.5, 0, -1, 1024, "TRI")
+            sel(B[:], pat, ALU.not_equal, f, -r, 1, n, k, T.ZZ[:, 0:n] if r == 12 else None)
+    sel(T.TRI[:], [[16, 8], [0, 8], [1, 16]], ALU.is_gt, 0.5, 0, -1, 1024, "TRI", T.ZZ[:])
     for h, f in ((0, BIG), (1, -BIG)):
-        ms(T.BE[:, 128 * h:128 * h + 128], 0, 128, ["BE%d" % h])
-        sel(T.BE[:, 128 * h:128 * h + 128], [[-1, 128]], ALU.not_equal, f, 0, 1, 128, "BE%d" % h)
+        sel(T.BE[:, 128 * h:128 * h + 128], [[-1, 128]], ALU.not_equal, f, 0, 1, 128, "BE%d" % h, T.ZZ[:, 0:128])
     ms(T.CN[:, V0:WD_], 0, 640, ["CN5"])
     ms(T.ONE[:, 0:2], BIG, 2, ["ONEa"])
     ms(T.ONE[:, 2:4], 1, 2, ["ONEb"])
     ms(T.ONE[:, 8:16], -OFF / 16, 8, ["ONEc"])
+    ms(T.ONE[:, 16:24], 1, 8, ["ONEd"])
     ms(T.CP[:], 0, 16, ["CP"])
     ms(T.FR[:, 0:1], V0 - BIG, 1, ["FR0"])
     op("V", vc(64), [], ["THCa"], lambda g: g.vector.memset(T.THC[:, 0:64], 0.125))
@@ -186,8 +188,8 @@ def build(T, topo, core, nxt):
     for kind, col, f in ((0, E_, 1.0), (1, E_, -1.0), (2, ODD, 1.0), (3, M1214, 1.0)):
         ts(T.WV[:, 8 * kind:8 * kind + 8], T.G8[:], C(col), f, ALU.mult, ALU.mult, 8, ["G8"] + k_(col), ["WV%d" % kind])
     WVK = ["WV%d" % i for i in range(4)]
-    for c in range(3):
-        cp(T["Z%d" % c][:], T.CN[:, V0:V0 + 272], 272, ["CN5"], ["Z%d" % c])
+    for c in range(2):
+        cp(T["Z%d" % c][:], T.ZZ[:, 0:272], 272, ["ZZ"], ["Z%d" % c], 0.5)
     ac(T.W[:, V0:WD_], T.CN[:, V0:WD_], ACT.Identity, C(NO15), 1.0, 640, ["CN5"] + k_(NO15), ["W5"])
     ts(T.OO[:, 0:16], T.IO[:, 0:16], 256.0, C(GE14), ALU.mult, ALU.mult, 16, ["IO"] + k_(GE14), ["OOa", "OOb"])
     ts(T.HM[:], T.OO[:, 0:16], C(NO15), None, ALU.add, None, 16, ["OOa", "OOb"] + k_(NO15), ["HM"])
@@ -223,9 +225,10 @@ def build(T, topo, core, nxt):
     for p in range(4):
         ts(T.X0[:, 512 * p:512 * p + 512], T.XS[:, 512 * p:512 * p + 512], 128.0, None, ALU.add, None, 512, ["XS%d" % p], [xk(0, p)], 0.5)
         for (a, b, k) in RUNS[p]:
-            cp(SL(0)[:, 8 * a:8 * (a + k)], T.STI[:, 8 * b:8 * (b + k)], 8 * k, ["STI"], ["S0_%d" % min(p, 2)])
+            cp(SL(0)[:, 8 * a:8 * (a + k)], T.STI[:, 8 * b:8 * (b + k)], 8 * k, ["STI"], ["S0_%d" % (p // 2)])
     Wwin, Cwin, Iwin = T.W[:, 0:WD_], T.CN[:, 0:WD_], T.ID[:, 0:WD_]
     acc = [0.5]
+    ck = lambda p: ["CG%d" % p, "CH%d" % p]
 
     def walk(v, c, step):
         j0, n = CH[c]
@@ -236,12 +239,15 @@ def build(T, topo, core, nxt):
         dst, dk = [(T.L1, "L1_%d" % c), (T.L2, "L2_%d" % c), (T["U%d" % v], "U%d_%d" % (v, c))][step]
         pcs = list(range(j0 // 512, (j0 + n) // 512))
         pv, Z = "pv%d" % c, T["Z%d" % c]
-        PV, b0 = (T.PVa, 160 * c) if c < 2 else (T.PVb, 0)
+        PV, b0 = (T.PVa, T.PVb)[c], 0
         for p in pcs:
             sl, ps = slice(512 * p, 512 * p + 512), "PS%d" % p
             mm([(T[ps][:], T.S1[:], X[:, sl], True, True)], 512, ["S1", xk(v, p)], [ps])
-            gat(T.CG[:, sl], Wwin.indirect(src[:, 32 * p:32 * p + 32]), 512, WK + [sk], ["CG%d" % p])
-            tt(T.PR[:, sl], T.CG[:, sl], T[ps][:], ALU.mult, 512, ["CG%d" % p], [ps, "PR%d" % p])
+            a = 32 - PAR["split"] if c == v % 2 else 32
+            gat(T.CG[:, 512 * p:512 * p + 16 * a], Wwin.indirect(src[:, 32 * p:32 * p + a]), 16 * a, WK + [sk], ck(p)[0:1] if a < 32 else ck(p))
+            if a < 32:
+                cp(T.CG[:, 512 * p + 16 * a:512 * p + 512], Wwin.indirect(src[:, 32 * p + a:32 * p + 32]), 512 - 16 * a, WK + [sk], ck(p)[1:2], GAT)
+            tt(T.PR[:, sl], T.CG[:, sl], T[ps][:], ALU.mult, 512, ck(p), [ps, "PR%d" % p])
         mm([(PV[:, b0 + i:b0 + 32 * nb:nb], T.PR[:, j0 + i:j0 + n:nb], T.WV[:], True, True) for i in range(nb)], 64 * nb,
            WVK + ["PR%d" % p for p in pcs], [pv])
         sn = T.SN[:, j0 // 8:j0 // 8 + 16 * nb]
@@ -257,7 +263,7 @@ def build(T, topo, core, nxt):
         for p in pcs:
             sl, ps = slice(512 * p, 512 * p + 512), "PS%d" % p
             mm([(T[ps][:], T.S1[:], X[:, sl], True, False), (T[ps][:], T.S2[:], T.CG[:, sl], False, True)], 1024,
-               ["S1", "S2", "CG%d" % p, xk(v, p)], [ps])
+               ["S1", "S2", xk(v, p)] + ck(p), [ps])
             acc[0] += PAR["round_v"]
             if acc[0] >= 0.999:
                 acc[0] -= 1.0
@@ -284,6 +290,9 @@ def build(T, topo, core, nxt):
                1024, ["SEL", "NSEL", gk], ["PD%d" % h])
             tt(E[:, 512 * h:512 * h + 512], PD[:], T.TRI[:, 512 * h:512 * h + 512], ALU.is_equal, 512, ["TRI"], ["PD%d" % h, ek + str(h)])
 
+    def earlier(o, E, w):
+        return [(T.PVa[:, o + k:o + 1 + k], E[:, 128 * k:128 * k + 128], T.ONE[:, w:w + 1], False, k == 7) for k in range(8)]
+
     def train(v):
         c = v % 2
         pos = POS.index(v)
@@ -294,17 +303,15 @@ def build(T, topo, core, nxt):
         tL, tk = T["U%d" % v][:, lc], "U%d_%d" % (v, c)
         pv, ps = "pvt", "PS%d" % p
         PV, PS = T.PVa, T[ps]
-        o8 = 160 * c + 128 + 8 * (pos % 4)
+        o8 = 256 + 8 * (pos % 4)
         gat(T.G1[:], Iwin.indirect(sL), 128, IDK + [sk], ["G1"])
         gat(T.GS[:], Cwin.indirect(sL), 128, CK + [sk], ["GS"])
         equalities(T.G1, "G1", T.E1, "E1")
-        mm([(PV[:, 448:456], T.OB[:], T.ONE[:, 8:16], True, False)] +
-           [(PV[:, 448 + k:449 + k], T.E1[:, 128 * k:128 * k + 128], T.ONE[:, 0:1], False, k == 7) for k in range(8)], 576,
-           ["E10", "E11", "ONEa", "ONEc", "OB"], [pv])
+        mm([(PV[:, 448:456], T.OB[:], T.ONE[:, 8:16], True, False)] + earlier(448, T.E1, 0), 576, ["E10", "E11", "ONEa", "ONEc", "OB"], [pv])
         tt(T.MD[:], PV[:, 448:456], T.DUM[:], ALU.min, 8, ["DUM"], [pv, "MD"])
         tt(T.A2[:, 0:8], T.MD[:], T.ST[:, 0:8], ALU.max, 8, ["MD", "STs"], ["A2s"])
         ts(T.IX1[:, 0:8], T.A2[:, 0:8], OFF, None, ALU.add, None, 8, ["A2s"], ["IXs"])
-        tt(T.A2[:, 8:16], PV[:, o8:o8 + 8], T.MD[:], ALU.max, 8, ["MD"], ["pv%d" % c, "A2t"])
+        tt(T.A2[:, 8:16], (T.PVa, T.PVb)[c][:, o8:o8 + 8], T.MD[:], ALU.max, 8, ["MD"], ["pv%d" % c, "A2t"])
         ts(T.IX1[:, 8:16], T.A2[:, 8:16], OFF, None, ALU.add, None, 8, ["A2t"], ["IXt"])
         tt(T.NE[:], T.A2[:, 0:8], T.A2[:, 8:16], ALU.not_equal, 8, ["A2s", "A2t"], ["NE"])
         mm([(T.PD0[:, 0, :], T.WB[:], T.PR[:, tc], True, True)], 128, ["WB", "PR%d" % p], ["PD0"])
@@ -312,7 +319,7 @@ def build(T, topo, core, nxt):
         ac(T.NB[:], T.MB[:], ACT.Identity, 1.0, -1.0, 128, ["MB"], ["NB"])
         tt(Cwin.indirect(T.IX1[:, 0:8]), T.GS[:], T.MB[:], ALU.add, 128, ["IXs", "GS", "MB"], CK, SCA)
         tt(T.GM[:], T.GS[:], T.MB[:], ALU.mult, 128, ["GS", "MB"], ["GM"], 2.0)
-        tt(T.KP[:], T.CG[:, tc], T.NB[:], ALU.mult, 128, ["CG%d" % p, "NB"], ["KP"])
+        tt(T.KP[:], T.CG[:, tc], T.NB[:], ALU.mult, 128, ck(p) + ["NB"], ["KP"])
         gat(T.G2[:], Iwin.indirect(T.IX1[:, 8:16]), 128, IDK + ["IXt"], ["G2"])
         equalities(T.G2, "G2", T.E2, "E2")
         gat(T.GT[:], Cwin.indirect(tL), 128, CK + [tk], ["GT"])
@@ -324,8 +331,7 @@ def build(T, topo, core, nxt):
            ["SW", "SD", "WT", xk(v, p)], [ps])
         ts(T.WDN[:], PS[:, 384:512], MAGIC, MAGIC, ALU.add, ALU.subtract, 128, [], [ps, "WDN"])
         mm([(PV[:, 464:472], T.FL[:, 0:128], T.G8[:], True, False), (PV[:, 464:472], T.FL[:, 128:256], T.G8[:], False, False)] +
-           [(PV[:, 464 + k:465 + k], T.E2[:, 128 * k:128 * k + 128], T.ONE[:, 2:3], False, k == 7) for k in range(8)], 640,
-           ["FL", "G8", "E20", "E21", "ONEb"], [pv])
+           earlier(464, T.E2, 2), 640, ["FL", "G8", "E20", "E21", "ONEb"], [pv])
         tt(T.CP[:, 0:8], PV[:, 464:472], T.NE[:], ALU.is_lt, 8, ["NE"], [pv, "CP"])
         fr, f2, fa, fb = (T.FR[:, 8 * v + i:8 * v + i + 1] for i in range(4))
         fk = "FR%d" % v
@@ -334,17 +340,18 @@ def build(T, topo, core, nxt):
         ac(fb, fr, ACT.Identity, OFF - 2 * BIG, -1.0, 1, [fk], [fk + "d"])
         ac(T.FT[:, 0:8], T.ST[:, 8:16], ACT.Identity, fa, 1.0, 8, ["STt", fk + "c"], ["FTa"])
         ac(T.FT[:, 8:16], T.DUM[:], ACT.Identity, fb, 1.0, 8, ["DUM", fk + "d"], ["FTb"])
+        op("V", vc(8), ["CP", "ONEd"], ["CX"], lambda g: g.vector.tensor_tensor_scan(T.CX[:, 0:8], T.ONE[:, 16:24], T.CP[:, 0:8], 0.0, ALU.mult, ALU.add))
 
         def ranks(o, h):
-            return ([(PV[:, o:o + 9], T.TB[:], T.CP[:, 0:9], True, False), (PV[:, o:o + 8], T.BE[:, 128 * h:128 * h + 128], T.CP[:, 0:8], False, False)] +
-                    [(PV[:, o + a:o + 9], T.OB[:], T.CP[:, 0:9 - a], False, a == 8) for a in range(1, 9)])
-        mm(ranks(472, 0), 640, ["TB", "OB", "BE0", "CP"], [pv])
+            return [(PV[:, o:o + 9], T.TB[:], T.CP[:, 0:9], True, False), (PV[:, o:o + 8], T.BE[:, 128 * h:128 * h + 128], T.CP[:, 0:8], False, False),
+                    (PV[:, o + 1:o + 9], T.OB[:], T.CX[:, 0:8], False, True)]
+        mm(ranks(472, 0), 192, ["TB", "OB", "BE0", "CP", "CX"], [pv])
         tt(T.OO[:, 0:8], PV[:, 472:480], T.FT[:, 0:8], ALU.max, 8, ["FTa"], [pv, "OOa"])
         ts(tL, T.OO[:, 0:8], fr, None, ALU.add, None, 8, ["OOa", fk], [tk])
         send_list(v, c)
         tt(T.YY[:], Iwin.indirect(tL), T.MB[:], ALU.mult, 128, IDK + [tk, "MB"], ["YY"], GAT)
         tt(Wwin.indirect(T.IX1[:, 0:8]), T.YY[:], T.KP[:], ALU.add, 128, ["IXs", "YY", "KP"], WK, SCA)
-        mm(ranks(484, 1) + [(PV[:, 496:504], T.BE[:, 128:256], T.CP[:, 0:8], True, True)], 704, ["TB", "OB", "BE1", "CP"], [pv])
+        mm(ranks(484, 1) + [(PV[:, 496:504], T.BE[:, 128:256], T.CP[:, 0:8], True, True)], 256, ["TB", "OB", "BE1", "CP", "CX"], [pv])
         tt(T.OO[:, 8:16], PV[:, 484:492], T.FT[:, 8:16], ALU.min, 8, ["FTb"], [pv, "OOb"])
         ts(T.IX2[:, 8:16], T.OO[:, 8:16], f2, None, ALU.add, None, 8, ["OOb", fk + "b"], ["IXd"])
         cp(Wwin.indirect(T.IX2[:, 8:16]), T.WDN[:], 128, ["IXd", "WDN"], WK, SCA)
@@ -359,7 +366,7 @@ def build(T, topo, core, nxt):
         tt(Cwin.indirect(T.IX2[:, 0:8]), T.GT[:], T.HF[:], ALU.subtract, 128, ["IXu", "GT", "HF"], CK, SCA)
 
     for v in range(NV):
-        for c in (v % 2, 1 - v % 2, 2):
+        for c in (v % 2, 1 - v % 2):
             for step in range(3):
                 walk(v, c, step)
             if c != v % 2:
@@ -386,7 +393,7 @@ def build(T, topo, core, nxt):
         dma("S", [(T.yx[:, 128 * b:128 * (b + k)], T["X%d" % NV][:, 128 * a:128 * (a + k)]) for (a, b, k) in RUNS[p]], "outs",
             [xk(NV, p)], ["yx%d" % p], 3.0)
         for (a, b, k) in RUNS[p]:
-            cp(T.YS[:, 8 * b:8 * (b + k)], SL(NV)[:, 8 * a:8 * (a + k)], 8 * k, ["S%d_%d" % (NV, min(p, 2))], ["YS%d" % b])
+            cp(T.YS[:, 8 * b:8 * (b + k)], SL(NV)[:, 8 * a:8 * (a + k)], 8 * k, ["S%d_%d" % (NV, p // 2)], ["YS%d" % b])
     dma("A", [(T.ys[:], T.YS[:])], "outs", ["YS%d" % b for r in RUNS for (a, b, k) in r], ["ys"], 2.5)
     return ops, neng
 
@@ -418,7 +425,7 @@ def place(ops, before, seq, back):
     for i in seq:
         o = ops[i]
         t = max([fin[j] + HOP for j in before[i]] + [0.0]) + (o["lat"] if back else 0.0)
-        res = [(o["q"], o["cost"])] + ([(o["bank"], o["cost"] + HOP)] if o["bank"] else [])
+        res = [(o["q"], o["cost"])] + ([(o["bank"], o["cost"] + HOP)] if o["bank"] else []) + ([("link", o["link"])] if o["link"] else [])
         moved = True
         while moved:
             moved = False
@@ -459,21 +466,24 @@ def plan(ops):
         for i in range(n - 1, -1, -1):
             prio[i] = ops[i]["cost"] + ops[i]["lat"] + PAR["hop"] + max([prio[j] for j in succ[i]] + [0.0])
         seq = sorted(range(n), key=lambda i: (-prio[i], i))
-        best = None
+        best = cur = None
         for k in range(PAR["tries"]):
             at, fin = place(ops, deps, seq, False)
             end = max(fin.values())
             if best is None or end < best[0]:
                 best = (end, at, fin)
-            elif k % 4 == 3:
-                at, fin = best[1], best[2]
+            if cur is None or end < cur[0] + PAR["tol"] * (1 - k / PAR["tries"]):
+                cur = (end, at, fin)
+            at, fin = cur[1], cur[2]
+            jit = PAR["jit"] * (0.15 + float(rng.random()))
+            noise = (jit * rng.random(2 * n)).tolist()
             key = {}
             for i in range(n):
-                key[i] = max([fin[i] + PAR["jit"] * float(rng.random())] + [key[j] + 1e-6 for j in deps[i]])
+                key[i] = max([fin[i] + noise[i]] + [key[j] + 1e-6 for j in deps[i]])
             atb, finb = place(ops, succ, sorted(range(n), key=lambda i: -key[i]), True)
             key = {}
             for i in range(n - 1, -1, -1):
-                key[i] = max([finb[i] + PAR["jit"] * float(rng.random())] + [key[j] + 1e-6 for j in succ[i]])
+                key[i] = max([finb[i] + noise[n + i]] + [key[j] + 1e-6 for j in succ[i]])
             seq = sorted(range(n), key=lambda i: -key[i])
         at = best[1]
         order = sorted(range(n), key=lambda i: (at[i], i))

@@ -1,14 +1,44 @@
+import math
 import numpy as np
-from concourse.mybir import AluOpType as ALU, ActivationFunctionType as ACT
+from concourse.mybir import AluOpType as ALU, ActivationFunctionType as ACT, AxisListType as AX
 
 V0, NS, NV, WD_ = 2560, 2048, 4, 3200
 DUMMY = 3072
-CH = [(0, 1024), (1024, 1024)]
-POS = [0, 2, 4, 5, 8, 9, 10, 11, 1, 3, 6, 7, 12, 13, 14, 15]
-RUNS = [[(0, 0, 1), (1, 2, 1), (2, 4, 2)], [(4, 8, 4)], [(8, 1, 1), (9, 3, 1), (10, 6, 2)], [(12, 12, 4)]]
+NP_ = 19
 MAGIC = 12582912.0
 BIG = 4096.0
 OFF = 1536.0
+
+
+def blocks(v):
+    d = dict(zip(range(8 - v), [4, 5, 6, 7, 8, 3, 2, 1]))
+    d.update(zip(range(8, 15), range(9, 16)))
+    d.update(zip(range(15, 15 + v), range(3)))
+    d[18] = v
+    return d
+
+
+def chunks(v):
+    l = [("T", 4, 18, 1, [(18, 1, "PT", 0, "ptX")], ("PT", 128, "ptV")),
+         ("A", 8, 0, 8 - v, [(0, 4, "PS0", 0, "PS0"), (4, 4 - v, "PS1", 0, "ps1a" if v >= 2 else "PS1")], ("PV", 0, "pvA")),
+         ("B", 8, 8, 8 if v else 7, [(8, 4, "PS2", 0, "PS2"), (12, 4 if v else 3, "PS3", 0, "PS3")], ("PV", 256, "pvB"))]
+    if v >= 2:
+        l.append(("L", 4, 16, v - 1, [(16, v - 1, "PS1", 256, "ps1b")], ("PT", 256, "ptL")))
+    return l
+
+
+def runs(pos, n, to):
+    out = []
+    for p in range(pos, pos + n):
+        if out and out[-1][1] + out[-1][2] == to[p]:
+            out[-1][2] += 1
+        else:
+            out.append([p, to[p], 1])
+    return out
+
+
+def halves(pos, n):
+    return [(pos, 2), (pos + 2, 2)] if n == 4 else [(pos, n)]
 
 
 def _sb(cols, dtype):
@@ -16,63 +46,78 @@ def _sb(cols, dtype):
 
 
 SCRATCH = {}
-for _d, _l in (("int32", dict(R=V0, STI=128, SGI=4, PC=12)),
-               ("uint16", dict(L1=128, L2=128, IX1=16, IX2=16)),
-               ("float16", dict(Z0=[34, 8], Z1=[34, 8], EYH=128)),
-               ("bfloat16", dict(W=WD_, ID=WD_, YB=1024, XS=NS, CG=NS, PR=NS, SN=256, ZZ=1024, SEL=1024,
-                                 NSEL=512, TRI=1024, BE=256, S1=128, S2=128, SW=128, SD=128, WV=32, G8=8, M2=128, M3=128, MW=132, MT=512,
-                                 OB=128, TB=128, WB=128, ONE=32, CP=16, CX=16, G1=128, G2=128, NB=128, KP=128, WT=128, WDN=128, YY=128, FL=256,
-                                 E1=1024, E2=1024)),
-               ("float32", dict(CN=WD_, THC=128, IO=256, COL=32, R16=16, HM=16, IG=128, IR=128, M1=128, M4=128, WN=256, THR=256,
-                                DUM=8, ST=16, MD=8, A2=16, NE=8, FT=16, OO=32, FR=40, GS=128, GT=128, GM=128, MB=128,
-                                H0=128, HF=128, YS=128, OT=512, ON=512))):
+NX, NL = 128 * NP_, 8 * NP_
+for _d, _l in (("int32", dict(R=V0, STI=128, SGI=4, PC=16)),
+               ("uint16", dict(L1=NL, L2=NL, TL=8, IX1=16, IX2=24)),
+               ("float16", dict(ZA=[34, 8], ZB=[34, 8], ZT=[68, 4], ZL=[68, 4], EYH=128, C0=NX, C1=NX, C2=NX, PR=NX, SL=128, H2=128, Q4=128,
+                                E8=128, SC=128, SM=128, SW=128, WV=32, WB=128, FT=128, MT=512)),
+               ("bfloat16", dict(XS=NX, SN=384, ZZ=1024, TRI=1024, BE=256, G8=8, OB=128, TB=128, ONE=40, CP=16, CX=64, GA=256, GB=256,
+                                 B0=128, BT=WD_, BB=256, ZF=[68, 4], EYK=32, EYB=128, E1=[8, 128], E2=[8, 128])),
+               ("float32", dict(F=WD_, CN=WD_, IDT=WD_, THC=128, IO=256, COL=48, R16=16, HM=16, IG=128, IR=128, WN=64, THR=64, I4=160,
+                                DUM=16, MD=8, A2=16, NE=8, OO=32, GS=128, FS=128, GT=128, GM=128, MB=128, YY=128, WDN=128, PW=32,
+                                H0=128, HF=128, YS=128, UF=NL, BU=256, BR=256))):
     for _n, _c in _l.items():
         SCRATCH[_n] = _sb(_c, _d)
 for _v in range(NV + 1):
-    SCRATCH["X%d" % _v] = _sb(NS, "bfloat16")
-    SCRATCH["S%d_" % _v] = _sb(128, "uint16")
+    SCRATCH["X%d" % _v] = _sb(NX, "bfloat16")
 for _v in range(NV):
-    SCRATCH["U%d" % _v] = _sb(128, "uint16")
-for _n in ("PS0", "PS1", "PS2", "PS3", "PVa", "PVb"):
+    SCRATCH["S%d_" % _v] = _sb(NL, "uint16")
+    SCRATCH["U%d" % _v] = _sb(NL, "uint16")
+for _n in ("PS0", "PS1", "PS2", "PS3", "PV", "PT"):
     SCRATCH[_n] = ("psum", [128, 512], "float32")
 for _n in ("PD0", "PD1"):
-    SCRATCH[_n] = ("psum", [128, 4, 128], "float32")
+    SCRATCH[_n] = ("psum", [128, 8, 64], "float32")
 
-SEMAPHORES = (["qV", "qA", "qP", "qG", "sent", "outs", "stat", "lsg", "lst"] + ["lr%d" % i for i in range(5)] + ["lx%d" % i for i in range(4)]
-              + ["ax%d_%d" % (v, p) for v in range(1, NV + 1) for p in range(4)] + ["as%d_%d" % (v, c) for v in range(1, NV + 1) for c in range(2)])
+SEMAPHORES = (["qV", "qA", "qP", "qG", "sent", "outs", "stat", "lsg", "lst", "lcn"] + ["lr%d" % i for i in range(8)] + ["lx%d" % i for i in range(6)]
+              + ["r%d" % i for i in range(60)])
 
-PAR = {"round_v": 0.0, "cyc": 0.00087, "pec": 0.00044, "gat": 1.56, "sca": 3.8, "hop": 0.18, "ov": 0.02, "lx": 1.0, "ls": 0.4, "lat": 2.2,
-       "split": 10, "mmo": 0.007, "tries": 9000, "jit": 0.5, "tol": 2.5}
+PAR = {"cyc": 0.00085, "pec": 0.000425, "gat": 1.56, "sca": 3.8, "hop": 0.14, "ov": 0.008, "lx": 0.35, "ls": 0.3, "lat": 1.9,
+       "mmo": 0.005, "starts": 100, "rounds": ((12, 50), (4, 1500), (1, 7000), (1, 100000)), "temp": 0.06, "lam": 0.1, "seed": 1,
+       "rp": [640, 640, 512, 512, 256], "ea": (),
+       "mode": {"T18": "xn", "L16": "xn", "A0": "xn", "A4": "xn", "B8": "xn", "B12": "xn"}}
 
 
 def build(T, topo, core, nxt):
-    ops = []
+    ops, tag = [], ["s"]
     CYC, PEC, GAT, SCA = PAR["cyc"], PAR["pec"], PAR["gat"], PAR["sca"]
 
-    def op(q, cost, rd, wr, fn, sem=None, n=1, lat=0.0, link=0.0):
-        bank = "a" if any(k in ("pv0", "pvt") for k in wr) else None
-        ops.append({"q": q, "cost": cost, "rd": rd, "wr": wr, "fn": fn, "sem": sem, "n": n, "lat": lat, "bank": bank, "link": link})
+    def op(opts, rd, wr, sem=None, n=1, lat=0.0, link=0.0, first=False):
+        bank = None
+        for k in wr:
+            if k[:2] in ("pv", "pt", "ps"):
+                bank = k[:2]
+        ops.append({"opts": opts, "rd": rd, "wr": wr, "sem": sem, "n": n, "lat": lat, "bank": bank, "link": link, "first": first,
+                    "tag": tag[0], "cont": -1})
 
     def vc(n, k=1.0):
         return PAR["ov"] + max(64, n * k) * CYC
 
-    def ts(out, in0, s1, s2, o0, o1, n, rd, wr, k=1.0):
+    def f_ts(out, in0, s1, s2, o0, o1):
         if o1 is None:
-            op("V", vc(n, k), rd, wr, lambda g: g.vector.tensor_scalar(out, in0, s1, None, o0))
-        else:
-            op("V", vc(n, k), rd, wr, lambda g: g.vector.tensor_scalar(out, in0, s1, s2, o0, o1))
+            return lambda g: g.vector.tensor_scalar(out, in0, s1, None, o0)
+        return lambda g: g.vector.tensor_scalar(out, in0, s1, s2, o0, o1)
+
+    def f_ac(out, a, f, bias, scale):
+        return lambda g: g.scalar.activation(out, a, f, bias=bias, scale=scale)
+
+    def ts(out, in0, s1, s2, o0, o1, n, rd, wr, k=1.0):
+        op([("V", vc(n, k), f_ts(out, in0, s1, s2, o0, o1))], rd, wr)
 
     def tt(out, a, b, o, n, rd, wr, k=1.0):
-        op("V", vc(n, k), rd, wr, lambda g: g.vector.tensor_tensor(out, a, b, o))
+        op([("V", vc(n, k), lambda g: g.vector.tensor_tensor(out, a, b, o))], rd, wr)
 
     def cp(out, a, n, rd, wr, k=1.0):
-        op("V", vc(n, k), rd, wr, lambda g: g.vector.tensor_copy(out, a))
+        op([("V", vc(n, k), lambda g: g.vector.tensor_copy(out, a))], rd, wr)
 
     def ac(out, a, f, bias, scale, n, rd, wr, k=1.0):
-        op("A", 0.02 + vc(n, k), rd, wr, lambda g: g.scalar.activation(out, a, f, bias=bias, scale=scale))
+        op([("A", 0.02 + vc(n, k), f_ac(out, a, f, bias, scale))], rd, wr)
 
-    def gat(out, a, n, rd, wr):
-        op("A", 0.02 + vc(n, GAT), rd, wr, lambda g: g.scalar.activation(out, a, ACT.Copy))
+    def lin(out, a, scale, bias, n, rd, wr, k=1.0, kv=None):
+        op([("A", 0.02 + vc(n, k), f_ac(out, a, ACT.Identity, bias, scale)),
+            ("V", vc(n, kv or k), f_ts(out, a, scale, bias, ALU.mult, ALU.add))], rd, wr)
+
+    def mset(out, val, n, wr, k=1.0):
+        op([("V", vc(n, k), lambda g: g.vector.memset(out, val))], [], wr)
 
     def mm(lst, cyc, rd, wr):
         def fn(g):
@@ -80,321 +125,377 @@ def build(T, topo, core, nxt):
             for (o, l, rh, st, sp) in lst:
                 r = g.tensor.matmul(o, l, rh, st, sp)
             return r
-        op("P", PAR["mmo"] * len(lst) + cyc * PEC, rd, wr, fn)
+        op([("P", PAR["mmo"] * len(lst) + cyc * PEC, fn)], rd, wr)
 
-    def dma(q, pairs, sem, rd, wr, lat):
+    def dma(q, pairs, sem, rd, wr, lat, first=False):
         def fn(g):
             e = g.sync if q == "S" else g.scalar
             for (o, i) in pairs:
                 e.dma_start(o, i).then_inc(T.sem[sem], 16)
-        op(q, 0.06 * len(pairs), rd, wr, fn, sem=sem, n=16 * len(pairs), lat=lat)
+        op([(q, 0.06 * len(pairs), fn)], rd, wr, sem=sem, n=16 * len(pairs), lat=lat, first=first)
 
     rid, pid = topo.addr(nxt)[0], topo.addr(nxt)[1]
     mask = topo.mask(core, nxt)
     neng = len(topo.engines(core, nxt))
+    nsend = [0]
 
-    def send(dst, src, sem, rd, wr, link):
-        op("G", 0.5, rd, wr, lambda g: g.remote_dma(dst, src, T.sem[sem], T.sem.sent, pid, rid, mask), sem=sem, n=neng,
+    def send(dst, src, rd, wr, link):
+        sem = "r%d" % nsend[0]
+        nsend[0] += 1
+        op([("G", 0.5, lambda g: g.remote_dma(dst, src, T.sem[sem], T.sem.sent, pid, rid, mask))], rd, wr, sem=sem, n=neng,
            lat=PAR["lat"] + link, link=link)
 
     def iota(out, pat, base, cm, n, wr, flag=True):
         if flag:
-            op("G", 0.15 + 2 * n * CYC, [], wr, lambda g: g.iota(out, pat, base, cm, allow_small_or_imprecise_dtypes=True))
+            op([("G", 0.15 + 2 * n * CYC, lambda g: g.iota(out, pat, base, cm, allow_small_or_imprecise_dtypes=True))], [], wr)
         else:
-            op("G", 0.15 + 2 * n * CYC, [], wr, lambda g: g.iota(out, pat, base, cm))
+            op([("G", 0.15 + 2 * n * CYC, lambda g: g.iota(out, pat, base, cm))], [], wr)
 
     def ms(out, val, n, wr):
         iota(out, [[0, n]], int(val), 0, n, wr)
 
-    def sel(B, pat, o, fill, base, cm, n, k, zero=None):
-        src = B if zero is None else zero
-        op("G", 0.2 + 2 * n * CYC, [k, "ZZ"], [k], lambda g: g.affine_select(B, src, pat, o, fill, base, cm))
+    def sel(B, pat, o, fill, base, cm, n, k, src):
+        op([("G", 0.2 + 2 * n * CYC, lambda g: g.affine_select(B, src, pat, o, fill, base, cm))], ["ZZ"], [k])
 
     C = lambda i: T.COL[:, i:i + 1]
-    SL = lambda v: T["S%d_" % v]
-    for c in range(5):
-        dma("S" if c % 2 == 0 else "A", [(T.R[:, 512 * c:512 * c + 512], T.recs[:, 512 * c:512 * c + 512])], "lr%d" % c, [], ["R%d" % c], 2.2 + 0.9 * c)
-    dma("A", [(T.SGI[:, 0:1], T.sg[:])], "lsg", [], ["SGI"], 2.0)
-    dma("S", [(T.STI[:], T.st0[:])], "lst", [], ["STI"], 3.0)
-    for p in range(4):
-        dma("S", [(T.XS[:, 128 * a:128 * (a + k)], T.cx0[:, 128 * b:128 * (b + k)]) for (a, b, k) in RUNS[p]], "lx%d" % p, [], ["XS%d" % p], 5.5 + 0.5 * p)
+    SLs = lambda v: T["S%d_" % v]
+    bk = lambda name, pos, n: ["%s_%d" % (name, p) for p in range(pos, pos + n)]
+    cs = lambda pos, n: slice(128 * pos, 128 * (pos + n))
+    ls = lambda pos, n: slice(8 * pos, 8 * (pos + n))
+    b0 = blocks(0)
+    RP = [sum(PAR["rp"][:i]) for i in range(len(PAR["rp"]) + 1)]
+    NR = len(PAR["rp"])
+    dma("A", [(T.SGI[:, 0:1], T.sg[:])], "lsg", [], ["SGI"], 2.0, True)
+    dma("S", [(T.STI[:], T.st0[:])], "lst", [], ["STI"], 2.2, True)
+    for c in range(NR):
+        dma("S" if c % 2 == 0 else "A", [(T.R[:, RP[c]:RP[c + 1]], T.recs[:, RP[c]:RP[c + 1]])], "lr%d" % c, [], ["R%d" % c], 2.3 + 4.2 * RP[c + 1] / V0, True)
+    first_pieces = [p for ch in chunks(0) for p in ch[4]]
+    for i, (pos, n, _a, _b, _c) in enumerate(first_pieces):
+        dma("S", [(T.XS[:, cs(a, k)], T.cx0[:, cs(b, k)]) for (a, b, k) in runs(pos, n, b0)], "lx%d" % i, [], ["XS%d" % i], 6.3 + 0.4 * i, True)
     iota(T.PC[:, 0:1], [[0, 1]], 0, 1, 1, ["PC0"], False)
     iota(T.IO[:], [[1, 256]], 0, 0, 256, ["IO"])
     iota(T.IG[:], [[1, 8], [0, 16]], 0, 0, 128, ["IG"])
     iota(T.IR[:], [[0, 8], [1, 16]], 0, 0, 128, ["IR"])
-    iota(T.MD[:], [[16, 8]], DUMMY - int(OFF), 0, 8, ["MD"])
-    op("V", vc(512), [], ["ZZ"], lambda g: g.vector.memset(T.ZZ[:], 0.0))
-    for (B, pat, n, f, k) in ((T.SEL, [[-16, 8], [0, 128]], 1024, 1.0, "SEL"), (T.NSEL, [[0, 4], [-16, 8], [0, 16]], 512, -1.0, "NSEL")):
-        for r in (12, 14):
-            sel(B[:], pat, ALU.not_equal, f, -r, 1, n, k, T.ZZ[:, 0:n] if r == 12 else None)
-    sel(T.TRI[:], [[16, 8], [0, 8], [1, 16]], ALU.is_gt, 0.5, 0, -1, 1024, "TRI", T.ZZ[:])
+    iota(T.MD[:], [[16, 8]], DUMMY, 0, 8, ["MD"])
+    iota(T.I4[:, 0:32], [[1, 4], [4, 8]], 0, 0, 32, ["I4a"])
+    iota(T.I4[:, 32:96], [[0, 16], [1, 4]], 0, 0, 64, ["I4b"])
+    iota(T.I4[:, 96:160], [[0, 2], [1, 8], [0, 4]], 0, 0, 64, ["I4c"])
+    mset(T.ZZ[:, 0:512], 11.0, 512, ["ZZ"], 0.5)
+    mset(T.ZZ[:, 512:1024], 0.0, 512, ["ZZ"], 0.5)
+    sel(T.TRI[:, 0:512], [[16, 8], [0, 4], [1, 16]], ALU.is_gt, 99.0, 0, -1, 512, "TRI0", T.ZZ[:, 0:512])
+    if PAR["ea"]:
+        sel(T.TRI[:, 512:1024], [[16, 8], [0, 4], [1, 16]], ALU.is_gt, -64.0, 0, -1, 512, "TRI1", T.ZZ[:, 512:1024])
     for h, f in ((0, BIG), (1, -BIG)):
-        sel(T.BE[:, 128 * h:128 * h + 128], [[-1, 128]], ALU.not_equal, f, 0, 1, 128, "BE%d" % h, T.ZZ[:, 0:128])
-    ms(T.CN[:, V0:WD_], 0, 640, ["CN5"])
+        sel(T.BE[:, 128 * h:128 * h + 128], [[-1, 128]], ALU.not_equal, f, 0, 1, 128, "BE%d" % h, T.ZZ[:, 512:640])
+    ms(T.F[:, V0:WD_], 0, 640, ["F%d" % NR])
+    for a in range(4):
+        iota(T.IDT[:, 800 * a:800 * a + 800], [[1, 800]], 800 * a, 0, 800, ["ID%d" % a])
     ms(T.ONE[:, 0:2], BIG, 2, ["ONEa"])
-    ms(T.ONE[:, 2:4], 1, 2, ["ONEb"])
-    ms(T.ONE[:, 8:16], -OFF / 16, 8, ["ONEc"])
-    ms(T.ONE[:, 16:24], 1, 8, ["ONEd"])
-    ms(T.CP[:], 0, 16, ["CP"])
-    ms(T.FR[:, 0:1], V0 - BIG, 1, ["FR0"])
-    op("V", vc(64), [], ["THCa"], lambda g: g.vector.memset(T.THC[:, 0:64], 0.125))
-    op("V", vc(64), [], ["THCb"], lambda g: g.vector.memset(T.THC[:, 64:128], -0.125))
+    ms(T.ONE[:, 2:4], 1.0, 2, ["ONEb"])
+    ms(T.ONE[:, 16:24], (V0 - BIG) / 16, 8, ["ONEd"])
+    ms(T.ONE[:, 24:32], (V0 + BIG) / 16, 8, ["ONEe"])
+    ms(T.ONE[:, 32:40], BIG / 16, 8, ["ONEf"])
+    ms(T.CP[:], 0.0, 16, ["CP"])
+    ms(T.PW[:, 16:32], 1.0, 16, ["PW1"])
+    mset(T.THC[:, 0:64], 0.5, 64, ["THCa"])
+    mset(T.THC[:, 64:128], -0.5, 64, ["THCb"])
     ts(T.PC[:, 4:5], T.PC[:, 0:1], 4, None, ALU.arith_shift_right, None, 1, ["PC0"], ["PC4"])
     ts(T.PC[:, 8:9], T.PC[:, 0:1], 15, None, ALU.bitwise_and, None, 1, ["PC0"], ["PC8"])
-    (P_, G_, R_, LT12, LT14, GE14, GE12, CH_, C1, CW, CA, CB, CR, E_, M1213, M1214, SIG, TAU, ODD, FW, FW2, PP2, PM2, NO13, NO15, PO13) = range(26)
+    ts(T.PC[:, 9:10], T.PC[:, 0:1], 7, None, ALU.bitwise_and, None, 1, ["PC0"], ["PC9"])
+    ts(T.PC[:, 10:11], T.PC[:, 0:1], 3, None, ALU.bitwise_and, None, 1, ["PC0"], ["PC10"])
+    ts(T.PC[:, 11:12], T.PC[:, 0:1], 16, None, ALU.bitwise_and, None, 1, ["PC0"], ["PC11"])
+    ts(T.PC[:, 12:13], T.PC[:, 0:1], 2, None, ALU.arith_shift_right, None, 1, ["PC0"], ["PC12"])
+    (G_, P_, R_, R8, R4, P16, P4, LT12, LT14, GE14, CH_, CR, E_, M1213, M1214, SIG, TAU, ODD, BI, BI0, CSL, CH2, CQ4, CE8, CSC, CSM, CSW,
+     CQ, CE, C14, PWC, PWL, PWH, LT8, CSI, ME, MO, K15, PO, M256, XP, XM) = range(42)
     k_ = lambda *a: ["c%d" % i for i in a]
     r16 = lambda i: T.R16[:, i:i + 1]
     IO = T.IO[:, 0:128]
     MT = lambda i: T.MT[:, 128 * i:128 * i + 128]
-    cp(C(P_), T.PC[:, 0:1], 1, ["PC0"], k_(P_))
     cp(C(G_), T.PC[:, 4:5], 1, ["PC4"], k_(G_))
-    cp(C(R_), T.PC[:, 8:9], 1, ["PC8"], k_(R_))
+    cp(C(P_), T.PC[:, 0:1], 1, ["PC0"], k_(P_))
+    cp(T.COL[:, R_:R_ + 5], T.PC[:, 8:13], 5, ["PC8", "PC9", "PC10", "PC11", "PC12"], k_(R_, R8, R4, P16, P4))
     cp(C(E_), T.SGI[:, 0:1], 1, ["SGI"], k_(E_))
     ts(C(LT14), C(R_), 14.0, None, ALU.is_lt, None, 1, k_(R_), k_(LT14))
-    ts(T.M1[:], IO, C(P_), C(LT14), ALU.is_equal, ALU.mult, 128, ["IO"] + k_(P_, LT14), ["M1"])
-    ts(T.R16[:], T.IO[:, 0:16], C(R_), None, ALU.is_equal, None, 16, ["IO"] + k_(R_), ["R16"])
-    tt(C(M1213), r16(12), r16(13), ALU.add, 1, ["R16"], k_(M1213))
-    ts(C(NO13), C(M1213), -OFF, None, ALU.mult, None, 1, k_(M1213), k_(NO13))
-    ts(C(PP2), C(P_), 2.0, None, ALU.add, None, 1, k_(P_), k_(PP2))
-    ts(MT(0), IO, C(PP2), C(M1213), ALU.is_equal, ALU.mult, 128, ["IO"] + k_(PP2, M1213), ["MT0"])
-    ts(MT(1), IO, C(P_), C(M1213), ALU.is_equal, ALU.mult, 128, ["IO"] + k_(P_, M1213), ["MT1"])
-    tt(T.M2[:], MT(0), MT(1), ALU.subtract, 128, ["MT0", "MT1"], ["M2"])
     ts(C(LT12), C(R_), 12.0, None, ALU.is_lt, None, 1, k_(R_), k_(LT12))
     ts(C(GE14), C(R_), 14.0, None, ALU.is_ge, None, 1, k_(R_), k_(GE14))
-    ts(C(NO15), C(R_), 14.0, -OFF, ALU.is_ge, ALU.mult, 1, k_(R_), k_(NO15))
-    ts(C(GE12), C(R_), 12.0, None, ALU.is_ge, None, 1, k_(R_), k_(GE12))
-    ts(C(CH_), C(R_), 12.0, 0.5, ALU.is_lt, ALU.mult, 1, k_(R_), k_(CH_))
-    ts(C(C1), C(GE12), 1.0 / 128, C(CH_), ALU.mult, ALU.add, 1, k_(GE12, CH_), k_(C1))
-    tt(C(CW), C(CH_), C(GE12), ALU.add, 1, k_(CH_, GE12), k_(CW))
-    ts(C(CA), r16(12), -0.5, None, ALU.mult, None, 1, ["R16"], k_(CA))
-    ts(C(CB), r16(13), -1.0 / 512, C(CA), ALU.mult, ALU.add, 1, ["R16"] + k_(CA), k_(CB))
-    ts(C(CR), C(LT12), 0.75, 127.0, ALU.mult, ALU.add, 1, k_(LT12), k_(CR))
-    tt(C(M1214), r16(12), r16(14), ALU.add, 1, ["R16"], k_(M1214))
-    tt(C(ODD), r16(13), r16(15), ALU.add, 1, ["R16"], k_(ODD))
-    tt(C(SIG), C(ODD), C(M1214), ALU.subtract, 1, k_(ODD, M1214), k_(SIG))
-    ts(C(TAU), C(M1214), -0.25, C(LT12), ALU.mult, ALU.add, 1, k_(M1214, LT12), k_(TAU))
+    lin(C(CH_), C(LT12), 0.5, 0.0, 1, k_(LT12), k_(CH_))
+    lin(C(CQ), C(LT12), 0.25, 0.0, 1, k_(LT12), k_(CQ))
+    ts(T.R16[:], T.IO[:, 0:16], C(R_), None, ALU.is_equal, None, 16, ["IO"] + k_(R_), ["R16"])
+    lin(C(C14), r16(14), -2050.0, 0.0, 1, ["R16"], k_(C14))
+    lin(C(K15), r16(15), 1.0 / 128, 0.0, 1, ["R16"], k_(K15))
+    lin(C(M1213), r16(12), 1.0, r16(13), 1, ["R16"], k_(M1213))
+    lin(C(PO), C(M1213), OFF, 0.0, 1, k_(M1213), k_(PO))
+    lin(C(CR), C(LT12), 70.25, 128.0, 1, k_(LT12), k_(CR))
+    lin(C(XP), C(LT12), 16.0, 128.0, 1, k_(LT12), k_(XP))
+    lin(C(XM), C(LT12), -16.0, -128.0, 1, k_(LT12), k_(XM))
+    lin(C(M1214), r16(12), 1.0, r16(14), 1, ["R16"], k_(M1214))
+    lin(C(ODD), r16(13), 1.0, r16(15), 1, ["R16"], k_(ODD))
+    lin(C(SIG), C(M1214), -1.0, C(ODD), 1, k_(ODD, M1214), k_(SIG))
+    lin(C(TAU), C(SIG), 0.5, C(LT12), 1, k_(SIG, LT12), k_(TAU))
+    lin(C(BI0), r16(14), 4092.0, 0.0, 1, ["R16"], k_(BI0))
+    lin(C(M256), r16(15), 128.0, C(BI0), 1, ["R16"] + k_(BI0), k_(M256))
+    lin(C(BI), C(M1213), -OFF, C(M256), 1, k_(M1213, M256), k_(BI))
+    lin(C(CSL), r16(15), -1.125, C(LT12), 1, ["R16"] + k_(LT12), k_(CSL))
+    lin(C(CH2), r16(15), -253.0 / 512, C(CH_), 1, ["R16"] + k_(CH_), k_(CH2))
+    lin(C(CQ4), r16(15), -219.0 / 2048, C(CQ), 1, ["R16"] + k_(CQ), k_(CQ4))
+    lin(C(CSC), C(C14), -1.0, C(CH_), 1, k_(C14, CH_), k_(CSC))
+    lin(C(CSM), r16(15), -9.0 / 128, C(C14), 1, ["R16"] + k_(C14), k_(CSM))
+    lin(C(CSW), r16(15), -9.0 / 128, C(CH_), 1, ["R16"] + k_(CH_), k_(CSW))
     ts(T.EYH[:], IO, C(P_), None, ALU.is_equal, None, 128, ["IO"] + k_(P_), ["EYH"])
-    ts(T.S2[:], IO, C(P_), C(CH_), ALU.is_equal, ALU.mult, 128, ["IO"] + k_(P_, CH_), ["S2"])
-    ts(T.SW[:], IO, C(P_), C(CW), ALU.is_equal, ALU.mult, 128, ["IO"] + k_(P_, CW), ["SW"])
     ts(T.OB[:], T.IG[:], C(G_), None, ALU.is_equal, None, 128, ["IG"] + k_(G_), ["OB"])
-    ts(T.G2[:], T.IR[:], 12.0, None, ALU.is_lt, None, 128, ["IR"], ["G2"])
-    tt(T.KP[:], T.G2[:], T.OB[:], ALU.mult, 128, ["G2", "OB"], ["KP"])
-    ts(MT(2), T.KP[:], C(CA), None, ALU.mult, None, 128, ["KP"] + k_(CA), ["MT2"], 0.5)
-    ts(MT(3), IO, C(P_), C(C1), ALU.is_equal, ALU.mult, 128, ["IO"] + k_(P_, C1), ["MT3"])
-    tt(T.S1[:], MT(2), MT(3), ALU.add, 128, ["MT2", "MT3"], ["S1"])
-    ts(T.YY[:], T.KP[:], C(CB), None, ALU.mult, None, 128, ["KP"] + k_(CB), ["YY"], 0.5)
-    tt(T.SD[:], T.YY[:], T.S2[:], ALU.add, 128, ["YY", "S2"], ["SD"])
+    ts(T.GA[:, 0:128], T.IR[:], 12.0, C(GE14), ALU.is_lt, ALU.mult, 128, ["IR"] + k_(GE14), ["GA0"])
+    tt(T.GA[:, 128:256], T.GA[:, 0:128], T.OB[:], ALU.mult, 128, ["GA0", "OB"], ["GA1"], 2.0)
+    lin(T.GB[:, 0:128], T.EYH[:], C(LT12), 0.0, 128, ["EYH"] + k_(LT12), ["GB0"], 1.0, 0.5)
+    tt(T.B0[:], T.GA[:, 128:256], T.GB[:, 0:128], ALU.add, 128, ["GA1", "GB0"], ["B0"], 2.0)
+    ac(T.EYB[:], T.IR[:], ACT.Abs, -12.5, 1.0, 128, ["IR"], ["EYB"])
+    ts(T.GB[:, 128:256], T.EYB[:], 1.0, C(K15), ALU.is_lt, ALU.mult, 128, ["EYB"] + k_(K15), ["GB1"], 0.5)
+    tt(MT(0), T.GB[:, 128:256], T.OB[:], ALU.mult, 128, ["GB1", "OB"], ["MT0"], 2.0)
+    mats = [("H2", CH2), ("Q4", CQ4), ("SC", CSC)]
+    if "nn" in PAR["mode"].values():
+        lin(C(CE), C(LT12), 0.125, 0.0, 1, k_(LT12), k_(CE))
+        lin(C(CE8), r16(15), 17.0 / 1024, C(CE), 1, ["R16"] + k_(CE), k_(CE8))
+        mats.append(("E8", CE8))
+    for (M, col) in mats:
+        lin(T[M][:], T.B0[:], C(col), 0.0, 128, ["B0"] + k_(col), [M], 1.0, 0.5)
+    for (M, col, i) in (("SL", CSL, 1), ("SM", CSM, 2)):
+        lin(MT(i), T.B0[:], C(col), 0.0, 128, ["B0"] + k_(col), ["MT%d" % i], 1.0, 0.5)
+        tt(T[M][:], MT(i), MT(0), ALU.add, 128, ["MT0", "MT%d" % i], [M], 2.0)
     ts(T.G8[:], T.IO[:, 0:8], C(G_), None, ALU.is_equal, None, 8, ["IO"] + k_(G_), ["G8"])
-    for kind, col, f in ((0, E_, 1.0), (1, E_, -1.0), (2, ODD, 1.0), (3, M1214, 1.0)):
-        ts(T.WV[:, 8 * kind:8 * kind + 8], T.G8[:], C(col), f, ALU.mult, ALU.mult, 8, ["G8"] + k_(col), ["WV%d" % kind])
+    lin(T.WV[:, 0:8], T.G8[:], C(E_), 0.0, 8, ["G8"] + k_(E_), ["WV0"])
+    lin(T.WV[:, 8:16], T.WV[:, 0:8], -1.0, 0.0, 8, ["WV0"], ["WV1"])
+    lin(T.WV[:, 16:24], T.G8[:], r16(13), 0.0, 8, ["G8", "R16"], ["WV2"])
+    lin(T.WV[:, 24:32], T.G8[:], r16(12), 0.0, 8, ["G8", "R16"], ["WV3"])
     WVK = ["WV%d" % i for i in range(4)]
-    for c in range(2):
-        cp(T["Z%d" % c][:], T.ZZ[:, 0:272], 272, ["ZZ"], ["Z%d" % c], 0.5)
-    ac(T.W[:, V0:WD_], T.CN[:, V0:WD_], ACT.Identity, C(NO15), 1.0, 640, ["CN5"] + k_(NO15), ["W5"])
-    ts(T.OO[:, 0:16], T.IO[:, 0:16], 256.0, C(GE14), ALU.mult, ALU.mult, 16, ["IO"] + k_(GE14), ["OOa", "OOb"])
-    ts(T.HM[:], T.OO[:, 0:16], C(NO15), None, ALU.add, None, 16, ["OOa", "OOb"] + k_(NO15), ["HM"])
+    for z in ("ZA", "ZB", "ZT", "ZL"):
+        mset(T[z][:], 0.0, 272, [z], 0.5)
+    ms(T.ZF[:], 0, 272, ["ZF"])
+    mset(T.PW[:, 8:16], 0.5, 8, ["PW0"])
+    op([("V", vc(8), lambda g: g.vector.tensor_tensor_scan(T.PW[:, 0:8], T.PW[:, 8:16], T.ZZ[:, 512:520], 1.0, ALU.mult, ALU.add))], ["PW0", "ZZ"], ["PWa"])
+    ts(T.NE[:], T.IO[:, 0:8], C(R8), None, ALU.is_equal, None, 8, ["IO"] + k_(R8), ["NE"])
+    tt(T.A2[:, 0:8], T.NE[:], T.PW[:, 0:8], ALU.mult, 8, ["NE", "PWa"], ["A2s"])
+    op([("V", vc(8), lambda g: g.vector.tensor_reduce(C(PWC), T.A2[:, 0:8], AX.X, ALU.add))], ["A2s"], k_(PWC))
+    ts(C(LT8), C(R_), 8.0, None, ALU.is_lt, None, 1, k_(R_), k_(LT8))
+    lin(C(PWL), C(PWC), C(LT8), 0.0, 1, k_(PWC, LT8), k_(PWL))
+    ts(C(PWH), C(PWC), C(PWL), C(LT12), ALU.subtract, ALU.mult, 1, k_(PWC, PWL, LT12), k_(PWH))
+    lin(C(CSI), C(LT8), 2.0, 0.0, 1, k_(LT8), k_(CSI))
+    lin(T.BU[:], T.IO[:], C(PWL), -0.499, 256, ["IO"] + k_(PWL), ["BU"])
+    ts(T.BR[:], T.BU[:], MAGIC, MAGIC, ALU.add, ALU.subtract, 256, ["BU"], ["BR"])
+    tt(T.BB[:], T.BU[:], T.BR[:], ALU.is_gt, 256, ["BU", "BR"], ["BB"], 2.0)
+    lin(T.OO[:, 0:16], T.IO[:, 0:16], C(PWH), -0.499, 16, ["IO"] + k_(PWH), ["OOa"])
+    ts(T.OO[:, 16:32], T.OO[:, 0:16], MAGIC, MAGIC, ALU.add, ALU.subtract, 16, ["OOa"], ["OOb"])
+    tt(T.DUM[:], T.OO[:, 0:16], T.OO[:, 16:32], ALU.is_gt, 16, ["OOa", "OOb"], ["DUM", "DUMb"])
+    ts(T.HM[:], T.DUM[:], 2.0, C(LT12), ALU.mult, ALU.subtract, 16, ["DUM", "DUMb"] + k_(LT12), ["HM"])
     for a in range(13):
         w = min(256, WD_ - 256 * a)
-        ac(T.ID[:, 256 * a:256 * a + w], T.IO[:, 0:w], ACT.Identity, T.HM[:, a:a + 1], C(M1213), w, ["IO", "HM"] + k_(M1213), ["ID%d" % a])
-    IDK = ["ID%d" % a for a in range(13)]
-    ts(T.WB[:], T.IG[:], C(G_), C(E_), ALU.is_equal, ALU.mult, 128, ["IG"] + k_(G_, E_), ["WB"])
-    ts(T.G1[:], T.IR[:], C(R_), None, ALU.is_gt, None, 128, ["IR"] + k_(R_), ["G1"])
-    tt(T.TB[:], T.G1[:], T.OB[:], ALU.mult, 128, ["G1", "OB"], ["TB"])
-    ts(T.WN[:, 0:128], T.IG[:], C(G_), C(GE14), ALU.is_equal, ALU.mult, 128, ["IG"] + k_(G_, GE14), ["WNa"])
-    ac(T.WN[:, 128:256], T.WN[:, 0:128], ACT.Copy, 0.0, -1.0, 128, ["WNa"], ["WNb"])
-    ts(T.GS[:], T.IR[:], C(R_), 65536.0, ALU.not_equal, ALU.mult, 128, ["IR"] + k_(R_), ["GS"])
-    ac(T.THR[:, 0:128], T.GS[:], ACT.Identity, 5.0, -1.0, 128, ["GS"], ["THRa"])
-    ac(T.THR[:, 128:256], T.GS[:], ACT.Identity, 21.0, -1.0, 128, ["GS"], ["THRb"])
-    ts(T.DUM[:], T.MD[:], C(R_), None, ALU.add, None, 8, ["MD"] + k_(R_), ["DUM"])
-    for c in range(5):
-        sl = slice(512 * c, 512 * c + 512)
-        yb = T.YB[:, 512 * (c % 2):512 * (c % 2) + 512]
-        ps = "PS%d" % (c % 4)
-        cp(T.CN[:, sl], T.R[:, sl], 512, ["R%d" % c], ["CN%d" % c])
-        ac(yb, T.CN[:, sl], ACT.Identity, C(NO13), 1.0, 512, ["CN%d" % c] + k_(NO13), ["YB%d" % (c % 2)])
-        mm([(T[ps][:], T.M1[:], T.CN[:, sl], True, False), (T[ps][:], T.M2[:], yb, False, True)], 2560,
-           ["M1", "M2", "CN%d" % c, "YB%d" % (c % 2)], [ps])
-        if c % 2 == 0:
-            ts(T.W[:, sl], T[ps][:], C(NO13), None, ALU.add, None, 512, k_(NO13), [ps, "W%d" % c])
+        lin(T.BT[:, 256 * a:256 * a + w], T.BB[:, 0:w], C(CSI), T.HM[:, a:a + 1], w, ["BB", "HM"] + k_(CSI), ["BT%d" % a], 1.0, 0.5)
+    IDK, BK = ["ID%d" % a for a in range(4)], ["BT%d" % a for a in range(13)]
+    ts(C(ME), C(P16), 0.0, C(LT12), ALU.is_equal, ALU.mult, 1, k_(P16, LT12), k_(ME))
+    lin(C(MO), C(ME), -1.0, C(LT12), 1, k_(LT12, ME), k_(MO))
+    lin(T.WB[:], T.OB[:], C(E_), 0.0, 128, ["OB"] + k_(E_), ["WB"], 1.0, 0.5)
+    ts(T.GA[:, 0:128], T.IR[:], C(R_), None, ALU.is_gt, None, 128, ["IR"] + k_(R_), ["GA0"])
+    tt(T.TB[:], T.GA[:, 0:128], T.OB[:], ALU.mult, 128, ["GA0", "OB"], ["TB"], 2.0)
+    ts(T.WN[:, 0:32], T.I4[:, 96:128], C(G_), C(GE14), ALU.is_equal, ALU.mult, 32, ["I4c"] + k_(G_, GE14), ["WNa"])
+    lin(T.WN[:, 32:64], T.WN[:, 0:32], -1.0, 0.0, 32, ["WNa"], ["WNb"])
+    ts(T.GS[:, 0:64], T.I4[:, 32:96], C(R4), -65536.0, ALU.not_equal, ALU.mult, 64, ["I4b"] + k_(R4), ["GS"])
+    lin(T.THR[:, 0:32], T.GS[:, 0:32], 1.0, 5.0, 32, ["GS"], ["THRa"])
+    lin(T.THR[:, 32:64], T.GS[:, 32:64], 1.0, 21.0, 32, ["GS"], ["THRb"])
+    ts(T.EYK[:], T.I4[:, 0:32], C(P4), None, ALU.is_equal, None, 32, ["I4a"] + k_(P4), ["EYK"])
+    if PAR["ea"]:
+        lin(T.EYB[:], T.EYH[:], 1.0, 0.0, 128, ["EYH"], ["EYB"], 1.0, 0.5)
+    lin(T.DUM[:, 0:8], T.MD[:], 1.0, C(R_), 8, ["MD"] + k_(R_), ["DUM"])
+    lin(T.DUM[:, 8:16], T.MD[:], 1.0, C(R_), 8, ["MD"] + k_(R_), ["DUMb"])
+    lin(MT(1), T.B0[:], C(CSW), 0.0, 128, ["B0"] + k_(CSW), ["MT1"], 1.0, 0.5)
+    lin(MT(2), MT(0), OFF, 0.0, 128, ["MT0"], ["MT2"], 1.0, 0.5)
+    lin(MT(3), T.EYH[:], C(M1213), 0.0, 128, ["EYH"] + k_(M1213), ["MT3"], 1.0, 0.5)
+    tt(T.FT[:], MT(1), MT(2), ALU.add, 128, ["MT1", "MT2"], ["FT"], 2.0)
+    tt(T.SW[:], T.FT[:], MT(3), ALU.add, 128, ["FT", "MT3"], ["SW"], 2.0)
+    for c in range(NR):
+        lin(T.F[:, RP[c]:RP[c + 1]], T.R[:, RP[c]:RP[c + 1]], 1.0, 0.0, RP[c + 1] - RP[c], ["R%d" % c], ["F%d" % c])
+    FK = ["F%d" % c for c in range(NR + 1)]
+    CK = ["CNa", "CNb"]
+    dma("S", [(T.CN[:], T.F[:])], "lcn", FK + ["XS%d" % (len(first_pieces) - 2)], CK + ["CNd"], 6.0)
+    dma("S", [(T.yp[16 * g:16 * g + 12, 0:V0], T.F[16 * g:16 * g + 12, 0:V0]) for g in range(8)], "stat",
+        FK[:NR] + ["CNd", "XS%d" % (len(first_pieces) - 1)], ["ypa"], 6.0)
+    for i, (pos, n, _a, _b, _c) in enumerate(first_pieces):
+        lin(T.X0[:, cs(pos, n)], T.XS[:, cs(pos, n)], 1.0, C(XP), 128 * n, ["XS%d" % i] + k_(XP) + bk("XF", pos, n), bk("X0", pos, n), 1.0, 0.5)
+    for ch in chunks(0):
+        for (a, b, k) in runs(ch[2], ch[3], b0):
+            cp(SLs(0)[:, ls(a, k)], T.STI[:, ls(b, k)], 8 * k, ["STI"], bk("S0", a, k))
+    Fwin, Cwin, Iwin = T.F[:, 0:WD_], T.CN[:, 0:WD_], T.IDT[:, 0:WD_]
+    GK = FK + k_(LT14, BI)
+
+    def where(v):
+        if v == NV - 1:
+            return {p: p for p in blocks(v)}
+        back = {b: p for p, b in blocks(v + 1).items()}
+        return {p: back[b] for p, b in blocks(v).items()}
+
+    def send_list(v, pos, n):
+        if v < NV - 1:
+            for (a, b, k) in runs(pos, n, where(v)):
+                send(SLs(v + 1)[:, ls(b, k)], T["U%d" % v][:, ls(a, k)], bk("U%d" % v, a, k), bk("S%d" % (v + 1), b, k), PAR["ls"])
         else:
-            ac(T.W[:, sl], T[ps][:], ACT.Identity, C(NO13), 1.0, 512, k_(NO13), [ps, "W%d" % c])
-    WK = ["W%d" % c for c in range(6)]
-    CK = ["CN%d" % c for c in range(6)]
-    dma("S", [(T.yp[16 * g:16 * g + 12, 0:V0], T.CN[16 * g:16 * g + 12, 0:V0]) for g in range(8)], "stat", CK[:5], ["ypa"], 6.0)
-    xk = lambda v, p: "X%d_%d" % (v, p)
-    for p in range(4):
-        ts(T.X0[:, 512 * p:512 * p + 512], T.XS[:, 512 * p:512 * p + 512], 128.0, None, ALU.add, None, 512, ["XS%d" % p], [xk(0, p)], 0.5)
-        for (a, b, k) in RUNS[p]:
-            cp(SL(0)[:, 8 * a:8 * (a + k)], T.STI[:, 8 * b:8 * (b + k)], 8 * k, ["STI"], ["S0_%d" % (p // 2)])
-    Wwin, Cwin, Iwin = T.W[:, 0:WD_], T.CN[:, 0:WD_], T.ID[:, 0:WD_]
-    acc = [0.5]
-    ck = lambda p: ["CG%d" % p, "CH%d" % p]
+            for (a, b, k) in runs(pos, n, blocks(v)):
+                send(T.YS[:, ls(b, k)], T.UF[:, ls(a, k)], bk("UF", a, k), bk("YS", b, k), PAR["ls"])
 
-    def walk(v, c, step):
-        j0, n = CH[c]
-        nb = n // 128
-        H = 16 // nb
-        X = T["X%d" % v]
-        src, sk = [(SL(v), "S%d_%d" % (v, c)), (T.L1, "L1_%d" % c), (T.L2, "L2_%d" % c)][step]
-        dst, dk = [(T.L1, "L1_%d" % c), (T.L2, "L2_%d" % c), (T["U%d" % v], "U%d_%d" % (v, c))][step]
-        pcs = list(range(j0 // 512, (j0 + n) // 512))
-        pv, Z = "pv%d" % c, T["Z%d" % c]
-        PV, b0 = (T.PVa, T.PVb)[c], 0
-        for p in pcs:
-            sl, ps = slice(512 * p, 512 * p + 512), "PS%d" % p
-            mm([(T[ps][:], T.S1[:], X[:, sl], True, True)], 512, ["S1", xk(v, p)], [ps])
-            a = 32 - PAR["split"] if c == v % 2 else 32
-            gat(T.CG[:, 512 * p:512 * p + 16 * a], Wwin.indirect(src[:, 32 * p:32 * p + a]), 16 * a, WK + [sk], ck(p)[0:1] if a < 32 else ck(p))
-            if a < 32:
-                cp(T.CG[:, 512 * p + 16 * a:512 * p + 512], Wwin.indirect(src[:, 32 * p + a:32 * p + 32]), 512 - 16 * a, WK + [sk], ck(p)[1:2], GAT)
-            tt(T.PR[:, sl], T.CG[:, sl], T[ps][:], ALU.mult, 512, ck(p), [ps, "PR%d" % p])
-        mm([(PV[:, b0 + i:b0 + 32 * nb:nb], T.PR[:, j0 + i:j0 + n:nb], T.WV[:], True, True) for i in range(nb)], 64 * nb,
-           WVK + ["PR%d" % p for p in pcs], [pv])
-        sn = T.SN[:, j0 // 8:j0 // 8 + 16 * nb]
-        tt(sn, PV[:, b0:b0 + 16 * nb], T.THC[:, 64 - 8 * nb:64 + 8 * nb], ALU.is_gt, 16 * nb, ["THCa", "THCb"], [pv, "SN%d" % c])
-        tt(Z[:, H:17 * H:H, :], sn, PV[:, b0 + 16 * nb:b0 + 32 * nb], ALU.mult, 16 * nb, ["SN%d" % c], [pv, "Z%d" % c])
-        lo = PV[:, b0 + 32 * nb:b0 + 40 * nb]
-        mm([(lo, Z[:, H * (1 + 8 * hl) - h:H * (9 + 8 * hl) - h, :], T.EYH[:, h:128:H], hl == 0 and h == 0, hl == 1 and h == H - 1)
-            for hl in range(2) for h in range(H)], 128 * H, ["EYH", "Z%d" % c], [pv])
-        ts(dst[:, j0 // 16:(j0 + n) // 16], lo, OFF, None, ALU.add, None, 8 * nb, [], [pv, dk])
-        if c == v % 2 and step > 0:
-            o8 = b0 + 32 * nb + 8 * (POS.index(v) % 4)
-            ac(T.ST[:, 8 * step - 8:8 * step], PV[:, o8:o8 + 8], ACT.Copy, 0.0, 1.0, 8, [], [pv, "STs" if step == 1 else "STt"])
-        for p in pcs:
-            sl, ps = slice(512 * p, 512 * p + 512), "PS%d" % p
-            mm([(T[ps][:], T.S1[:], X[:, sl], True, False), (T[ps][:], T.S2[:], T.CG[:, sl], False, True)], 1024,
-               ["S1", "S2", xk(v, p)] + ck(p), [ps])
-            acc[0] += PAR["round_v"]
-            if acc[0] >= 0.999:
-                acc[0] -= 1.0
-                ts(X[:, sl], T[ps][:], C(CR), None, ALU.add, None, 512, k_(CR), [ps, xk(v, p)])
+    pend, held = {}, {}
+
+    def walk(v, ch, step):
+        name, nb, pos0, nblk, pieces, (pvb, c0, pv) = ch
+        H, M, j0, n = 16 // nb, 128 * nblk // nb, 128 * pos0, 128 * nblk
+        X, xn = T["X%d" % v], "X%d" % v
+        src, sk = [(SLs(v), "S%d" % v), (T.L1, "L1"), (T.L2, "L2")][step]
+        cn = "C%d" % step
+        CB = T[cn]
+        PV, Z, zk = T[pvb], T["Z" + name], "Z" + name
+        last = v == NV - 1
+        for (pos, k, psb, pc, ps) in pieces:
+            sl, PS, w = cs(pos, k), T[psb][:, pc:pc + 128 * k], 128 * k
+            if step == 0:
+                pend[pos], held[pos] = [], False
+            if not held[pos]:
+                mm([(PS, T.SL[:], X[:, sl], True, True)], w, ["SL"] + bk(xn, pos, k) + (["PS1"] if ps[:2] == "ps" else []), [ps])
+            lin(CB[:, sl], Fwin.indirect(src[:, ls(pos, k)]), C(LT14), C(BI), w, GK + bk(sk, pos, k), bk(cn, pos, k), GAT)
+            tt(T.PR[:, sl], CB[:, sl], PS, ALU.mult, w, bk(cn, pos, k), [ps] + bk("PR", pos, k))
+        mm([(PV[0:M, c0 + i:c0 + 32 * nb:nb], T.PR[:, j0 + i:j0 + n:nb], T.WV[:], True, True) for i in range(nb)], max(32, min(64, M)) * nb,
+           WVK + bk("PR", pos0, nblk), [pv])
+        so = {"A": 0, "B": 128, "T": 256, "L": 320}[name]
+        sn = T.SN[0:M, so:so + 16 * nb]
+        tt(sn, PV[0:M, c0:c0 + 16 * nb], T.THC[0:M, 64 - 8 * nb:64 + 8 * nb], ALU.is_gt, 16 * nb, ["THCa", "THCb"], [pv, "SN" + name])
+        tt(Z[0:M, H:17 * H:H, :], sn, PV[0:M, c0 + 16 * nb:c0 + 32 * nb], ALU.mult, 16 * nb, ["SN" + name], [pv, zk])
+        lo = PV[:, c0:c0 + 8 * nblk]
+        mm([(lo, Z[0:M, H * (1 + 8 * hl) - h:H * (9 + 8 * hl) - h, :], T.EYH[0:M, h:M:H], hl == 0 and h == 0, hl == 1 and h == H - 1)
+            for hl in range(2) for h in range(H)], 128 * H, ["EYH", zk], [pv])
+        if step < 2:
+            dst, dk = [(T.L1, "L1"), (T.L2, "L2")][step]
+            lin(dst[:, ls(pos0, nblk)], lo, 1.0, OFF, 8 * nblk, [], [pv] + bk(dk, pos0, nblk))
+        elif name == "T":
+            lin(T.TL[:], lo, 1.0, OFF, 8, [], [pv, "TL"])
+        else:
+            dst, dk = (T.UF, "UF") if last else (T["U%d" % v], "U%d" % v)
+            lin(dst[:, ls(pos0, nblk)], lo, 1.0, OFF, 8 * nblk, [], [pv] + bk(dk, pos0, nblk))
+            send_list(v, pos0, nblk)
+        for (pos, k, psb, pc, ps) in pieces:
+            sl, PS, w = cs(pos, k), T[psb][:, pc:pc + 128 * k], 128 * k
+            pd = pend[pos]
+            md = PAR["mode"]["%s%d" % (name, pos)][step] if step < 2 else "r"
+            lst = list(zip([["H2"], ["Q4", "Q4"], ["E8", "E8", "Q4"]][len(pd)], [xn] + ["C%d" % s for s in pd]))
+            lst += [("H2", cn)] if md == "r" else [("SC", cn), ("SM", cn)]
+            if ps[0] == "P":
+                for i, (m, q) in enumerate(lst):
+                    mm([(PS, T[m][:], T[q][:, sl], i == 0, i == len(lst) - 1)], w, [m] + bk(q, pos, k), [ps])
+                    ops[-1]["cont"] = len(ops) - 2 if i else -1
             else:
-                ac(X[:, sl], T[ps][:], ACT.Identity, C(CR), 1.0, 512, k_(CR), [ps, xk(v, p)])
+                mm([(PS, T[m][:], T[q][:, sl], i == 0, i == len(lst) - 1) for i, (m, q) in enumerate(lst)], w * len(lst),
+                   sorted(set(m for m, q in lst)) + [y for m, q in lst for y in bk(q, pos, k)], [ps])
+            held[pos] = md != "r"
+            if md == "n":
+                pd.append(step)
+                continue
+            pend[pos] = []
+            if md == "x":
+                lin(X[:, sl], PS, C(LT12), C(XP), w, k_(LT12, XP), [ps] + bk(xn, pos, k))
+            else:
+                lin(X[:, sl], PS, 1.0, C(CR), w, k_(CR), [ps] + bk(xn, pos, k))
             if step == 2:
-                if v < NV - 1:
-                    send(T["X%d" % (v + 1)][:, sl], X[:, sl], "ax%d_%d" % (v + 1, p), [xk(v, p)], [xk(v + 1, p)], PAR["lx"])
-                else:
-                    ts(T.XS[:, sl], X[:, sl], -128.0, None, ALU.add, None, 512, [xk(v, p)], ["XS%d" % p], 0.5)
-                    send(T["X%d" % (v + 1)][:, sl], T.XS[:, sl], "ax%d_%d" % (v + 1, p), ["XS%d" % p], [xk(v + 1, p)], PAR["lx"])
+                xo = "X%d" % (v + 1)
+                for (a, b, kk) in ([(a, a, b) for a, b in halves(pos, k)] if last else runs(pos, k, where(v))):
+                    send(T[xo][:, cs(b, kk)], X[:, cs(a, kk)], bk(xn, a, kk), bk(xo, b, kk), PAR["lx"] * kk)
 
-    def send_list(v, c):
-        j0, n = CH[c]
-        cs = slice(j0 // 16, (j0 + n) // 16)
-        send(SL(v + 1)[:, cs], T["U%d" % v][:, cs], "as%d_%d" % (v + 1, c), ["U%d_%d" % (v, c)], ["S%d_%d" % (v + 1, c)], PAR["ls"])
+    def equalities(lst, lk, G, gk, E, ek):
+        for o, col in ((0, ME), (1, MO)):
+            lin(G[:, 128 * o:128 * o + 128], T.BT[:, 0:WD_].indirect(lst), C(col), 0.0, 128, BK + lk + k_(col), [gk + str(o)], GAT)
+        sa = ek in PAR["ea"]
+        if sa:
+            mm([(T.PD1[:], T.EYB[:], T.TRI[:, 512:1024], True, False)], 512, ["EYB", "TRI1"], ["PD1"])
+        for t in range(2):
+            mm([(T["PD%d" % h][:, :, 32 * t + 16 * o:32 * t + 16 * o + 16], G[64 * h + 32 * t:64 * h + 32 * t + 32, 128 * o:128 * o + 128],
+                 G[64 * h + 32 * t:64 * h + 32 * t + 32, 128 * o:128 * o + 128], not (h and sa), not (h and sa) or (t, o) == (1, 1))
+                for h in (1, 0) for o in (0, 1)], 512, [gk + "0", gk + "1"], ["PD0", "PD1"])
+        if sa:
+            ac(E[:, :, 64:128], T.PD1[:], ACT.Relu, -11.0, 1.0, 512, [], ["PD1", ek + "1"])
+        else:
+            tt(E[:, :, 64:128], T.PD1[:], T.TRI[:, 0:512], ALU.is_gt, 512, ["TRI0"], ["PD1", ek + "1"])
+        tt(E[:, :, 0:64], T.PD0[:], T.TRI[:, 0:512], ALU.is_gt, 512, ["TRI0"], ["PD0", ek + "0"])
 
-    def equalities(G, gk, E, ek):
-        for h in (1, 0):
-            PD = T["PD%d" % h]
-            mm([(PD[:], G[:], T.NSEL[:], True, False)] +
-               [(PD[:, :, 16 * q:16 * q + 16], T.SEL[:, 128 * q:128 * q + 128], G[:, 64 * h:64 * h + 64], False, q == 7) for q in range(8)],
-               1024, ["SEL", "NSEL", gk], ["PD%d" % h])
-            tt(E[:, 512 * h:512 * h + 512], PD[:], T.TRI[:, 512 * h:512 * h + 512], ALU.is_equal, 512, ["TRI"], ["PD%d" % h, ek + str(h)])
+    def earlier(o, E, w, st):
+        return [(T.PT[:, o + k:o + 1 + k], E[:, k, :], T.ONE[:, w:w + 1], st, st or k == 7) for k in range(8)]
 
-    def earlier(o, E, w):
-        return [(T.PVa[:, o + k:o + 1 + k], E[:, 128 * k:128 * k + 128], T.ONE[:, w:w + 1], False, k == 7) for k in range(8)]
+    def stage1(v):
+        sL = T.L2[:, ls(18, 1)]
+        equalities(sL, ["L2_18"], T.GA, "GA", T.E1, "E1")
+        lin(T.GS[:], Cwin.indirect(sL), 1.0, 0.0, 128, CK + ["L2_18"], ["GS"], GAT)
+        mm(earlier(384, T.E1, 0, True), 512, ["E10", "E11", "ONEa"], ["pt1"])
+        tt(T.MD[:], T.PT[:, 384:392], T.DUM[:, 0:8], ALU.min, 8, ["DUM"], ["pt1", "MD"])
+        tt(T.IX1[:, 0:8], T.MD[:], sL, ALU.max, 8, ["MD", "L2_18"], ["IXs"])
 
     def train(v):
-        c = v % 2
-        pos = POS.index(v)
-        p = pos // 4
-        tc = slice(128 * pos, 128 * pos + 128)
-        lc = slice(8 * pos, 8 * pos + 8)
-        sL, sk = T.L2[:, lc], "L2_%d" % c
-        tL, tk = T["U%d" % v][:, lc], "U%d_%d" % (v, c)
-        pv, ps = "pvt", "PS%d" % p
-        PV, PS = T.PVa, T[ps]
-        o8 = 256 + 8 * (pos % 4)
-        gat(T.G1[:], Iwin.indirect(sL), 128, IDK + [sk], ["G1"])
-        gat(T.GS[:], Cwin.indirect(sL), 128, CK + [sk], ["GS"])
-        equalities(T.G1, "G1", T.E1, "E1")
-        mm([(PV[:, 448:456], T.OB[:], T.ONE[:, 8:16], True, False)] + earlier(448, T.E1, 0), 576, ["E10", "E11", "ONEa", "ONEc", "OB"], [pv])
-        tt(T.MD[:], PV[:, 448:456], T.DUM[:], ALU.min, 8, ["DUM"], [pv, "MD"])
-        tt(T.A2[:, 0:8], T.MD[:], T.ST[:, 0:8], ALU.max, 8, ["MD", "STs"], ["A2s"])
-        ts(T.IX1[:, 0:8], T.A2[:, 0:8], OFF, None, ALU.add, None, 8, ["A2s"], ["IXs"])
-        tt(T.A2[:, 8:16], (T.PVa, T.PVb)[c][:, o8:o8 + 8], T.MD[:], ALU.max, 8, ["MD"], ["pv%d" % c, "A2t"])
-        ts(T.IX1[:, 8:16], T.A2[:, 8:16], OFF, None, ALU.add, None, 8, ["A2t"], ["IXt"])
-        tt(T.NE[:], T.A2[:, 0:8], T.A2[:, 8:16], ALU.not_equal, 8, ["A2s", "A2t"], ["NE"])
-        mm([(T.PD0[:, 0, :], T.WB[:], T.PR[:, tc], True, True)], 128, ["WB", "PR%d" % p], ["PD0"])
-        ts(T.MB[:], T.PD0[:, 0, :], C(SIG), C(TAU), ALU.mult, ALU.is_gt, 128, k_(SIG, TAU), ["PD0", "MB"])
-        ac(T.NB[:], T.MB[:], ACT.Identity, 1.0, -1.0, 128, ["MB"], ["NB"])
+        tc, lc = cs(18, 1), ls(18, 1)
+        PT = T.PT
+        tt(T.IX1[:, 8:16], T.MD[:], T.TL[:], ALU.max, 8, ["MD", "TL"], ["IXt"])
+        tt(T.NE[:], T.IX1[:, 0:8], T.IX1[:, 8:16], ALU.not_equal, 8, ["IXs", "IXt"], ["NE"])
+        lin(T.FS[:], T.C2[:, tc], 1.0, C(PO), 128, ["C2_18"] + k_(PO), ["FS"])
+        mm([(T.PD0[:, 0:2, :], T.WB[:], T.PR[:, tc], True, True)], 128, ["WB", "PR_18"], ["PD0"])
+        ts(T.MB[:], T.PD0[:, 0:2, :], C(SIG), C(TAU), ALU.mult, ALU.is_gt, 128, k_(SIG, TAU), ["PD0", "MB"])
         tt(Cwin.indirect(T.IX1[:, 0:8]), T.GS[:], T.MB[:], ALU.add, 128, ["IXs", "GS", "MB"], CK, SCA)
         tt(T.GM[:], T.GS[:], T.MB[:], ALU.mult, 128, ["GS", "MB"], ["GM"], 2.0)
-        tt(T.KP[:], T.CG[:, tc], T.NB[:], ALU.mult, 128, ck(p) + ["NB"], ["KP"])
-        gat(T.G2[:], Iwin.indirect(T.IX1[:, 8:16]), 128, IDK + ["IXt"], ["G2"])
-        equalities(T.G2, "G2", T.E2, "E2")
-        gat(T.GT[:], Cwin.indirect(tL), 128, CK + [tk], ["GT"])
-        gat(T.WT[:], Wwin.indirect(tL), 128, WK + [tk], ["WT"])
-        mm([(PS[:, 128:256], T.GM[:], T.WN[:, 0:128], True, True), (PS[:, 256:384], T.GM[:], T.WN[:, 128:256], True, False),
-            (PS[:, 256:384], T.GT[:], T.WN[:, 0:128], False, True)], 1536, ["GM", "GT", "WNa", "WNb"], [ps])
-        tt(T.FL[:], PS[:, 128:384], T.THR[:], ALU.is_lt, 256, ["THRa", "THRb"], [ps, "FL"])
-        mm([(PS[:, 384:512], T.SW[:], T.WT[:], True, False), (PS[:, 384:512], T.SD[:], T["X%d" % v][:, tc], False, True)], 256,
-           ["SW", "SD", "WT", xk(v, p)], [ps])
-        ts(T.WDN[:], PS[:, 384:512], MAGIC, MAGIC, ALU.add, ALU.subtract, 128, [], [ps, "WDN"])
-        mm([(PV[:, 464:472], T.FL[:, 0:128], T.G8[:], True, False), (PV[:, 464:472], T.FL[:, 128:256], T.G8[:], False, False)] +
-           earlier(464, T.E2, 2), 640, ["FL", "G8", "E20", "E21", "ONEb"], [pv])
-        tt(T.CP[:, 0:8], PV[:, 464:472], T.NE[:], ALU.is_lt, 8, ["NE"], [pv, "CP"])
-        fr, f2, fa, fb = (T.FR[:, 8 * v + i:8 * v + i + 1] for i in range(4))
-        fk = "FR%d" % v
-        ac(f2, fr, ACT.Identity, 2 * BIG, 1.0, 1, [fk], [fk + "b"])
-        ac(fa, fr, ACT.Identity, OFF, -1.0, 1, [fk], [fk + "c"])
-        ac(fb, fr, ACT.Identity, OFF - 2 * BIG, -1.0, 1, [fk], [fk + "d"])
-        ac(T.FT[:, 0:8], T.ST[:, 8:16], ACT.Identity, fa, 1.0, 8, ["STt", fk + "c"], ["FTa"])
-        ac(T.FT[:, 8:16], T.DUM[:], ACT.Identity, fb, 1.0, 8, ["DUM", fk + "d"], ["FTb"])
-        op("V", vc(8), ["CP", "ONEd"], ["CX"], lambda g: g.vector.tensor_tensor_scan(T.CX[:, 0:8], T.ONE[:, 16:24], T.CP[:, 0:8], 0.0, ALU.mult, ALU.add))
+        equalities(T.IX1[:, 8:16], ["IXt"], T.GB, "GB", T.E2, "E2")
+        lin(T.GT[:], Cwin.indirect(T.TL[:]), 1.0, 0.0, 128, CK + ["TL"], ["GT"], GAT)
+        lin(T.FT[:], Fwin.indirect(T.TL[:]), C(LT14), C(BI), 128, GK + ["TL"], ["FT"], GAT)
+        mm([(PT[:, 392:456], T.GM[:], T.WN[:], True, False), (PT[:, 424:456], T.GT[:], T.WN[:, 0:32], False, True)], 512,
+           ["GM", "GT", "WNa", "WNb"], ["ptB"])
+        tt(T.ZF[:, 4:68:4, :], PT[:, 392:456], T.THR[:], ALU.is_lt, 64, ["THRa", "THRb"], ["ptB", "ZF"])
+        mm([(PT[:, 0:128], T.SW[:], T.FT[:], True, False), (PT[:, 0:128], T.H2[:], T["X%d" % v][:, tc], False, True)], 256,
+           ["SW", "H2", "FT", "X%d_18" % v], ["ptX"])
+        ts(T.WDN[:], PT[:, 0:128], MAGIC, MAGIC, ALU.add, ALU.subtract, 128, [], ["ptX", "WDN"])
+        mm([(PT[:, 456:464], T.ZF[:, 4 * (1 + 8 * hl) - h:4 * (9 + 8 * hl) - h, :], T.EYK[:, 8 * h:8 * h + 8], hl == 0 and h == 0, False)
+            for hl in range(2) for h in range(4)] + earlier(456, T.E2, 2, False), 1024, ["ZF", "EYK", "E20", "E21", "ONEb"], ["ptW"])
+        tt(T.CP[:, 1:9], PT[:, 456:464], T.NE[:], ALU.is_lt, 8, ["NE"], ["ptW", "CP"])
+        cx = T.CX[:, 16 * v:16 * v + 9]
+        ini = T.CX[:, 16 * v - 8:16 * v - 7] if v else 0.0
+        op([("V", vc(9), lambda g: g.vector.tensor_tensor_scan(cx, T.PW[:, 16:25], T.CP[:, 0:9], ini, ALU.mult, ALU.add))], ["CP", "PW1"], ["CX"])
+        cpv = T.CP[:, 1:9]
 
-        def ranks(o, h):
-            return [(PV[:, o:o + 9], T.TB[:], T.CP[:, 0:9], True, False), (PV[:, o:o + 8], T.BE[:, 128 * h:128 * h + 128], T.CP[:, 0:8], False, False),
-                    (PV[:, o + 1:o + 9], T.OB[:], T.CX[:, 0:8], False, True)]
-        mm(ranks(472, 0), 192, ["TB", "OB", "BE0", "CP", "CX"], [pv])
-        tt(T.OO[:, 0:8], PV[:, 472:480], T.FT[:, 0:8], ALU.max, 8, ["FTa"], [pv, "OOa"])
-        ts(tL, T.OO[:, 0:8], fr, None, ALU.add, None, 8, ["OOa", fk], [tk])
-        send_list(v, c)
-        tt(T.YY[:], Iwin.indirect(tL), T.MB[:], ALU.mult, 128, IDK + [tk, "MB"], ["YY"], GAT)
-        tt(Wwin.indirect(T.IX1[:, 0:8]), T.YY[:], T.KP[:], ALU.add, 128, ["IXs", "YY", "KP"], WK, SCA)
-        mm(ranks(484, 1) + [(PV[:, 496:504], T.BE[:, 128:256], T.CP[:, 0:8], True, True)], 256, ["TB", "OB", "BE1", "CP", "CX"], [pv])
-        tt(T.OO[:, 8:16], PV[:, 484:492], T.FT[:, 8:16], ALU.min, 8, ["FTb"], [pv, "OOb"])
-        ts(T.IX2[:, 8:16], T.OO[:, 8:16], f2, None, ALU.add, None, 8, ["OOb", fk + "b"], ["IXd"])
-        cp(Wwin.indirect(T.IX2[:, 8:16]), T.WDN[:], 128, ["IXd", "WDN"], WK, SCA)
-        tt(T.OO[:, 16:24], PV[:, 496:504], T.DUM[:], ALU.add, 8, ["DUM"], [pv, "OOc"])
-        if v < NV - 1:
-            ac(T.FR[:, 8 * v + 8:8 * v + 9], PV[:, 492:493], ACT.Identity, fr, 1.0, 1, [fk], [pv, "FR%d" % (v + 1)])
-        tt(T.OO[:, 24:32], T.OO[:, 16:24], T.ST[:, 8:16], ALU.max, 8, ["OOc", "STt"], ["OOd"])
-        ts(T.IX2[:, 0:8], T.OO[:, 24:32], OFF, None, ALU.add, None, 8, ["OOd"], ["IXu"])
-        ac(T.H0[:], T.GT[:], ACT.Identity, -0.25, 0.5, 128, ["GT"], ["H0"])
+        def ranks(o, h, w):
+            return [(PT[:, o:o + 8], T.OB[:], T.ONE[:, w:w + 8], True, False), (PT[:, o:o + 8], T.TB[:], cpv, False, False),
+                    (PT[:, o:o + 8], T.BE[:, 128 * h:128 * h + 128], cpv, False, False), (PT[:, o:o + 8], T.OB[:], cx[:, 0:8], False, True)]
+        mm(ranks(464, 0, 16), 256, ["TB", "OB", "BE0", "CP", "CX", "ONEd"], ["ptA"])
+        uL, uk = T["U%d" % v][:, lc], "U%d_18" % v
+        tt(uL, PT[:, 464:472], T.TL[:], ALU.max, 8, ["TL"], ["ptA", uk])
+        if v == NV - 1:
+            lin(T.UF[:, lc], uL, 1.0, 0.0, 8, [uk], ["UF_18"])
+        send_list(v, 18, 1)
+        tt(T.YY[:], Iwin.indirect(uL), T.MB[:], ALU.mult, 128, IDK + [uk, "MB"], ["YY"], GAT)
+        tt(Fwin.indirect(T.IX1[:, 0:8]), T.YY[:], T.FS[:], ALU.max, 128, ["IXs", "YY", "FS"], FK, SCA)
+        mm(ranks(472, 1, 24) + [(PT[:, 480:488], T.OB[:], T.ONE[:, 32:40], True, False), (PT[:, 480:488], T.BE[:, 128:256], cpv, False, True)], 384,
+           ["TB", "OB", "BE1", "CP", "CX", "ONEe", "ONEf"], ["ptC"])
+        tt(T.IX2[:, 0:16], PT[:, 472:488], T.DUM[:], ALU.min, 16, ["DUM", "DUMb"], ["ptC", "IXd"])
+        cp(Fwin.indirect(T.IX2[:, 0:8]), T.WDN[:], 128, ["IXd", "WDN"], FK, SCA)
+        tt(T.IX2[:, 16:24], T.IX2[:, 8:16], T.TL[:], ALU.max, 8, ["IXd", "TL"], ["IXu"])
+        lin(T.H0[:], T.GT[:], 0.5, -0.25, 128, ["GT"], ["H0"])
         ts(T.HF[:], T.H0[:], MAGIC, MAGIC, ALU.add, ALU.subtract, 128, ["H0"], ["HF"])
-        cp(Cwin.indirect(T.IX2[:, 8:16]), T.HF[:], 128, ["IXd", "HF"], CK, SCA)
-        tt(Cwin.indirect(T.IX2[:, 0:8]), T.GT[:], T.HF[:], ALU.subtract, 128, ["IXu", "GT", "HF"], CK, SCA)
+        cp(Cwin.indirect(T.IX2[:, 0:8]), T.HF[:], 128, ["IXd", "HF"], CK, SCA)
+        tt(Cwin.indirect(T.IX2[:, 16:24]), T.GT[:], T.HF[:], ALU.subtract, 128, ["IXu", "GT", "HF"], CK, SCA)
 
     for v in range(NV):
-        for c in (v % 2, 1 - v % 2):
+        for ch in chunks(v):
             for step in range(3):
-                walk(v, c, step)
-            if c != v % 2:
-                send_list(v, c)
+                tag[0] = ch[0] + str(v)
+                if ch[0] == "T" and step == 2:
+                    stage1(v)
+                walk(v, ch, step)
+        tag[0] = "t" + str(v)
         train(v)
-        if v == 0:
-            ts(C(FW), C(ODD), 64.0, 4.0, ALU.mult, ALU.add, 1, k_(ODD), k_(FW))
-            ts(C(FW2), C(G_), 5.0, C(FW), ALU.mult, ALU.add, 1, k_(G_, FW), k_(FW2))
-            ts(T.MW[:], T.IO[:, 0:132], C(FW2), C(GE12), ALU.is_equal, ALU.mult, 132, ["IO"] + k_(FW2, GE12), ["MW"])
-            ts(C(PM2), C(P_), -2.0, None, ALU.add, None, 1, k_(P_), k_(PM2))
-            ts(C(PO13), C(M1213), OFF, None, ALU.mult, None, 1, k_(M1213), k_(PO13))
-            ts(MT(0), IO, C(PM2), C(GE14), ALU.is_equal, ALU.mult, 128, ["IO"] + k_(PM2, GE14), ["MT0"])
-            tt(T.M3[:], MT(0), T.M1[:], ALU.add, 128, ["MT0", "M1"], ["M3"])
-            ts(T.M4[:], IO, C(P_), C(GE14), ALU.is_equal, ALU.mult, 128, ["IO"] + k_(P_, GE14), ["M4"])
-    mm([(T.PD0[:], T.MW[:, 4 - c:132 - c], T.W[:, 512 * c:512 * c + 512], c == 0, c == 4) for c in range(5)], 2560, ["MW"] + WK, ["PD0"])
-    ac(T.OT[:], T.PD0[:], ACT.Identity, OFF, 1.0, 512, [], ["PD0", "OT"])
-    dma("S", [(T.yp[12:128:16, 0:V0], T.OT[0:40, :]), (T.yp[13:128:16, 0:V0], T.OT[64:104, :])], "outs", ["OT"], ["ypb"], 2.5)
-    dma("S", [(T.yp[14:128:16, 0:V0], T.CN[14:128:16, 0:V0]), (T.yp[15:128:16, 0:V0], T.CN[15:128:16, 0:V0])], "outs", CK, ["ypc"], 2.5)
-    mm([(T.PD1[:], T.M3[:], T.W[:, V0:V0 + 512], True, False), (T.PD1[:], T.M4[:], T.CN[:, V0:V0 + 512], False, True)], 2560,
-       ["M3", "M4"] + WK + CK, ["PD1"])
-    ts(T.ON[:], T.PD1[:], C(PO13), None, ALU.add, None, 512, k_(PO13), ["PD1", "ON"])
-    dma("S", [(T.yp[:, V0:V0 + 512], T.ON[:])], "outs", ["ON"], ["ypd"], 3.0)
-    for p in range(4):
-        dma("S", [(T.yx[:, 128 * b:128 * (b + k)], T["X%d" % NV][:, 128 * a:128 * (a + k)]) for (a, b, k) in RUNS[p]], "outs",
-            [xk(NV, p)], ["yx%d" % p], 3.0)
-        for (a, b, k) in RUNS[p]:
-            cp(T.YS[:, 8 * b:8 * (b + k)], SL(NV)[:, 8 * a:8 * (a + k)], 8 * k, ["S%d_%d" % (NV, p // 2)], ["YS%d" % b])
-    dma("A", [(T.ys[:], T.YS[:])], "outs", ["YS%d" % b for r in RUNS for (a, b, k) in r], ["ys"], 2.5)
+    tag[0] = "o"
+    dma("S", [(T.yp[r:128:16, 0:V0], T.F[r:128:16, 0:V0]) for r in (12, 13)] +
+        [(T.yp[16 * g:16 * g + 14, V0:DUMMY], T.F[16 * g:16 * g + 14, V0:DUMMY]) for g in range(4)], "outs", FK, ["ypb"], 2.5)
+    dma("A", [(T.yp[16 * g:16 * g + 14, V0:DUMMY], T.F[16 * g:16 * g + 14, V0:DUMMY]) for g in range(4, 8)], "outs", FK, ["ypd"], 2.5)
+    dma("S", [(T.yp[r:128:16, 0:DUMMY], T.CN[r:128:16, 0:DUMMY]) for r in (14, 15)], "outs", CK, ["ypc"], 2.5)
+    bl = blocks(NV - 1)
+    for (pos, n) in [q for ch in chunks(NV - 1) for p in ch[4] for q in halves(p[0], p[1])]:
+        lin(T.XS[:, cs(pos, n)], T["X%d" % NV][:, cs(pos, n)], 1.0, C(XM), 128 * n, bk("X%d" % NV, pos, n) + k_(XM), bk("XF", pos, n), 1.0, 0.5)
+        dma("S", [(T.yx[:, cs(b, k)], T.XS[:, cs(a, k)]) for (a, b, k) in runs(pos, n, bl)], "outs", bk("XF", pos, n), ["yx%d" % pos], 2.3 + 0.125 * n)
+    dma("A", [(T.ys[:], T.YS[:])], "outs", bk("YS", 0, 16), ["ys"], 2.5)
     return ops, neng
 
 
@@ -419,35 +520,154 @@ def depend(ops):
     return deps
 
 
-def place(ops, before, seq, back):
-    HOP = PAR["hop"]
-    busy, at, fin = {}, {}, {}
-    for i in seq:
+def first_order(ops, deps, succ, rng):
+    HOP, n, u = PAR["hop"], len(ops), rng.random(5).tolist()
+    al, w = 0.005 + 0.015 * u[0], np.exp(0.4 * u[1] * rng.normal(size=len(ops))).tolist()
+    prio = [0.0] * n
+    for i in range(n - 1, -1, -1):
+        prio[i] = w[i] * (1.3 * ops[i]["opts"][0][1] + ops[i]["lat"] + HOP) + max([prio[j] for j in succ[i]] + [0.0])
+    off = {"A": 6 * u[2], "T": 10 * u[3], "t": 10 * u[3]}
+    prio = [prio[i] + off.get(ops[i]["tag"][0], 0.0) for i in range(n)]
+    pen = [(0.4 + u[4]) * o["opts"][-1][1] if len(o["opts"]) > 1 else 0.0 for o in ops]
+    left = [len(d) for d in deps]
+    ready = [0.0] * n
+    free = {r: 0.0 for r in ("V", "A", "P", "G", "S", "pv", "pt", "ps", "link")}
+    pool = {q: [] for q in "VAPGS"}
+    at, asg = [0.0] * n, [0] * n
+    for i in range(n):
+        if not left[i]:
+            for o in ops[i]["opts"]:
+                pool[o[0]].append(i)
+    for cnt in range(n):
+        best = None
+        for q in "VAPGS":
+            smin, cand = 1e9, None
+            for i in pool[q]:
+                o = ops[i]
+                t = max(ready[i], free[q], free[o["bank"]] + HOP if o["bank"] else 0.0, free["link"] if o["link"] else 0.0)
+                t2 = t + pen[i] if q == "V" else t
+                if t2 - al * prio[i] < smin:
+                    smin, cand = t2 - al * prio[i], (i, t, t2, q)
+            if cand and (best is None or cand[2] < best[2]):
+                best = cand
+        i, t, q = best[0], best[1], best[3]
         o = ops[i]
-        t = max([fin[j] + HOP for j in before[i]] + [0.0]) + (o["lat"] if back else 0.0)
-        res = [(o["q"], o["cost"])] + ([(o["bank"], o["cost"] + HOP)] if o["bank"] else []) + ([("link", o["link"])] if o["link"] else [])
-        moved = True
-        while moved:
-            moved = False
-            for (r, d) in res:
-                l = busy.setdefault(r, [])
-                k = len(l)
-                while k > 0 and l[k - 1][1] > t + 1e-9:
-                    k -= 1
-                while k < len(l) and l[k][0] < t + d - 1e-9:
-                    if l[k][1] > t + 1e-9:
-                        t = l[k][1]
-                        moved = True
-                    k += 1
-        for (r, d) in res:
-            l = busy[r]
-            k = len(l)
-            while k > 0 and l[k - 1][0] > t:
-                k -= 1
-            l.insert(k, (t, t + d))
-        at[i] = t
-        fin[i] = t + o["cost"] + (0.0 if back else o["lat"])
-    return at, fin
+        a = 0 if o["opts"][0][0] == q else 1
+        for x in o["opts"]:
+            pool[x[0]].remove(i)
+        c = o["opts"][a][1]
+        at[i], asg[i], free[q] = t, a, t + c
+        if o["bank"]:
+            free[o["bank"]] = t + c
+        if o["link"]:
+            free["link"] = t + o["link"]
+        for j in succ[i]:
+            ready[j] = max(ready[j], t + c + o["lat"] + (0.0 if ops[j]["cont"] == i else HOP))
+            left[j] -= 1
+            if not left[j]:
+                for x in ops[j]["opts"]:
+                    pool[x[0]].append(j)
+    return sorted(range(n), key=lambda i: (-1.0 if ops[i]["first"] else at[i], i)), asg
+
+
+def refine(ops, deps, succ, order, asg, tries, temp, rng):
+    HOP, LAM = PAR["hop"], PAR["lam"]
+    n = len(ops)
+    Q = {"V": 0, "A": 1, "P": 2, "G": 3, "S": 4, "pv": 5, "pt": 6, "ps": 7, None: -1}
+    qs = [[Q[x[0]] for x in o["opts"]] for o in ops]
+    cs = [[x[1] for x in o["opts"]] for o in ops]
+    bank = [Q[o["bank"]] for o in ops]
+    link, lat = [o["link"] for o in ops], [o["lat"] for o in ops]
+    hard = [[j for j in deps[i] if j != ops[i]["cont"]] for i in range(n)]
+    fixed = sum(1 for o in ops if o["first"])
+
+    def run(order, asg):
+        free, user, bq = [0.0] * 9, [-1] * 9, [-1] * 9
+        fin, why = [0.0] * n, [-1] * n
+        end, last, vb = 0.0, -1, 0.0
+        for i in order:
+            a = asg[i]
+            q = qs[i][a]
+            t, w = free[q], user[q]
+            for j in hard[i]:
+                if fin[j] > t:
+                    t, w = fin[j], j
+            b = bank[i]
+            c = cs[i][a]
+            if b >= 0:
+                if bq[b] != q and free[b] > t:
+                    t, w = free[b], user[b]
+                free[b], user[b], bq[b] = t + c + HOP, i, q
+            f = t + c
+            free[q], user[q] = f, i
+            if q == 0:
+                vb += c
+            if link[i]:
+                if free[8] > f:
+                    f, w = free[8], user[8]
+                free[8], user[8] = f + link[i], i
+            f += lat[i]
+            fin[i], why[i] = f + HOP, w
+            if f > end:
+                end, last = f, i
+        edges = []
+        while why[last] >= 0:
+            if why[last] not in deps[last]:
+                edges.append((why[last], last))
+            last = why[last]
+        return end + LAM * vb, edges, end
+    flex = [i for i in range(n) if len(qs[i]) > 1]
+    cur = run(order, asg)
+    best = (cur[0], order, asg, cur[2])
+    pos = [0] * n
+    for k, i in enumerate(order):
+        pos[i] = k
+    rnd = rng.random((tries, 4)).tolist()
+    for it in range(tries):
+        u = rnd[it]
+        p, i = cur[1][int(u[0] * len(cur[1]))]
+        a2, o2 = asg, order
+        a, b = pos[p], pos[i]
+        if u[1] < 0.08 or (0.14 <= u[1] < 0.3 and (len(qs[p]) > 1 or len(qs[i]) > 1)):
+            j = flex[int(u[2] * len(flex))] if u[1] < 0.08 else (p if len(qs[p]) > 1 and (u[2] < 0.5 or len(qs[i]) == 1) else i)
+            a2 = list(asg)
+            a2[j] = 1 - a2[j]
+        else:
+            if u[1] < 0.14:
+                a = fixed + int(u[2] * (n - fixed - 1))
+                b = a + 1
+                while b < n - 1 and qs[order[b]][asg[order[b]]] != qs[order[a]][asg[order[a]]]:
+                    b += 1
+                p, i = order[a], order[b]
+            if a < fixed:
+                continue
+            seg = order[a:b + 1]
+            if u[1] < 0.65:
+                s = {i}
+                for x in reversed(seg):
+                    if x in s:
+                        s.update(deps[x])
+                if p in s:
+                    continue
+                o2 = order[:a] + [x for x in seg if x in s] + [x for x in seg if x not in s] + order[b + 1:]
+            else:
+                s = {p}
+                for x in seg:
+                    if x in s:
+                        s.update(succ[x])
+                if i in s:
+                    continue
+                o2 = order[:a] + [x for x in seg if x not in s] + [x for x in seg if x in s] + order[b + 1:]
+        r = run(o2, a2)
+        if r[0] < cur[0] - temp * (1 - it / tries) * math.log(u[3] + 1e-12) and r[1]:
+            cur, asg = r, a2
+            if o2 is not order:
+                order = o2
+                for k in range(a, b + 1):
+                    pos[order[k]] = k
+            if r[0] < best[0]:
+                best = (r[0], order, asg, r[2])
+    return best[1:]
 
 
 PLANS = {}
@@ -455,46 +675,24 @@ PLANS = {}
 
 def plan(ops):
     if "best" not in PLANS:
-        n = len(ops)
         deps = depend(ops)
-        succ = [[] for _ in range(n)]
-        for i in range(n):
+        succ = [[] for _ in ops]
+        for i in range(len(ops)):
             for j in deps[i]:
                 succ[j].append(i)
-        rng = np.random.default_rng(7)
-        prio = [0.0] * n
-        for i in range(n - 1, -1, -1):
-            prio[i] = ops[i]["cost"] + ops[i]["lat"] + PAR["hop"] + max([prio[j] for j in succ[i]] + [0.0])
-        seq = sorted(range(n), key=lambda i: (-prio[i], i))
-        best = cur = None
-        for k in range(PAR["tries"]):
-            at, fin = place(ops, deps, seq, False)
-            end = max(fin.values())
-            if best is None or end < best[0]:
-                best = (end, at, fin)
-            if cur is None or end < cur[0] + PAR["tol"] * (1 - k / PAR["tries"]):
-                cur = (end, at, fin)
-            at, fin = cur[1], cur[2]
-            jit = PAR["jit"] * (0.15 + float(rng.random()))
-            noise = (jit * rng.random(2 * n)).tolist()
-            key = {}
-            for i in range(n):
-                key[i] = max([fin[i] + noise[i]] + [key[j] + 1e-6 for j in deps[i]])
-            atb, finb = place(ops, succ, sorted(range(n), key=lambda i: -key[i]), True)
-            key = {}
-            for i in range(n - 1, -1, -1):
-                key[i] = max([finb[i] + noise[n + i]] + [key[j] + 1e-6 for j in succ[i]])
-            seq = sorted(range(n), key=lambda i: -key[i])
-        at = best[1]
-        order = sorted(range(n), key=lambda i: (at[i], i))
+        rng = np.random.default_rng(PAR["seed"])
+        pool = [first_order(ops, deps, succ, rng) for k in range(PAR["starts"])]
+        for keep, tries in PAR["rounds"]:
+            pool = sorted([refine(ops, deps, succ, p[0], p[1], tries, PAR["temp"], rng) for p in pool], key=lambda p: p[2])[:keep]
+        order, asg, end = pool[0]
         last = {}
         for i in order:
             b = ops[i]["bank"]
             if b:
-                if b in last and ops[last[b]]["q"] != ops[i]["q"]:
+                if b in last and ops[last[b]]["opts"][asg[last[b]]][0] != ops[i]["opts"][asg[i]][0]:
                     deps[i] = sorted(set(deps[i] + [last[b]]))
                 last[b] = i
-        PLANS["best"] = (order, deps, best[0], at)
+        PLANS["best"] = (order, deps, asg, end)
     return PLANS["best"]
 
 
@@ -505,7 +703,7 @@ def rank_program(g, core, T, topo):
     nxt = T.cores[(rank + 1) % len(T.cores)]
     assert topo.may_write(core, nxt)
     ops, neng = build(T, topo, core, nxt)
-    order, deps = plan(ops)[:2]
+    order, deps, asg = plan(ops)[:3]
     spot = {i: k for k, i in enumerate(order)}
     eng = {"V": g.vector, "A": g.scalar, "P": g.tensor, "G": g, "S": g.sync}
     count, token, clock = {}, {}, {}
@@ -513,12 +711,12 @@ def rank_program(g, core, T, topo):
     nsent = 0
     for i in order:
         o = ops[i]
-        q = o["q"]
+        q, fn = o["opts"][asg[i]][0], o["opts"][asg[i]][2]
         kn = known[q]
         need = {}
         for j in deps[i]:
             s, val = token[j]
-            if kn.get(s, 0) < val and need.get(s, (0, 0))[0] < val:
+            if j != o["cont"] and kn.get(s, 0) < val and need.get(s, (0, 0))[0] < val:
                 need[s] = (val, j)
         for s, (val, j) in sorted(need.items(), key=lambda e: -spot[e[1][1]]):
             if kn.get(s, 0) < val:
@@ -527,7 +725,7 @@ def rank_program(g, core, T, topo):
                 for s2, v2 in clock[j].items():
                     if kn.get(s2, 0) < v2:
                         kn[s2] = v2
-        r = o["fn"](g)
+        r = fn(g)
         s = o["sem"] or "q" + q
         count[s] = count.get(s, 0) + o["n"]
         if o["sem"] is None:

@@ -1,5 +1,3 @@
-import math
-import numpy as np
 from concourse.mybir import AluOpType as ALU, ActivationFunctionType as ACT, AxisListType as AX
 
 V0, NS, NV, WD_ = 2560, 2048, 4, 3200
@@ -10,16 +8,20 @@ BIG = 4096.0
 OFF = 1536.0
 
 
+def tpos(v):
+    return 8 - v if v else 18
+
+
 def blocks(v):
     d = dict(zip(range(8 - v), [4, 5, 6, 7, 8, 3, 2, 1]))
     d.update(zip(range(8, 15), range(9, 16)))
     d.update(zip(range(15, 15 + v), range(3)))
-    d[18] = v
+    d[tpos(v)] = v
     return d
 
 
 def chunks(v):
-    l = [("T", 4, 18, 1, [(18, 1, "PT", 0, "ptX")], ("PT", 128, "ptV")),
+    l = [("T", 4, tpos(v), 1, [(tpos(v), 1, "PT", 0, "ptX")], ("PT", 128, "ptV")),
          ("A", 8, 0, 8 - v, [(0, 4, "PS0", 0, "PS0"), (4, 4 - v, "PS1", 0, "ps1a" if v >= 2 else "PS1")], ("PV", 0, "pvA")),
          ("B", 8, 8, 8 if v else 7, [(8, 4, "PS2", 0, "PS2"), (12, 4 if v else 3, "PS3", 0, "PS3")], ("PV", 256, "pvB"))]
     if v >= 2:
@@ -38,7 +40,7 @@ def runs(pos, n, to):
 
 
 def halves(pos, n):
-    return [(pos, 2), (pos + 2, 2)] if n == 4 else [(pos, n)]
+    return [(pos, 2), (pos + 2, 2)] if n == 4 and pos in PAR["half"] else [(pos, n)]
 
 
 def _sb(cols, dtype):
@@ -50,12 +52,12 @@ NX, NL = 128 * NP_, 8 * NP_
 for _d, _l in (("int32", dict(R=V0, STI=128, SGI=4, PC=16)),
                ("uint16", dict(L1=NL, L2=NL, TL=8, IX1=16, IX2=24)),
                ("float16", dict(ZA=[34, 8], ZB=[34, 8], ZT=[68, 4], ZL=[68, 4], EYH=128, C0=NX, C1=NX, C2=NX, PR=NX, SL=128, H2=128, Q4=128,
-                                E8=128, SC=128, SM=128, SW=128, WV=32, WB=128, FT=128, MT=512)),
-               ("bfloat16", dict(XS=NX, SN=384, ZZ=1024, TRI=1024, BE=256, G8=8, OB=128, TB=128, ONE=40, CP=16, CX=64, GA=256, GB=256,
+                                SC=128, SM=128, SW=128, WV=32, WB=128, FT=128, MT=512)),
+               ("bfloat16", dict(XS=NX, SN=384, ZZ=1024, TRI=512, BE=256, G8=8, OB=128, TB=128, ONE=40, CP=16, CX=64, GA=256, GB=256,
                                  B0=128, BT=WD_, BB=256, ZF=[68, 4], EYK=32, EYB=128, E1=[8, 128], E2=[8, 128])),
                ("float32", dict(F=WD_, CN=WD_, IDT=WD_, THC=128, IO=256, COL=48, R16=16, HM=16, IG=128, IR=128, WN=64, THR=64, I4=160,
                                 DUM=16, MD=8, A2=16, NE=8, OO=32, GS=128, FS=128, GT=128, GM=128, MB=128, YY=128, WDN=128, PW=32,
-                                H0=128, HF=128, YS=128, UF=NL, BU=256, BR=256))):
+                                H0=128, HF=128, YS=NL, UF=NL, BU=256, BR=256))):
     for _n, _c in _l.items():
         SCRATCH[_n] = _sb(_c, _d)
 for _v in range(NV + 1):
@@ -72,9 +74,38 @@ SEMAPHORES = (["qV", "qA", "qP", "qG", "sent", "outs", "stat", "lsg", "lst", "lc
               + ["r%d" % i for i in range(60)])
 
 PAR = {"cyc": 0.00085, "pec": 0.000425, "gat": 1.56, "sca": 3.8, "hop": 0.14, "ov": 0.008, "lx": 0.35, "ls": 0.3, "lat": 1.9,
-       "mmo": 0.005, "starts": 100, "rounds": ((12, 50), (4, 1500), (1, 7000), (1, 100000)), "temp": 0.06, "lam": 0.1, "seed": 1,
-       "rp": [640, 640, 512, 512, 256], "ea": (),
-       "mode": {"T18": "xn", "L16": "xn", "A0": "xn", "A4": "xn", "B8": "xn", "B12": "xn"}}
+       "mmo": 0.005, "rp": [640, 640, 512, 512, 256], "first": 3.0, "half": (8, 12), "mode": "xnr"}
+
+ORDER = """
+0 1 2 3 4 5 6 7 8 9 10 11 12 13 15 101 20 42 41 43 40 44 21 47 39 102 14 31 17 19 35 28 16 25 18 22 30 103 50 45 54 104 51 91 106 81 53 105
+46 -94 77 76 75 55 52 66 71 107 56 59 110 70 57 95 73 67 109 38 108 48 78 -79 130 82 49 80 37 165 -60 111 133 113 -132 114 -89 83 69 162 98
+92 74 68 148 93 62 72 63 84 149 115 112 140 -87 135 164 160 150 64 61 151 116 163 90 88 96 161 -144 32 23 100 24 26 27 33 34 29 36 152 124
+-131 -86 -121 -123 134 -155 97 137 206 -85 -156 -138 -167 209 166 205 260 143 263 -157 168 169 207 170 -158 -159 171 208 153 216 217 259 172
+174 173 136 175 126 210 -145 261 262 211 270 220 221 -118 -117 -176 212 177 213 178 214 264 179 -215 -127 218 274 -125 180 -219 265 181 275
+271 222 276 65 120 122 128 226 224 266 -182 -119 267 -129 146 -185 -184 147 183 268 272 194 58 223 186 195 -269 225 154 196 201 187 227 -139
+197 189 233 234 228 229 -190 230 198 -202 273 280 278 277 279 236 235 237 231 238 316 199 287 281 232 141 142 239 288 282 188 200 317 240
+191 192 283 203 241 313 193 284 320 321 315 327 242 314 318 319 289 290 249 250 251 285 322 243 252 326 244 -286 245 323 254 255 246 328 330
+291 256 325 -247 324 329 204 253 292 248 293 295 332 294 296 303 297 257 344 333 331 334 258 335 304 345 298 336 299 338 305 300 308 340 301
+306 309 310 386 339 341 337 342 346 343 311 387 349 390 302 307 348 389 347 388 350 391 312 351 356 397 392 401 398 352 353 99 393 394 444
+357 441 354 399 395 440 402 403 -355 -358 -396 400 405 359 360 365 442 361 362 443 445 406 451 452 363 446 -364 447 407 404 448 455 456 457
+453 449 366 372 408 376 -367 409 368 458 -496 454 377 378 410 411 379 369 412 380 371 370 414 415 383 417 416 381 373 418 413 -450 420 421
+419 430 497 431 432 459 374 -382 460 375 494 498 461 495 462 468 502 501 500 499 469 470 463 503 471 472 504 464 -507 465 433 384 422 508
+466 423 509 435 436 437 473 525 505 510 511 506 467 385 434 424 474 513 475 425 484 438 426 526 514 427 485 515 439 476 486 516 477 428 517
+512 478 519 479 487 489 490 669 521 491 520 480 481 522 529 567 429 570 488 523 524 527 482 492 530 531 528 537 532 483 493 568 538 571 569
+533 518 534 572 578 616 535 573 579 615 580 582 -536 574 575 -539 540 576 546 541 618 619 581 617 -577 542 543 626 627 544 620 628 621 630
+631 632 -586 -545 584 583 670 547 548 629 553 633 585 622 623 587 -557 549 671 558 624 588 550 596 677 564 593 559 -625 589 552 590 551 560
+636 637 594 701 591 -592 672 554 595 646 561 634 635 702 562 647 643 638 644 597 555 673 563 700 598 565 712 698 -678 639 674 556 640 703
+699 705 706 607 608 599 711 600 609 707 641 715 -642 704 610 729 708 645 675 713 648 612 601 651 710 709 714 -676 679 613 716 649 652 602
+717 664 603 680 718 719 604 665 605 666 730 650 720 725 681 566 611 614 606 667 668 653 659 682 721 726 683 654 723 655 731 728 684 685 687
+724 656 660 661 686 688 695 771 774 727 657 662 658 663 733 689 732 -775 734 690 776 735 691 722 786 692 736 772 773 822 777 -787 823 -693
+737 -696 778 694 697 820 741 782 738 779 783 739 780 784 824 834 819 835 781 -740 743 -742 -790 744 821 791 745 836 750 825 746 747 830 800
+748 875 831 832 785 788 826 789 -749 827 828 792 -757 837 876 877 -761 752 751 753 -829 793 833 838 878 794 762 754 797 795 883 768 798 799
+756 755 758 763 839 847 796 840 841 801 884 803 764 759 765 906 907 848 842 766 850 760 802 843 804 767 844 904 879 908 912 911 769 -918 909
+880 -917 770 851 811 852 845 849 812 846 805 910 806 855 807 856 813 913 814 881 914 919 869 808 916 -882 920 915 870 853 936 809 885 854
+871 921 816 923 886 -817 937 -943 905 872 815 887 863 888 924 889 922 864 925 944 865 810 874 873 818 866 890 857 -891 926 858 927 893 859
+928 892 867 868 929 932 894 860 901 902 861 955 953 947 959 960 903 862 933 930 895 938 896 897 898 935 -899 931 934 945 -949 941 961 -951
+939 900 962 940 954 956 946 950 948 942 -957 952 958
+"""
 
 
 def build(T, topo, core, nxt):
@@ -141,6 +172,9 @@ def build(T, topo, core, nxt):
 
     def send(dst, src, rd, wr, link):
         sem = "r%d" % nsend[0]
+        if not nsend[0]:
+            op([("G", PAR["first"], None)], rd, ["G1"])
+        rd = rd + ["G1"]
         nsend[0] += 1
         op([("G", 0.5, lambda g: g.remote_dma(dst, src, T.sem[sem], T.sem.sent, pid, rid, mask))], rd, wr, sem=sem, n=neng,
            lat=PAR["lat"] + link, link=link)
@@ -183,8 +217,6 @@ def build(T, topo, core, nxt):
     mset(T.ZZ[:, 0:512], 11.0, 512, ["ZZ"], 0.5)
     mset(T.ZZ[:, 512:1024], 0.0, 512, ["ZZ"], 0.5)
     sel(T.TRI[:, 0:512], [[16, 8], [0, 4], [1, 16]], ALU.is_gt, 99.0, 0, -1, 512, "TRI0", T.ZZ[:, 0:512])
-    if PAR["ea"]:
-        sel(T.TRI[:, 512:1024], [[16, 8], [0, 4], [1, 16]], ALU.is_gt, -64.0, 0, -1, 512, "TRI1", T.ZZ[:, 512:1024])
     for h, f in ((0, BIG), (1, -BIG)):
         sel(T.BE[:, 128 * h:128 * h + 128], [[-1, 128]], ALU.not_equal, f, 0, 1, 128, "BE%d" % h, T.ZZ[:, 512:640])
     ms(T.F[:, V0:WD_], 0, 640, ["F%d" % NR])
@@ -205,8 +237,8 @@ def build(T, topo, core, nxt):
     ts(T.PC[:, 10:11], T.PC[:, 0:1], 3, None, ALU.bitwise_and, None, 1, ["PC0"], ["PC10"])
     ts(T.PC[:, 11:12], T.PC[:, 0:1], 16, None, ALU.bitwise_and, None, 1, ["PC0"], ["PC11"])
     ts(T.PC[:, 12:13], T.PC[:, 0:1], 2, None, ALU.arith_shift_right, None, 1, ["PC0"], ["PC12"])
-    (G_, P_, R_, R8, R4, P16, P4, LT12, LT14, GE14, CH_, CR, E_, M1213, M1214, SIG, TAU, ODD, BI, BI0, CSL, CH2, CQ4, CE8, CSC, CSM, CSW,
-     CQ, CE, C14, PWC, PWL, PWH, LT8, CSI, ME, MO, K15, PO, M256, XP, XM) = range(42)
+    (G_, P_, R_, R8, R4, P16, P4, LT12, LT14, GE14, CH_, CR, E_, M1213, M1214, SIG, TAU, ODD, BI, BI0, CSL, CH2, CQ4, CSC, CSM, CSW,
+     CQ, C14, PWC, PWL, PWH, LT8, CSI, ME, MO, K15, PO, M256, XP, XM) = range(40)
     k_ = lambda *a: ["c%d" % i for i in a]
     r16 = lambda i: T.R16[:, i:i + 1]
     IO = T.IO[:, 0:128]
@@ -250,12 +282,7 @@ def build(T, topo, core, nxt):
     ac(T.EYB[:], T.IR[:], ACT.Abs, -12.5, 1.0, 128, ["IR"], ["EYB"])
     ts(T.GB[:, 128:256], T.EYB[:], 1.0, C(K15), ALU.is_lt, ALU.mult, 128, ["EYB"] + k_(K15), ["GB1"], 0.5)
     tt(MT(0), T.GB[:, 128:256], T.OB[:], ALU.mult, 128, ["GB1", "OB"], ["MT0"], 2.0)
-    mats = [("H2", CH2), ("Q4", CQ4), ("SC", CSC)]
-    if "nn" in PAR["mode"].values():
-        lin(C(CE), C(LT12), 0.125, 0.0, 1, k_(LT12), k_(CE))
-        lin(C(CE8), r16(15), 17.0 / 1024, C(CE), 1, ["R16"] + k_(CE), k_(CE8))
-        mats.append(("E8", CE8))
-    for (M, col) in mats:
+    for (M, col) in (("H2", CH2), ("Q4", CQ4), ("SC", CSC)):
         lin(T[M][:], T.B0[:], C(col), 0.0, 128, ["B0"] + k_(col), [M], 1.0, 0.5)
     for (M, col, i) in (("SL", CSL, 1), ("SM", CSM, 2)):
         lin(MT(i), T.B0[:], C(col), 0.0, 128, ["B0"] + k_(col), ["MT%d" % i], 1.0, 0.5)
@@ -300,8 +327,6 @@ def build(T, topo, core, nxt):
     lin(T.THR[:, 0:32], T.GS[:, 0:32], 1.0, 5.0, 32, ["GS"], ["THRa"])
     lin(T.THR[:, 32:64], T.GS[:, 32:64], 1.0, 21.0, 32, ["GS"], ["THRb"])
     ts(T.EYK[:], T.I4[:, 0:32], C(P4), None, ALU.is_equal, None, 32, ["I4a"] + k_(P4), ["EYK"])
-    if PAR["ea"]:
-        lin(T.EYB[:], T.EYH[:], 1.0, 0.0, 128, ["EYH"], ["EYB"], 1.0, 0.5)
     lin(T.DUM[:, 0:8], T.MD[:], 1.0, C(R_), 8, ["MD"] + k_(R_), ["DUM"])
     lin(T.DUM[:, 8:16], T.MD[:], 1.0, C(R_), 8, ["MD"] + k_(R_), ["DUMb"])
     lin(MT(1), T.B0[:], C(CSW), 0.0, 128, ["B0"] + k_(CSW), ["MT1"], 1.0, 0.5)
@@ -335,10 +360,7 @@ def build(T, topo, core, nxt):
             for (a, b, k) in runs(pos, n, where(v)):
                 send(SLs(v + 1)[:, ls(b, k)], T["U%d" % v][:, ls(a, k)], bk("U%d" % v, a, k), bk("S%d" % (v + 1), b, k), PAR["ls"])
         else:
-            for (a, b, k) in runs(pos, n, blocks(v)):
-                send(T.YS[:, ls(b, k)], T.UF[:, ls(a, k)], bk("UF", a, k), bk("YS", b, k), PAR["ls"])
-
-    pend, held = {}, {}
+            send(T.YS[:, ls(pos, n)], T.UF[:, ls(pos, n)], bk("UF", pos, n), bk("YS", pos, n), PAR["ls"])
 
     def walk(v, ch, step):
         name, nb, pos0, nblk, pieces, (pvb, c0, pv) = ch
@@ -352,8 +374,6 @@ def build(T, topo, core, nxt):
         for (pos, k, psb, pc, ps) in pieces:
             sl, PS, w = cs(pos, k), T[psb][:, pc:pc + 128 * k], 128 * k
             if step == 0:
-                pend[pos], held[pos] = [], False
-            if not held[pos]:
                 mm([(PS, T.SL[:], X[:, sl], True, True)], w, ["SL"] + bk(xn, pos, k) + (["PS1"] if ps[:2] == "ps" else []), [ps])
             lin(CB[:, sl], Fwin.indirect(src[:, ls(pos, k)]), C(LT14), C(BI), w, GK + bk(sk, pos, k), bk(cn, pos, k), GAT)
             tt(T.PR[:, sl], CB[:, sl], PS, ALU.mult, w, bk(cn, pos, k), [ps] + bk("PR", pos, k))
@@ -377,10 +397,8 @@ def build(T, topo, core, nxt):
             send_list(v, pos0, nblk)
         for (pos, k, psb, pc, ps) in pieces:
             sl, PS, w = cs(pos, k), T[psb][:, pc:pc + 128 * k], 128 * k
-            pd = pend[pos]
-            md = PAR["mode"]["%s%d" % (name, pos)][step] if step < 2 else "r"
-            lst = list(zip([["H2"], ["Q4", "Q4"], ["E8", "E8", "Q4"]][len(pd)], [xn] + ["C%d" % s for s in pd]))
-            lst += [("H2", cn)] if md == "r" else [("SC", cn), ("SM", cn)]
+            md = PAR["mode"][step]
+            lst = [("Q4", xn), ("Q4", "C1"), ("H2", cn)] if md == "r" else [("H2", xn), ("SC", cn), ("SM", cn)]
             if ps[0] == "P":
                 for i, (m, q) in enumerate(lst):
                     mm([(PS, T[m][:], T[q][:, sl], i == 0, i == len(lst) - 1)], w, [m] + bk(q, pos, k), [ps])
@@ -388,16 +406,10 @@ def build(T, topo, core, nxt):
             else:
                 mm([(PS, T[m][:], T[q][:, sl], i == 0, i == len(lst) - 1) for i, (m, q) in enumerate(lst)], w * len(lst),
                    sorted(set(m for m, q in lst)) + [y for m, q in lst for y in bk(q, pos, k)], [ps])
-            held[pos] = md != "r"
-            if md == "n":
-                pd.append(step)
-                continue
-            pend[pos] = []
             if md == "x":
                 lin(X[:, sl], PS, C(LT12), C(XP), w, k_(LT12, XP), [ps] + bk(xn, pos, k))
-            else:
+            if md == "r":
                 lin(X[:, sl], PS, 1.0, C(CR), w, k_(CR), [ps] + bk(xn, pos, k))
-            if step == 2:
                 xo = "X%d" % (v + 1)
                 for (a, b, kk) in ([(a, a, b) for a, b in halves(pos, k)] if last else runs(pos, k, where(v))):
                     send(T[xo][:, cs(b, kk)], X[:, cs(a, kk)], bk(xn, a, kk), bk(xo, b, kk), PAR["lx"] * kk)
@@ -405,37 +417,32 @@ def build(T, topo, core, nxt):
     def equalities(lst, lk, G, gk, E, ek):
         for o, col in ((0, ME), (1, MO)):
             lin(G[:, 128 * o:128 * o + 128], T.BT[:, 0:WD_].indirect(lst), C(col), 0.0, 128, BK + lk + k_(col), [gk + str(o)], GAT)
-        sa = ek in PAR["ea"]
-        if sa:
-            mm([(T.PD1[:], T.EYB[:], T.TRI[:, 512:1024], True, False)], 512, ["EYB", "TRI1"], ["PD1"])
         for t in range(2):
             mm([(T["PD%d" % h][:, :, 32 * t + 16 * o:32 * t + 16 * o + 16], G[64 * h + 32 * t:64 * h + 32 * t + 32, 128 * o:128 * o + 128],
-                 G[64 * h + 32 * t:64 * h + 32 * t + 32, 128 * o:128 * o + 128], not (h and sa), not (h and sa) or (t, o) == (1, 1))
+                 G[64 * h + 32 * t:64 * h + 32 * t + 32, 128 * o:128 * o + 128], True, True)
                 for h in (1, 0) for o in (0, 1)], 512, [gk + "0", gk + "1"], ["PD0", "PD1"])
-        if sa:
-            ac(E[:, :, 64:128], T.PD1[:], ACT.Relu, -11.0, 1.0, 512, [], ["PD1", ek + "1"])
-        else:
-            tt(E[:, :, 64:128], T.PD1[:], T.TRI[:, 0:512], ALU.is_gt, 512, ["TRI0"], ["PD1", ek + "1"])
+        tt(E[:, :, 64:128], T.PD1[:], T.TRI[:, 0:512], ALU.is_gt, 512, ["TRI0"], ["PD1", ek + "1"])
         tt(E[:, :, 0:64], T.PD0[:], T.TRI[:, 0:512], ALU.is_gt, 512, ["TRI0"], ["PD0", ek + "0"])
 
     def earlier(o, E, w, st):
         return [(T.PT[:, o + k:o + 1 + k], E[:, k, :], T.ONE[:, w:w + 1], st, st or k == 7) for k in range(8)]
 
     def stage1(v):
-        sL = T.L2[:, ls(18, 1)]
-        equalities(sL, ["L2_18"], T.GA, "GA", T.E1, "E1")
-        lin(T.GS[:], Cwin.indirect(sL), 1.0, 0.0, 128, CK + ["L2_18"], ["GS"], GAT)
+        sL, lk = T.L2[:, ls(tpos(v), 1)], "L2_%d" % tpos(v)
+        equalities(sL, [lk], T.GA, "GA", T.E1, "E1")
+        lin(T.GS[:], Cwin.indirect(sL), 1.0, 0.0, 128, CK + [lk], ["GS"], GAT)
         mm(earlier(384, T.E1, 0, True), 512, ["E10", "E11", "ONEa"], ["pt1"])
         tt(T.MD[:], T.PT[:, 384:392], T.DUM[:, 0:8], ALU.min, 8, ["DUM"], ["pt1", "MD"])
-        tt(T.IX1[:, 0:8], T.MD[:], sL, ALU.max, 8, ["MD", "L2_18"], ["IXs"])
+        tt(T.IX1[:, 0:8], T.MD[:], sL, ALU.max, 8, ["MD", lk], ["IXs"])
 
     def train(v):
-        tc, lc = cs(18, 1), ls(18, 1)
+        tp = tpos(v)
+        tc, lc = cs(tp, 1), ls(tp, 1)
         PT = T.PT
         tt(T.IX1[:, 8:16], T.MD[:], T.TL[:], ALU.max, 8, ["MD", "TL"], ["IXt"])
         tt(T.NE[:], T.IX1[:, 0:8], T.IX1[:, 8:16], ALU.not_equal, 8, ["IXs", "IXt"], ["NE"])
-        lin(T.FS[:], T.C2[:, tc], 1.0, C(PO), 128, ["C2_18"] + k_(PO), ["FS"])
-        mm([(T.PD0[:, 0:2, :], T.WB[:], T.PR[:, tc], True, True)], 128, ["WB", "PR_18"], ["PD0"])
+        lin(T.FS[:], T.C2[:, tc], 1.0, C(PO), 128, ["C2_%d" % tp] + k_(PO), ["FS"])
+        mm([(T.PD0[:, 0:2, :], T.WB[:], T.PR[:, tc], True, True)], 128, ["WB", "PR_%d" % tp], ["PD0"])
         ts(T.MB[:], T.PD0[:, 0:2, :], C(SIG), C(TAU), ALU.mult, ALU.is_gt, 128, k_(SIG, TAU), ["PD0", "MB"])
         tt(Cwin.indirect(T.IX1[:, 0:8]), T.GS[:], T.MB[:], ALU.add, 128, ["IXs", "GS", "MB"], CK, SCA)
         tt(T.GM[:], T.GS[:], T.MB[:], ALU.mult, 128, ["GS", "MB"], ["GM"], 2.0)
@@ -446,7 +453,7 @@ def build(T, topo, core, nxt):
            ["GM", "GT", "WNa", "WNb"], ["ptB"])
         tt(T.ZF[:, 4:68:4, :], PT[:, 392:456], T.THR[:], ALU.is_lt, 64, ["THRa", "THRb"], ["ptB", "ZF"])
         mm([(PT[:, 0:128], T.SW[:], T.FT[:], True, False), (PT[:, 0:128], T.H2[:], T["X%d" % v][:, tc], False, True)], 256,
-           ["SW", "H2", "FT", "X%d_18" % v], ["ptX"])
+           ["SW", "H2", "FT", "X%d_%d" % (v, tp)], ["ptX"])
         ts(T.WDN[:], PT[:, 0:128], MAGIC, MAGIC, ALU.add, ALU.subtract, 128, [], ["ptX", "WDN"])
         mm([(PT[:, 456:464], T.ZF[:, 4 * (1 + 8 * hl) - h:4 * (9 + 8 * hl) - h, :], T.EYK[:, 8 * h:8 * h + 8], hl == 0 and h == 0, False)
             for hl in range(2) for h in range(4)] + earlier(456, T.E2, 2, False), 1024, ["ZF", "EYK", "E20", "E21", "ONEb"], ["ptW"])
@@ -460,11 +467,11 @@ def build(T, topo, core, nxt):
             return [(PT[:, o:o + 8], T.OB[:], T.ONE[:, w:w + 8], True, False), (PT[:, o:o + 8], T.TB[:], cpv, False, False),
                     (PT[:, o:o + 8], T.BE[:, 128 * h:128 * h + 128], cpv, False, False), (PT[:, o:o + 8], T.OB[:], cx[:, 0:8], False, True)]
         mm(ranks(464, 0, 16), 256, ["TB", "OB", "BE0", "CP", "CX", "ONEd"], ["ptA"])
-        uL, uk = T["U%d" % v][:, lc], "U%d_18" % v
+        uL, uk = T["U%d" % v][:, lc], "U%d_%d" % (v, tp)
         tt(uL, PT[:, 464:472], T.TL[:], ALU.max, 8, ["TL"], ["ptA", uk])
         if v == NV - 1:
-            lin(T.UF[:, lc], uL, 1.0, 0.0, 8, [uk], ["UF_18"])
-        send_list(v, 18, 1)
+            lin(T.UF[:, lc], uL, 1.0, 0.0, 8, [uk], ["UF_%d" % tp])
+        send_list(v, tp, 1)
         tt(T.YY[:], Iwin.indirect(uL), T.MB[:], ALU.mult, 128, IDK + [uk, "MB"], ["YY"], GAT)
         tt(Fwin.indirect(T.IX1[:, 0:8]), T.YY[:], T.FS[:], ALU.max, 128, ["IXs", "YY", "FS"], FK, SCA)
         mm(ranks(472, 1, 24) + [(PT[:, 480:488], T.OB[:], T.ONE[:, 32:40], True, False), (PT[:, 480:488], T.BE[:, 128:256], cpv, False, True)], 384,
@@ -495,7 +502,8 @@ def build(T, topo, core, nxt):
     for (pos, n) in [q for ch in chunks(NV - 1) for p in ch[4] for q in halves(p[0], p[1])]:
         lin(T.XS[:, cs(pos, n)], T["X%d" % NV][:, cs(pos, n)], 1.0, C(XM), 128 * n, bk("X%d" % NV, pos, n) + k_(XM), bk("XF", pos, n), 1.0, 0.5)
         dma("S", [(T.yx[:, cs(b, k)], T.XS[:, cs(a, k)]) for (a, b, k) in runs(pos, n, bl)], "outs", bk("XF", pos, n), ["yx%d" % pos], 2.3 + 0.125 * n)
-    dma("A", [(T.ys[:], T.YS[:])], "outs", bk("YS", 0, 16), ["ys"], 2.5)
+    for ch in chunks(NV - 1):
+        dma("A", [(T.ys[:, ls(b, k)], T.YS[:, ls(a, k)]) for (a, b, k) in runs(ch[2], ch[3], bl)], "outs", bk("YS", ch[2], ch[3]), ["ys" + ch[0]], 2.4)
     return ops, neng
 
 
@@ -520,180 +528,21 @@ def depend(ops):
     return deps
 
 
-def first_order(ops, deps, succ, rng):
-    HOP, n, u = PAR["hop"], len(ops), rng.random(5).tolist()
-    al, w = 0.005 + 0.015 * u[0], np.exp(0.4 * u[1] * rng.normal(size=len(ops))).tolist()
-    prio = [0.0] * n
-    for i in range(n - 1, -1, -1):
-        prio[i] = w[i] * (1.3 * ops[i]["opts"][0][1] + ops[i]["lat"] + HOP) + max([prio[j] for j in succ[i]] + [0.0])
-    off = {"A": 6 * u[2], "T": 10 * u[3], "t": 10 * u[3]}
-    prio = [prio[i] + off.get(ops[i]["tag"][0], 0.0) for i in range(n)]
-    pen = [(0.4 + u[4]) * o["opts"][-1][1] if len(o["opts"]) > 1 else 0.0 for o in ops]
-    left = [len(d) for d in deps]
-    ready = [0.0] * n
-    free = {r: 0.0 for r in ("V", "A", "P", "G", "S", "pv", "pt", "ps", "link")}
-    pool = {q: [] for q in "VAPGS"}
-    at, asg = [0.0] * n, [0] * n
-    for i in range(n):
-        if not left[i]:
-            for o in ops[i]["opts"]:
-                pool[o[0]].append(i)
-    for cnt in range(n):
-        best = None
-        for q in "VAPGS":
-            smin, cand = 1e9, None
-            for i in pool[q]:
-                o = ops[i]
-                t = max(ready[i], free[q], free[o["bank"]] + HOP if o["bank"] else 0.0, free["link"] if o["link"] else 0.0)
-                t2 = t + pen[i] if q == "V" else t
-                if t2 - al * prio[i] < smin:
-                    smin, cand = t2 - al * prio[i], (i, t, t2, q)
-            if cand and (best is None or cand[2] < best[2]):
-                best = cand
-        i, t, q = best[0], best[1], best[3]
-        o = ops[i]
-        a = 0 if o["opts"][0][0] == q else 1
-        for x in o["opts"]:
-            pool[x[0]].remove(i)
-        c = o["opts"][a][1]
-        at[i], asg[i], free[q] = t, a, t + c
-        if o["bank"]:
-            free[o["bank"]] = t + c
-        if o["link"]:
-            free["link"] = t + o["link"]
-        for j in succ[i]:
-            ready[j] = max(ready[j], t + c + o["lat"] + (0.0 if ops[j]["cont"] == i else HOP))
-            left[j] -= 1
-            if not left[j]:
-                for x in ops[j]["opts"]:
-                    pool[x[0]].append(j)
-    return sorted(range(n), key=lambda i: (-1.0 if ops[i]["first"] else at[i], i)), asg
-
-
-def refine(ops, deps, succ, order, asg, tries, temp, rng):
-    HOP, LAM = PAR["hop"], PAR["lam"]
-    n = len(ops)
-    Q = {"V": 0, "A": 1, "P": 2, "G": 3, "S": 4, "pv": 5, "pt": 6, "ps": 7, None: -1}
-    qs = [[Q[x[0]] for x in o["opts"]] for o in ops]
-    cs = [[x[1] for x in o["opts"]] for o in ops]
-    bank = [Q[o["bank"]] for o in ops]
-    link, lat = [o["link"] for o in ops], [o["lat"] for o in ops]
-    hard = [[j for j in deps[i] if j != ops[i]["cont"]] for i in range(n)]
-    fixed = sum(1 for o in ops if o["first"])
-
-    def run(order, asg):
-        free, user, bq = [0.0] * 9, [-1] * 9, [-1] * 9
-        fin, why = [0.0] * n, [-1] * n
-        end, last, vb = 0.0, -1, 0.0
-        for i in order:
-            a = asg[i]
-            q = qs[i][a]
-            t, w = free[q], user[q]
-            for j in hard[i]:
-                if fin[j] > t:
-                    t, w = fin[j], j
-            b = bank[i]
-            c = cs[i][a]
-            if b >= 0:
-                if bq[b] != q and free[b] > t:
-                    t, w = free[b], user[b]
-                free[b], user[b], bq[b] = t + c + HOP, i, q
-            f = t + c
-            free[q], user[q] = f, i
-            if q == 0:
-                vb += c
-            if link[i]:
-                if free[8] > f:
-                    f, w = free[8], user[8]
-                free[8], user[8] = f + link[i], i
-            f += lat[i]
-            fin[i], why[i] = f + HOP, w
-            if f > end:
-                end, last = f, i
-        edges = []
-        while why[last] >= 0:
-            if why[last] not in deps[last]:
-                edges.append((why[last], last))
-            last = why[last]
-        return end + LAM * vb, edges, end
-    flex = [i for i in range(n) if len(qs[i]) > 1]
-    cur = run(order, asg)
-    best = (cur[0], order, asg, cur[2])
-    pos = [0] * n
-    for k, i in enumerate(order):
-        pos[i] = k
-    rnd = rng.random((tries, 4)).tolist()
-    for it in range(tries):
-        u = rnd[it]
-        p, i = cur[1][int(u[0] * len(cur[1]))]
-        a2, o2 = asg, order
-        a, b = pos[p], pos[i]
-        if u[1] < 0.08 or (0.14 <= u[1] < 0.3 and (len(qs[p]) > 1 or len(qs[i]) > 1)):
-            j = flex[int(u[2] * len(flex))] if u[1] < 0.08 else (p if len(qs[p]) > 1 and (u[2] < 0.5 or len(qs[i]) == 1) else i)
-            a2 = list(asg)
-            a2[j] = 1 - a2[j]
-        else:
-            if u[1] < 0.14:
-                a = fixed + int(u[2] * (n - fixed - 1))
-                b = a + 1
-                while b < n - 1 and qs[order[b]][asg[order[b]]] != qs[order[a]][asg[order[a]]]:
-                    b += 1
-                p, i = order[a], order[b]
-            if a < fixed:
-                continue
-            seg = order[a:b + 1]
-            if u[1] < 0.65:
-                s = {i}
-                for x in reversed(seg):
-                    if x in s:
-                        s.update(deps[x])
-                if p in s:
-                    continue
-                o2 = order[:a] + [x for x in seg if x in s] + [x for x in seg if x not in s] + order[b + 1:]
-            else:
-                s = {p}
-                for x in seg:
-                    if x in s:
-                        s.update(succ[x])
-                if i in s:
-                    continue
-                o2 = order[:a] + [x for x in seg if x not in s] + [x for x in seg if x in s] + order[b + 1:]
-        r = run(o2, a2)
-        if r[0] < cur[0] - temp * (1 - it / tries) * math.log(u[3] + 1e-12) and r[1]:
-            cur, asg = r, a2
-            if o2 is not order:
-                order = o2
-                for k in range(a, b + 1):
-                    pos[order[k]] = k
-            if r[0] < best[0]:
-                best = (r[0], order, asg, r[2])
-    return best[1:]
-
-
-PLANS = {}
-
-
 def plan(ops):
-    if "best" not in PLANS:
-        deps = depend(ops)
-        succ = [[] for _ in ops]
-        for i in range(len(ops)):
-            for j in deps[i]:
-                succ[j].append(i)
-        rng = np.random.default_rng(PAR["seed"])
-        pool = [first_order(ops, deps, succ, rng) for k in range(PAR["starts"])]
-        for keep, tries in PAR["rounds"]:
-            pool = sorted([refine(ops, deps, succ, p[0], p[1], tries, PAR["temp"], rng) for p in pool], key=lambda p: p[2])[:keep]
-        order, asg, end = pool[0]
-        last = {}
-        for i in order:
-            b = ops[i]["bank"]
-            if b:
-                if b in last and ops[last[b]]["opts"][asg[last[b]]][0] != ops[i]["opts"][asg[i]][0]:
-                    deps[i] = sorted(set(deps[i] + [last[b]]))
-                last[b] = i
-        PLANS["best"] = (order, deps, asg, end)
-    return PLANS["best"]
+    deps = depend(ops)
+    nums = [int(x) for x in ORDER.split()]
+    order, asg = [abs(x) for x in nums], [0] * len(ops)
+    for x in nums:
+        asg[abs(x)] = 1 if x < 0 else 0
+    assert sorted(order) == list(range(len(ops)))
+    last = {}
+    for i in order:
+        b = ops[i]["bank"]
+        if b:
+            if b in last and ops[last[b]]["opts"][asg[last[b]]][0] != ops[i]["opts"][asg[i]][0]:
+                deps[i] = sorted(set(deps[i] + [last[b]]))
+            last[b] = i
+    return order, deps, asg
 
 
 def rank_program(g, core, T, topo):
@@ -703,7 +552,7 @@ def rank_program(g, core, T, topo):
     nxt = T.cores[(rank + 1) % len(T.cores)]
     assert topo.may_write(core, nxt)
     ops, neng = build(T, topo, core, nxt)
-    order, deps, asg = plan(ops)[:3]
+    order, deps, asg = plan(ops)
     spot = {i: k for k, i in enumerate(order)}
     eng = {"V": g.vector, "A": g.scalar, "P": g.tensor, "G": g, "S": g.sync}
     count, token, clock = {}, {}, {}
@@ -712,6 +561,9 @@ def rank_program(g, core, T, topo):
     for i in order:
         o = ops[i]
         q, fn = o["opts"][asg[i]][0], o["opts"][asg[i]][2]
+        if fn is None:
+            token[i] = ("qG", 0)
+            continue
         kn = known[q]
         need = {}
         for j in deps[i]:

from concourse.mybir import AluOpType as ALU, ActivationFunctionType as ACT, AxisListType as AX

V0, NS, NV, WD_ = 2560, 2048, 4, 3200
DUMMY = 3072
NP_ = 19
MAGIC = 12582912.0
BIG = 4096.0
OFF = 1536.0


def tpos(v):
    return 8 - v if v else 18


def blocks(v):
    d = dict(zip(range(8 - v), [4, 5, 6, 7, 8, 3, 2, 1]))
    d.update(zip(range(8, 15), range(9, 16)))
    d.update(zip(range(15, 15 + v), range(3)))
    d[tpos(v)] = v
    return d


def chunks(v):
    l = [("T", 4, tpos(v), 1, [(tpos(v), 1, "PT", 0, "ptX")], ("PT", 128, "ptV")),
         ("A", 8, 0, 8 - v, [(0, 4, "PS0", 0, "PS0"), (4, 4 - v, "PS1", 0, "ps1a" if v >= 2 else "PS1")], ("PV", 0, "pvA")),
         ("B", 8, 8, 8 if v else 7, [(8, 4, "PS2", 0, "PS2"), (12, 4 if v else 3, "PS3", 0, "PS3")], ("PV", 256, "pvB"))]
    if v >= 2:
        l.append(("L", 4, 16, v - 1, [(16, v - 1, "PS1", 256, "ps1b")], ("PT", 256, "ptL")))
    return l


def runs(pos, n, to):
    out = []
    for p in range(pos, pos + n):
        if out and out[-1][1] + out[-1][2] == to[p]:
            out[-1][2] += 1
        else:
            out.append([p, to[p], 1])
    return out


def halves(pos, n):
    return [(pos, 2), (pos + 2, 2)] if n == 4 and pos in PAR["half"] else [(pos, n)]


def _sb(cols, dtype):
    return ("sbuf", [128] + (cols if isinstance(cols, list) else [cols]), dtype)


SCRATCH = {}
NX, NL = 128 * NP_, 8 * NP_
for _d, _l in (("int32", dict(R=V0, STI=128, SGI=4, PC=16)),
               ("uint16", dict(L1=NL, L2=NL, TL=8, IX1=16, IX2=24)),
               ("float16", dict(ZA=[34, 8], ZB=[34, 8], ZT=[68, 4], ZL=[68, 4], EYH=128, C0=NX, C1=NX, C2=NX, PR=NX, SL=128, H2=128, Q4=128,
                                SC=128, SM=128, SW=128, WV=32, WB=128, FT=128, MT=512)),
               ("bfloat16", dict(XS=NX, SN=384, ZZ=1024, TRI=512, BE=256, G8=8, OB=128, TB=128, ONE=40, CP=16, CX=64, GA=256, GB=256,
                                 B0=128, BT=WD_, BB=256, ZF=[68, 4], EYK=32, EYB=128, E1=[8, 128], E2=[8, 128])),
               ("float32", dict(F=WD_, CN=WD_, IDT=WD_, THC=128, IO=256, COL=48, R16=16, HM=16, IG=128, IR=128, WN=64, THR=64, I4=160,
                                DUM=16, MD=8, A2=16, NE=8, OO=32, GS=128, FS=128, GT=128, GM=128, MB=128, YY=128, WDN=128, PW=32,
                                H0=128, HF=128, YS=NL, UF=NL, BU=256, BR=256))):
    for _n, _c in _l.items():
        SCRATCH[_n] = _sb(_c, _d)
for _v in range(NV + 1):
    SCRATCH["X%d" % _v] = _sb(NX, "bfloat16")
for _v in range(NV):
    SCRATCH["S%d_" % _v] = _sb(NL, "uint16")
    SCRATCH["U%d" % _v] = _sb(NL, "uint16")
for _n in ("PS0", "PS1", "PS2", "PS3", "PV", "PT"):
    SCRATCH[_n] = ("psum", [128, 512], "float32")
for _n in ("PD0", "PD1"):
    SCRATCH[_n] = ("psum", [128, 8, 64], "float32")

SEMAPHORES = (["qV", "qA", "qP", "qG", "sent", "outs", "stat", "lsg", "lst", "lcn"] + ["lr%d" % i for i in range(8)] + ["lx%d" % i for i in range(6)]
              + ["r%d" % i for i in range(60)])

PAR = {"cyc": 0.00085, "pec": 0.000425, "gat": 1.56, "sca": 3.8, "hop": 0.14, "ov": 0.008, "lx": 0.35, "ls": 0.3, "lat": 1.9,
       "mmo": 0.005, "rp": [640, 640, 512, 512, 256], "first": 3.0, "half": (8, 12), "mode": "xnr"}

ORDER = """
0 1 2 3 4 5 6 7 8 9 10 11 12 13 15 101 20 42 41 43 40 44 21 47 39 102 14 31 17 19 35 28 16 25 18 22 30 103 50 45 54 104 51 91 106 81 53 105
46 -94 77 76 75 55 52 66 71 107 56 59 110 70 57 95 73 67 109 38 108 48 78 -79 130 82 49 80 37 165 -60 111 133 113 -132 114 -89 83 69 162 98
92 74 68 148 93 62 72 63 84 149 115 112 140 -87 135 164 160 150 64 61 151 116 163 90 88 96 161 -144 32 23 100 24 26 27 33 34 29 36 152 124
-131 -86 -121 -123 134 -155 97 137 206 -85 -156 -138 -167 209 166 205 260 143 263 -157 168 169 207 170 -158 -159 171 208 153 216 217 259 172
174 173 136 175 126 210 -145 261 262 211 270 220 221 -118 -117 -176 212 177 213 178 214 264 179 -215 -127 218 274 -125 180 -219 265 181 275
271 222 276 65 120 122 128 226 224 266 -182 -119 267 -129 146 -185 -184 147 183 268 272 194 58 223 186 195 -269 225 154 196 201 187 227 -139
197 189 233 234 228 229 -190 230 198 -202 273 280 278 277 279 236 235 237 231 238 316 199 287 281 232 141 142 239 288 282 188 200 317 240
191 192 283 203 241 313 193 284 320 321 315 327 242 314 318 319 289 290 249 250 251 285 322 243 252 326 244 -286 245 323 254 255 246 328 330
291 256 325 -247 324 329 204 253 292 248 293 295 332 294 296 303 297 257 344 333 331 334 258 335 304 345 298 336 299 338 305 300 308 340 301
306 309 310 386 339 341 337 342 346 343 311 387 349 390 302 307 348 389 347 388 350 391 312 351 356 397 392 401 398 352 353 99 393 394 444
357 441 354 399 395 440 402 403 -355 -358 -396 400 405 359 360 365 442 361 362 443 445 406 451 452 363 446 -364 447 407 404 448 455 456 457
453 449 366 372 408 376 -367 409 368 458 -496 454 377 378 410 411 379 369 412 380 371 370 414 415 383 417 416 381 373 418 413 -450 420 421
419 430 497 431 432 459 374 -382 460 375 494 498 461 495 462 468 502 501 500 499 469 470 463 503 471 472 504 464 -507 465 433 384 422 508
466 423 509 435 436 437 473 525 505 510 511 506 467 385 434 424 474 513 475 425 484 438 426 526 514 427 485 515 439 476 486 516 477 428 517
512 478 519 479 487 489 490 669 521 491 520 480 481 522 529 567 429 570 488 523 524 527 482 492 530 531 528 537 532 483 493 568 538 571 569
533 518 534 572 578 616 535 573 579 615 580 582 -536 574 575 -539 540 576 546 541 618 619 581 617 -577 542 543 626 627 544 620 628 621 630
631 632 -586 -545 584 583 670 547 548 629 553 633 585 622 623 587 -557 549 671 558 624 588 550 596 677 564 593 559 -625 589 552 590 551 560
636 637 594 701 591 -592 672 554 595 646 561 634 635 702 562 647 643 638 644 597 555 673 563 700 598 565 712 698 -678 639 674 556 640 703
699 705 706 607 608 599 711 600 609 707 641 715 -642 704 610 729 708 645 675 713 648 612 601 651 710 709 714 -676 679 613 716 649 652 602
717 664 603 680 718 719 604 665 605 666 730 650 720 725 681 566 611 614 606 667 668 653 659 682 721 726 683 654 723 655 731 728 684 685 687
724 656 660 661 686 688 695 771 774 727 657 662 658 663 733 689 732 -775 734 690 776 735 691 722 786 692 736 772 773 822 777 -787 823 -693
737 -696 778 694 697 820 741 782 738 779 783 739 780 784 824 834 819 835 781 -740 743 -742 -790 744 821 791 745 836 750 825 746 747 830 800
748 875 831 832 785 788 826 789 -749 827 828 792 -757 837 876 877 -761 752 751 753 -829 793 833 838 878 794 762 754 797 795 883 768 798 799
756 755 758 763 839 847 796 840 841 801 884 803 764 759 765 906 907 848 842 766 850 760 802 843 804 767 844 904 879 908 912 911 769 -918 909
880 -917 770 851 811 852 845 849 812 846 805 910 806 855 807 856 813 913 814 881 914 919 869 808 916 -882 920 915 870 853 936 809 885 854
871 921 816 923 886 -817 937 -943 905 872 815 887 863 888 924 889 922 864 925 944 865 810 874 873 818 866 890 857 -891 926 858 927 893 859
928 892 867 868 929 932 894 860 901 902 861 955 953 947 959 960 903 862 933 930 895 938 896 897 898 935 -899 931 934 945 -949 941 961 -951
939 900 962 940 954 956 946 950 948 942 -957 952 958
"""


def build(T, topo, core, nxt):
    ops, tag = [], ["s"]
    CYC, PEC, GAT, SCA = PAR["cyc"], PAR["pec"], PAR["gat"], PAR["sca"]

    def op(opts, rd, wr, sem=None, n=1, lat=0.0, link=0.0, first=False):
        bank = None
        for k in wr:
            if k[:2] in ("pv", "pt", "ps"):
                bank = k[:2]
        ops.append({"opts": opts, "rd": rd, "wr": wr, "sem": sem, "n": n, "lat": lat, "bank": bank, "link": link, "first": first,
                    "tag": tag[0], "cont": -1})

    def vc(n, k=1.0):
        return PAR["ov"] + max(64, n * k) * CYC

    def f_ts(out, in0, s1, s2, o0, o1):
        if o1 is None:
            return lambda g: g.vector.tensor_scalar(out, in0, s1, None, o0)
        return lambda g: g.vector.tensor_scalar(out, in0, s1, s2, o0, o1)

    def f_ac(out, a, f, bias, scale):
        return lambda g: g.scalar.activation(out, a, f, bias=bias, scale=scale)

    def ts(out, in0, s1, s2, o0, o1, n, rd, wr, k=1.0):
        op([("V", vc(n, k), f_ts(out, in0, s1, s2, o0, o1))], rd, wr)

    def tt(out, a, b, o, n, rd, wr, k=1.0):
        op([("V", vc(n, k), lambda g: g.vector.tensor_tensor(out, a, b, o))], rd, wr)

    def cp(out, a, n, rd, wr, k=1.0):
        op([("V", vc(n, k), lambda g: g.vector.tensor_copy(out, a))], rd, wr)

    def ac(out, a, f, bias, scale, n, rd, wr, k=1.0):
        op([("A", 0.02 + vc(n, k), f_ac(out, a, f, bias, scale))], rd, wr)

    def lin(out, a, scale, bias, n, rd, wr, k=1.0, kv=None):
        op([("A", 0.02 + vc(n, k), f_ac(out, a, ACT.Identity, bias, scale)),
            ("V", vc(n, kv or k), f_ts(out, a, scale, bias, ALU.mult, ALU.add))], rd, wr)

    def mset(out, val, n, wr, k=1.0):
        op([("V", vc(n, k), lambda g: g.vector.memset(out, val))], [], wr)

    def mm(lst, cyc, rd, wr):
        def fn(g):
            r = None
            for (o, l, rh, st, sp) in lst:
                r = g.tensor.matmul(o, l, rh, st, sp)
            return r
        op([("P", PAR["mmo"] * len(lst) + cyc * PEC, fn)], rd, wr)

    def dma(q, pairs, sem, rd, wr, lat, first=False):
        def fn(g):
            e = g.sync if q == "S" else g.scalar
            for (o, i) in pairs:
                e.dma_start(o, i).then_inc(T.sem[sem], 16)
        op([(q, 0.06 * len(pairs), fn)], rd, wr, sem=sem, n=16 * len(pairs), lat=lat, first=first)

    rid, pid = topo.addr(nxt)[0], topo.addr(nxt)[1]
    mask = topo.mask(core, nxt)
    neng = len(topo.engines(core, nxt))
    nsend = [0]

    def send(dst, src, rd, wr, link):
        sem = "r%d" % nsend[0]
        if not nsend[0]:
            op([("G", PAR["first"], None)], rd, ["G1"])
        rd = rd + ["G1"]
        nsend[0] += 1
        op([("G", 0.5, lambda g: g.remote_dma(dst, src, T.sem[sem], T.sem.sent, pid, rid, mask))], rd, wr, sem=sem, n=neng,
           lat=PAR["lat"] + link, link=link)

    def iota(out, pat, base, cm, n, wr, flag=True):
        if flag:
            op([("G", 0.15 + 2 * n * CYC, lambda g: g.iota(out, pat, base, cm, allow_small_or_imprecise_dtypes=True))], [], wr)
        else:
            op([("G", 0.15 + 2 * n * CYC, lambda g: g.iota(out, pat, base, cm))], [], wr)

    def ms(out, val, n, wr):
        iota(out, [[0, n]], int(val), 0, n, wr)

    def sel(B, pat, o, fill, base, cm, n, k, src):
        op([("G", 0.2 + 2 * n * CYC, lambda g: g.affine_select(B, src, pat, o, fill, base, cm))], ["ZZ"], [k])

    C = lambda i: T.COL[:, i:i + 1]
    SLs = lambda v: T["S%d_" % v]
    bk = lambda name, pos, n: ["%s_%d" % (name, p) for p in range(pos, pos + n)]
    cs = lambda pos, n: slice(128 * pos, 128 * (pos + n))
    ls = lambda pos, n: slice(8 * pos, 8 * (pos + n))
    b0 = blocks(0)
    RP = [sum(PAR["rp"][:i]) for i in range(len(PAR["rp"]) + 1)]
    NR = len(PAR["rp"])
    dma("A", [(T.SGI[:, 0:1], T.sg[:])], "lsg", [], ["SGI"], 2.0, True)
    dma("S", [(T.STI[:], T.st0[:])], "lst", [], ["STI"], 2.2, True)
    for c in range(NR):
        dma("S" if c % 2 == 0 else "A", [(T.R[:, RP[c]:RP[c + 1]], T.recs[:, RP[c]:RP[c + 1]])], "lr%d" % c, [], ["R%d" % c], 2.3 + 4.2 * RP[c + 1] / V0, True)
    first_pieces = [p for ch in chunks(0) for p in ch[4]]
    for i, (pos, n, _a, _b, _c) in enumerate(first_pieces):
        dma("S", [(T.XS[:, cs(a, k)], T.cx0[:, cs(b, k)]) for (a, b, k) in runs(pos, n, b0)], "lx%d" % i, [], ["XS%d" % i], 6.3 + 0.4 * i, True)
    iota(T.PC[:, 0:1], [[0, 1]], 0, 1, 1, ["PC0"], False)
    iota(T.IO[:], [[1, 256]], 0, 0, 256, ["IO"])
    iota(T.IG[:], [[1, 8], [0, 16]], 0, 0, 128, ["IG"])
    iota(T.IR[:], [[0, 8], [1, 16]], 0, 0, 128, ["IR"])
    iota(T.MD[:], [[16, 8]], DUMMY, 0, 8, ["MD"])
    iota(T.I4[:, 0:32], [[1, 4], [4, 8]], 0, 0, 32, ["I4a"])
    iota(T.I4[:, 32:96], [[0, 16], [1, 4]], 0, 0, 64, ["I4b"])
    iota(T.I4[:, 96:160], [[0, 2], [1, 8], [0, 4]], 0, 0, 64, ["I4c"])
    mset(T.ZZ[:, 0:512], 11.0, 512, ["ZZ"], 0.5)
    mset(T.ZZ[:, 512:1024], 0.0, 512, ["ZZ"], 0.5)
    sel(T.TRI[:, 0:512], [[16, 8], [0, 4], [1, 16]], ALU.is_gt, 99.0, 0, -1, 512, "TRI0", T.ZZ[:, 0:512])
    for h, f in ((0, BIG), (1, -BIG)):
        sel(T.BE[:, 128 * h:128 * h + 128], [[-1, 128]], ALU.not_equal, f, 0, 1, 128, "BE%d" % h, T.ZZ[:, 512:640])
    ms(T.F[:, V0:WD_], 0, 640, ["F%d" % NR])
    for a in range(4):
        iota(T.IDT[:, 800 * a:800 * a + 800], [[1, 800]], 800 * a, 0, 800, ["ID%d" % a])
    ms(T.ONE[:, 0:2], BIG, 2, ["ONEa"])
    ms(T.ONE[:, 2:4], 1.0, 2, ["ONEb"])
    ms(T.ONE[:, 16:24], (V0 - BIG) / 16, 8, ["ONEd"])
    ms(T.ONE[:, 24:32], (V0 + BIG) / 16, 8, ["ONEe"])
    ms(T.ONE[:, 32:40], BIG / 16, 8, ["ONEf"])
    ms(T.CP[:], 0.0, 16, ["CP"])
    ms(T.PW[:, 16:32], 1.0, 16, ["PW1"])
    mset(T.THC[:, 0:64], 0.5, 64, ["THCa"])
    mset(T.THC[:, 64:128], -0.5, 64, ["THCb"])
    ts(T.PC[:, 4:5], T.PC[:, 0:1], 4, None, ALU.arith_shift_right, None, 1, ["PC0"], ["PC4"])
    ts(T.PC[:, 8:9], T.PC[:, 0:1], 15, None, ALU.bitwise_and, None, 1, ["PC0"], ["PC8"])
    ts(T.PC[:, 9:10], T.PC[:, 0:1], 7, None, ALU.bitwise_and, None, 1, ["PC0"], ["PC9"])
    ts(T.PC[:, 10:11], T.PC[:, 0:1], 3, None, ALU.bitwise_and, None, 1, ["PC0"], ["PC10"])
    ts(T.PC[:, 11:12], T.PC[:, 0:1], 16, None, ALU.bitwise_and, None, 1, ["PC0"], ["PC11"])
    ts(T.PC[:, 12:13], T.PC[:, 0:1], 2, None, ALU.arith_shift_right, None, 1, ["PC0"], ["PC12"])
    (G_, P_, R_, R8, R4, P16, P4, LT12, LT14, GE14, CH_, CR, E_, M1213, M1214, SIG, TAU, ODD, BI, BI0, CSL, CH2, CQ4, CSC, CSM, CSW,
     CQ, C14, PWC, PWL, PWH, LT8, CSI, ME, MO, K15, PO, M256, XP, XM) = range(40)
    k_ = lambda *a: ["c%d" % i for i in a]
    r16 = lambda i: T.R16[:, i:i + 1]
    IO = T.IO[:, 0:128]
    MT = lambda i: T.MT[:, 128 * i:128 * i + 128]
    cp(C(G_), T.PC[:, 4:5], 1, ["PC4"], k_(G_))
    cp(C(P_), T.PC[:, 0:1], 1, ["PC0"], k_(P_))
    cp(T.COL[:, R_:R_ + 5], T.PC[:, 8:13], 5, ["PC8", "PC9", "PC10", "PC11", "PC12"], k_(R_, R8, R4, P16, P4))
    cp(C(E_), T.SGI[:, 0:1], 1, ["SGI"], k_(E_))
    ts(C(LT14), C(R_), 14.0, None, ALU.is_lt, None, 1, k_(R_), k_(LT14))
    ts(C(LT12), C(R_), 12.0, None, ALU.is_lt, None, 1, k_(R_), k_(LT12))
    ts(C(GE14), C(R_), 14.0, None, ALU.is_ge, None, 1, k_(R_), k_(GE14))
    lin(C(CH_), C(LT12), 0.5, 0.0, 1, k_(LT12), k_(CH_))
    lin(C(CQ), C(LT12), 0.25, 0.0, 1, k_(LT12), k_(CQ))
    ts(T.R16[:], T.IO[:, 0:16], C(R_), None, ALU.is_equal, None, 16, ["IO"] + k_(R_), ["R16"])
    lin(C(C14), r16(14), -2050.0, 0.0, 1, ["R16"], k_(C14))
    lin(C(K15), r16(15), 1.0 / 128, 0.0, 1, ["R16"], k_(K15))
    lin(C(M1213), r16(12), 1.0, r16(13), 1, ["R16"], k_(M1213))
    lin(C(PO), C(M1213), OFF, 0.0, 1, k_(M1213), k_(PO))
    lin(C(CR), C(LT12), 70.25, 128.0, 1, k_(LT12), k_(CR))
    lin(C(XP), C(LT12), 16.0, 128.0, 1, k_(LT12), k_(XP))
    lin(C(XM), C(LT12), -16.0, -128.0, 1, k_(LT12), k_(XM))
    lin(C(M1214), r16(12), 1.0, r16(14), 1, ["R16"], k_(M1214))
    lin(C(ODD), r16(13), 1.0, r16(15), 1, ["R16"], k_(ODD))
    lin(C(SIG), C(M1214), -1.0, C(ODD), 1, k_(ODD, M1214), k_(SIG))
    lin(C(TAU), C(SIG), 0.5, C(LT12), 1, k_(SIG, LT12), k_(TAU))
    lin(C(BI0), r16(14), 4092.0, 0.0, 1, ["R16"], k_(BI0))
    lin(C(M256), r16(15), 128.0, C(BI0), 1, ["R16"] + k_(BI0), k_(M256))
    lin(C(BI), C(M1213), -OFF, C(M256), 1, k_(M1213, M256), k_(BI))
    lin(C(CSL), r16(15), -1.125, C(LT12), 1, ["R16"] + k_(LT12), k_(CSL))
    lin(C(CH2), r16(15), -253.0 / 512, C(CH_), 1, ["R16"] + k_(CH_), k_(CH2))
    lin(C(CQ4), r16(15), -219.0 / 2048, C(CQ), 1, ["R16"] + k_(CQ), k_(CQ4))
    lin(C(CSC), C(C14), -1.0, C(CH_), 1, k_(C14, CH_), k_(CSC))
    lin(C(CSM), r16(15), -9.0 / 128, C(C14), 1, ["R16"] + k_(C14), k_(CSM))
    lin(C(CSW), r16(15), -9.0 / 128, C(CH_), 1, ["R16"] + k_(CH_), k_(CSW))
    ts(T.EYH[:], IO, C(P_), None, ALU.is_equal, None, 128, ["IO"] + k_(P_), ["EYH"])
    ts(T.OB[:], T.IG[:], C(G_), None, ALU.is_equal, None, 128, ["IG"] + k_(G_), ["OB"])
    ts(T.GA[:, 0:128], T.IR[:], 12.0, C(GE14), ALU.is_lt, ALU.mult, 128, ["IR"] + k_(GE14), ["GA0"])
    tt(T.GA[:, 128:256], T.GA[:, 0:128], T.OB[:], ALU.mult, 128, ["GA0", "OB"], ["GA1"], 2.0)
    lin(T.GB[:, 0:128], T.EYH[:], C(LT12), 0.0, 128, ["EYH"] + k_(LT12), ["GB0"], 1.0, 0.5)
    tt(T.B0[:], T.GA[:, 128:256], T.GB[:, 0:128], ALU.add, 128, ["GA1", "GB0"], ["B0"], 2.0)
    ac(T.EYB[:], T.IR[:], ACT.Abs, -12.5, 1.0, 128, ["IR"], ["EYB"])
    ts(T.GB[:, 128:256], T.EYB[:], 1.0, C(K15), ALU.is_lt, ALU.mult, 128, ["EYB"] + k_(K15), ["GB1"], 0.5)
    tt(MT(0), T.GB[:, 128:256], T.OB[:], ALU.mult, 128, ["GB1", "OB"], ["MT0"], 2.0)
    for (M, col) in (("H2", CH2), ("Q4", CQ4), ("SC", CSC)):
        lin(T[M][:], T.B0[:], C(col), 0.0, 128, ["B0"] + k_(col), [M], 1.0, 0.5)
    for (M, col, i) in (("SL", CSL, 1), ("SM", CSM, 2)):
        lin(MT(i), T.B0[:], C(col), 0.0, 128, ["B0"] + k_(col), ["MT%d" % i], 1.0, 0.5)
        tt(T[M][:], MT(i), MT(0), ALU.add, 128, ["MT0", "MT%d" % i], [M], 2.0)
    ts(T.G8[:], T.IO[:, 0:8], C(G_), None, ALU.is_equal, None, 8, ["IO"] + k_(G_), ["G8"])
    lin(T.WV[:, 0:8], T.G8[:], C(E_), 0.0, 8, ["G8"] + k_(E_), ["WV0"])
    lin(T.WV[:, 8:16], T.WV[:, 0:8], -1.0, 0.0, 8, ["WV0"], ["WV1"])
    lin(T.WV[:, 16:24], T.G8[:], r16(13), 0.0, 8, ["G8", "R16"], ["WV2"])
    lin(T.WV[:, 24:32], T.G8[:], r16(12), 0.0, 8, ["G8", "R16"], ["WV3"])
    WVK = ["WV%d" % i for i in range(4)]
    for z in ("ZA", "ZB", "ZT", "ZL"):
        mset(T[z][:], 0.0, 272, [z], 0.5)
    ms(T.ZF[:], 0, 272, ["ZF"])
    mset(T.PW[:, 8:16], 0.5, 8, ["PW0"])
    op([("V", vc(8), lambda g: g.vector.tensor_tensor_scan(T.PW[:, 0:8], T.PW[:, 8:16], T.ZZ[:, 512:520], 1.0, ALU.mult, ALU.add))], ["PW0", "ZZ"], ["PWa"])
    ts(T.NE[:], T.IO[:, 0:8], C(R8), None, ALU.is_equal, None, 8, ["IO"] + k_(R8), ["NE"])
    tt(T.A2[:, 0:8], T.NE[:], T.PW[:, 0:8], ALU.mult, 8, ["NE", "PWa"], ["A2s"])
    op([("V", vc(8), lambda g: g.vector.tensor_reduce(C(PWC), T.A2[:, 0:8], AX.X, ALU.add))], ["A2s"], k_(PWC))
    ts(C(LT8), C(R_), 8.0, None, ALU.is_lt, None, 1, k_(R_), k_(LT8))
    lin(C(PWL), C(PWC), C(LT8), 0.0, 1, k_(PWC, LT8), k_(PWL))
    ts(C(PWH), C(PWC), C(PWL), C(LT12), ALU.subtract, ALU.mult, 1, k_(PWC, PWL, LT12), k_(PWH))
    lin(C(CSI), C(LT8), 2.0, 0.0, 1, k_(LT8), k_(CSI))
    lin(T.BU[:], T.IO[:], C(PWL), -0.499, 256, ["IO"] + k_(PWL), ["BU"])
    ts(T.BR[:], T.BU[:], MAGIC, MAGIC, ALU.add, ALU.subtract, 256, ["BU"], ["BR"])
    tt(T.BB[:], T.BU[:], T.BR[:], ALU.is_gt, 256, ["BU", "BR"], ["BB"], 2.0)
    lin(T.OO[:, 0:16], T.IO[:, 0:16], C(PWH), -0.499, 16, ["IO"] + k_(PWH), ["OOa"])
    ts(T.OO[:, 16:32], T.OO[:, 0:16], MAGIC, MAGIC, ALU.add, ALU.subtract, 16, ["OOa"], ["OOb"])
    tt(T.DUM[:], T.OO[:, 0:16], T.OO[:, 16:32], ALU.is_gt, 16, ["OOa", "OOb"], ["DUM", "DUMb"])
    ts(T.HM[:], T.DUM[:], 2.0, C(LT12), ALU.mult, ALU.subtract, 16, ["DUM", "DUMb"] + k_(LT12), ["HM"])
    for a in range(13):
        w = min(256, WD_ - 256 * a)
        lin(T.BT[:, 256 * a:256 * a + w], T.BB[:, 0:w], C(CSI), T.HM[:, a:a + 1], w, ["BB", "HM"] + k_(CSI), ["BT%d" % a], 1.0, 0.5)
    IDK, BK = ["ID%d" % a for a in range(4)], ["BT%d" % a for a in range(13)]
    ts(C(ME), C(P16), 0.0, C(LT12), ALU.is_equal, ALU.mult, 1, k_(P16, LT12), k_(ME))
    lin(C(MO), C(ME), -1.0, C(LT12), 1, k_(LT12, ME), k_(MO))
    lin(T.WB[:], T.OB[:], C(E_), 0.0, 128, ["OB"] + k_(E_), ["WB"], 1.0, 0.5)
    ts(T.GA[:, 0:128], T.IR[:], C(R_), None, ALU.is_gt, None, 128, ["IR"] + k_(R_), ["GA0"])
    tt(T.TB[:], T.GA[:, 0:128], T.OB[:], ALU.mult, 128, ["GA0", "OB"], ["TB"], 2.0)
    ts(T.WN[:, 0:32], T.I4[:, 96:128], C(G_), C(GE14), ALU.is_equal, ALU.mult, 32, ["I4c"] + k_(G_, GE14), ["WNa"])
    lin(T.WN[:, 32:64], T.WN[:, 0:32], -1.0, 0.0, 32, ["WNa"], ["WNb"])
    ts(T.GS[:, 0:64], T.I4[:, 32:96], C(R4), -65536.0, ALU.not_equal, ALU.mult, 64, ["I4b"] + k_(R4), ["GS"])
    lin(T.THR[:, 0:32], T.GS[:, 0:32], 1.0, 5.0, 32, ["GS"], ["THRa"])
    lin(T.THR[:, 32:64], T.GS[:, 32:64], 1.0, 21.0, 32, ["GS"], ["THRb"])
    ts(T.EYK[:], T.I4[:, 0:32], C(P4), None, ALU.is_equal, None, 32, ["I4a"] + k_(P4), ["EYK"])
    lin(T.DUM[:, 0:8], T.MD[:], 1.0, C(R_), 8, ["MD"] + k_(R_), ["DUM"])
    lin(T.DUM[:, 8:16], T.MD[:], 1.0, C(R_), 8, ["MD"] + k_(R_), ["DUMb"])
    lin(MT(1), T.B0[:], C(CSW), 0.0, 128, ["B0"] + k_(CSW), ["MT1"], 1.0, 0.5)
    lin(MT(2), MT(0), OFF, 0.0, 128, ["MT0"], ["MT2"], 1.0, 0.5)
    lin(MT(3), T.EYH[:], C(M1213), 0.0, 128, ["EYH"] + k_(M1213), ["MT3"], 1.0, 0.5)
    tt(T.FT[:], MT(1), MT(2), ALU.add, 128, ["MT1", "MT2"], ["FT"], 2.0)
    tt(T.SW[:], T.FT[:], MT(3), ALU.add, 128, ["FT", "MT3"], ["SW"], 2.0)
    for c in range(NR):
        lin(T.F[:, RP[c]:RP[c + 1]], T.R[:, RP[c]:RP[c + 1]], 1.0, 0.0, RP[c + 1] - RP[c], ["R%d" % c], ["F%d" % c])
    FK = ["F%d" % c for c in range(NR + 1)]
    CK = ["CNa", "CNb"]
    dma("S", [(T.CN[:], T.F[:])], "lcn", FK + ["XS%d" % (len(first_pieces) - 2)], CK + ["CNd"], 6.0)
    dma("S", [(T.yp[16 * g:16 * g + 12, 0:V0], T.F[16 * g:16 * g + 12, 0:V0]) for g in range(8)], "stat",
        FK[:NR] + ["CNd", "XS%d" % (len(first_pieces) - 1)], ["ypa"], 6.0)
    for i, (pos, n, _a, _b, _c) in enumerate(first_pieces):
        lin(T.X0[:, cs(pos, n)], T.XS[:, cs(pos, n)], 1.0, C(XP), 128 * n, ["XS%d" % i] + k_(XP) + bk("XF", pos, n), bk("X0", pos, n), 1.0, 0.5)
    for ch in chunks(0):
        for (a, b, k) in runs(ch[2], ch[3], b0):
            cp(SLs(0)[:, ls(a, k)], T.STI[:, ls(b, k)], 8 * k, ["STI"], bk("S0", a, k))
    Fwin, Cwin, Iwin = T.F[:, 0:WD_], T.CN[:, 0:WD_], T.IDT[:, 0:WD_]
    GK = FK + k_(LT14, BI)

    def where(v):
        if v == NV - 1:
            return {p: p for p in blocks(v)}
        back = {b: p for p, b in blocks(v + 1).items()}
        return {p: back[b] for p, b in blocks(v).items()}

    def send_list(v, pos, n):
        if v < NV - 1:
            for (a, b, k) in runs(pos, n, where(v)):
                send(SLs(v + 1)[:, ls(b, k)], T["U%d" % v][:, ls(a, k)], bk("U%d" % v, a, k), bk("S%d" % (v + 1), b, k), PAR["ls"])
        else:
            send(T.YS[:, ls(pos, n)], T.UF[:, ls(pos, n)], bk("UF", pos, n), bk("YS", pos, n), PAR["ls"])

    def walk(v, ch, step):
        name, nb, pos0, nblk, pieces, (pvb, c0, pv) = ch
        H, M, j0, n = 16 // nb, 128 * nblk // nb, 128 * pos0, 128 * nblk
        X, xn = T["X%d" % v], "X%d" % v
        src, sk = [(SLs(v), "S%d" % v), (T.L1, "L1"), (T.L2, "L2")][step]
        cn = "C%d" % step
        CB = T[cn]
        PV, Z, zk = T[pvb], T["Z" + name], "Z" + name
        last = v == NV - 1
        for (pos, k, psb, pc, ps) in pieces:
            sl, PS, w = cs(pos, k), T[psb][:, pc:pc + 128 * k], 128 * k
            if step == 0:
                mm([(PS, T.SL[:], X[:, sl], True, True)], w, ["SL"] + bk(xn, pos, k) + (["PS1"] if ps[:2] == "ps" else []), [ps])
            lin(CB[:, sl], Fwin.indirect(src[:, ls(pos, k)]), C(LT14), C(BI), w, GK + bk(sk, pos, k), bk(cn, pos, k), GAT)
            tt(T.PR[:, sl], CB[:, sl], PS, ALU.mult, w, bk(cn, pos, k), [ps] + bk("PR", pos, k))
        mm([(PV[0:M, c0 + i:c0 + 32 * nb:nb], T.PR[:, j0 + i:j0 + n:nb], T.WV[:], True, True) for i in range(nb)], max(32, min(64, M)) * nb,
           WVK + bk("PR", pos0, nblk), [pv])
        so = {"A": 0, "B": 128, "T": 256, "L": 320}[name]
        sn = T.SN[0:M, so:so + 16 * nb]
        tt(sn, PV[0:M, c0:c0 + 16 * nb], T.THC[0:M, 64 - 8 * nb:64 + 8 * nb], ALU.is_gt, 16 * nb, ["THCa", "THCb"], [pv, "SN" + name])
        tt(Z[0:M, H:17 * H:H, :], sn, PV[0:M, c0 + 16 * nb:c0 + 32 * nb], ALU.mult, 16 * nb, ["SN" + name], [pv, zk])
        lo = PV[:, c0:c0 + 8 * nblk]
        mm([(lo, Z[0:M, H * (1 + 8 * hl) - h:H * (9 + 8 * hl) - h, :], T.EYH[0:M, h:M:H], hl == 0 and h == 0, hl == 1 and h == H - 1)
            for hl in range(2) for h in range(H)], 128 * H, ["EYH", zk], [pv])
        if step < 2:
            dst, dk = [(T.L1, "L1"), (T.L2, "L2")][step]
            lin(dst[:, ls(pos0, nblk)], lo, 1.0, OFF, 8 * nblk, [], [pv] + bk(dk, pos0, nblk))
        elif name == "T":
            lin(T.TL[:], lo, 1.0, OFF, 8, [], [pv, "TL"])
        else:
            dst, dk = (T.UF, "UF") if last else (T["U%d" % v], "U%d" % v)
            lin(dst[:, ls(pos0, nblk)], lo, 1.0, OFF, 8 * nblk, [], [pv] + bk(dk, pos0, nblk))
            send_list(v, pos0, nblk)
        for (pos, k, psb, pc, ps) in pieces:
            sl, PS, w = cs(pos, k), T[psb][:, pc:pc + 128 * k], 128 * k
            md = PAR["mode"][step]
            lst = [("Q4", xn), ("Q4", "C1"), ("H2", cn)] if md == "r" else [("H2", xn), ("SC", cn), ("SM", cn)]
            if ps[0] == "P":
                for i, (m, q) in enumerate(lst):
                    mm([(PS, T[m][:], T[q][:, sl], i == 0, i == len(lst) - 1)], w, [m] + bk(q, pos, k), [ps])
                    ops[-1]["cont"] = len(ops) - 2 if i else -1
            else:
                mm([(PS, T[m][:], T[q][:, sl], i == 0, i == len(lst) - 1) for i, (m, q) in enumerate(lst)], w * len(lst),
                   sorted(set(m for m, q in lst)) + [y for m, q in lst for y in bk(q, pos, k)], [ps])
            if md == "x":
                lin(X[:, sl], PS, C(LT12), C(XP), w, k_(LT12, XP), [ps] + bk(xn, pos, k))
            if md == "r":
                lin(X[:, sl], PS, 1.0, C(CR), w, k_(CR), [ps] + bk(xn, pos, k))
                xo = "X%d" % (v + 1)
                for (a, b, kk) in ([(a, a, b) for a, b in halves(pos, k)] if last else runs(pos, k, where(v))):
                    send(T[xo][:, cs(b, kk)], X[:, cs(a, kk)], bk(xn, a, kk), bk(xo, b, kk), PAR["lx"] * kk)

    def equalities(lst, lk, G, gk, E, ek):
        for o, col in ((0, ME), (1, MO)):
            lin(G[:, 128 * o:128 * o + 128], T.BT[:, 0:WD_].indirect(lst), C(col), 0.0, 128, BK + lk + k_(col), [gk + str(o)], GAT)
        for t in range(2):
            mm([(T["PD%d" % h][:, :, 32 * t + 16 * o:32 * t + 16 * o + 16], G[64 * h + 32 * t:64 * h + 32 * t + 32, 128 * o:128 * o + 128],
                 G[64 * h + 32 * t:64 * h + 32 * t + 32, 128 * o:128 * o + 128], True, True)
                for h in (1, 0) for o in (0, 1)], 512, [gk + "0", gk + "1"], ["PD0", "PD1"])
        tt(E[:, :, 64:128], T.PD1[:], T.TRI[:, 0:512], ALU.is_gt, 512, ["TRI0"], ["PD1", ek + "1"])
        tt(E[:, :, 0:64], T.PD0[:], T.TRI[:, 0:512], ALU.is_gt, 512, ["TRI0"], ["PD0", ek + "0"])

    def earlier(o, E, w, st):
        return [(T.PT[:, o + k:o + 1 + k], E[:, k, :], T.ONE[:, w:w + 1], st, st or k == 7) for k in range(8)]

    def stage1(v):
        sL, lk = T.L2[:, ls(tpos(v), 1)], "L2_%d" % tpos(v)
        equalities(sL, [lk], T.GA, "GA", T.E1, "E1")
        lin(T.GS[:], Cwin.indirect(sL), 1.0, 0.0, 128, CK + [lk], ["GS"], GAT)
        mm(earlier(384, T.E1, 0, True), 512, ["E10", "E11", "ONEa"], ["pt1"])
        tt(T.MD[:], T.PT[:, 384:392], T.DUM[:, 0:8], ALU.min, 8, ["DUM"], ["pt1", "MD"])
        tt(T.IX1[:, 0:8], T.MD[:], sL, ALU.max, 8, ["MD", lk], ["IXs"])

    def train(v):
        tp = tpos(v)
        tc, lc = cs(tp, 1), ls(tp, 1)
        PT = T.PT
        tt(T.IX1[:, 8:16], T.MD[:], T.TL[:], ALU.max, 8, ["MD", "TL"], ["IXt"])
        tt(T.NE[:], T.IX1[:, 0:8], T.IX1[:, 8:16], ALU.not_equal, 8, ["IXs", "IXt"], ["NE"])
        lin(T.FS[:], T.C2[:, tc], 1.0, C(PO), 128, ["C2_%d" % tp] + k_(PO), ["FS"])
        mm([(T.PD0[:, 0:2, :], T.WB[:], T.PR[:, tc], True, True)], 128, ["WB", "PR_%d" % tp], ["PD0"])
        ts(T.MB[:], T.PD0[:, 0:2, :], C(SIG), C(TAU), ALU.mult, ALU.is_gt, 128, k_(SIG, TAU), ["PD0", "MB"])
        tt(Cwin.indirect(T.IX1[:, 0:8]), T.GS[:], T.MB[:], ALU.add, 128, ["IXs", "GS", "MB"], CK, SCA)
        tt(T.GM[:], T.GS[:], T.MB[:], ALU.mult, 128, ["GS", "MB"], ["GM"], 2.0)
        equalities(T.IX1[:, 8:16], ["IXt"], T.GB, "GB", T.E2, "E2")
        lin(T.GT[:], Cwin.indirect(T.TL[:]), 1.0, 0.0, 128, CK + ["TL"], ["GT"], GAT)
        lin(T.FT[:], Fwin.indirect(T.TL[:]), C(LT14), C(BI), 128, GK + ["TL"], ["FT"], GAT)
        mm([(PT[:, 392:456], T.GM[:], T.WN[:], True, False), (PT[:, 424:456], T.GT[:], T.WN[:, 0:32], False, True)], 512,
           ["GM", "GT", "WNa", "WNb"], ["ptB"])
        tt(T.ZF[:, 4:68:4, :], PT[:, 392:456], T.THR[:], ALU.is_lt, 64, ["THRa", "THRb"], ["ptB", "ZF"])
        mm([(PT[:, 0:128], T.SW[:], T.FT[:], True, False), (PT[:, 0:128], T.H2[:], T["X%d" % v][:, tc], False, True)], 256,
           ["SW", "H2", "FT", "X%d_%d" % (v, tp)], ["ptX"])
        ts(T.WDN[:], PT[:, 0:128], MAGIC, MAGIC, ALU.add, ALU.subtract, 128, [], ["ptX", "WDN"])
        mm([(PT[:, 456:464], T.ZF[:, 4 * (1 + 8 * hl) - h:4 * (9 + 8 * hl) - h, :], T.EYK[:, 8 * h:8 * h + 8], hl == 0 and h == 0, False)
            for hl in range(2) for h in range(4)] + earlier(456, T.E2, 2, False), 1024, ["ZF", "EYK", "E20", "E21", "ONEb"], ["ptW"])
        tt(T.CP[:, 1:9], PT[:, 456:464], T.NE[:], ALU.is_lt, 8, ["NE"], ["ptW", "CP"])
        cx = T.CX[:, 16 * v:16 * v + 9]
        ini = T.CX[:, 16 * v - 8:16 * v - 7] if v else 0.0
        op([("V", vc(9), lambda g: g.vector.tensor_tensor_scan(cx, T.PW[:, 16:25], T.CP[:, 0:9], ini, ALU.mult, ALU.add))], ["CP", "PW1"], ["CX"])
        cpv = T.CP[:, 1:9]

        def ranks(o, h, w):
            return [(PT[:, o:o + 8], T.OB[:], T.ONE[:, w:w + 8], True, False), (PT[:, o:o + 8], T.TB[:], cpv, False, False),
                    (PT[:, o:o + 8], T.BE[:, 128 * h:128 * h + 128], cpv, False, False), (PT[:, o:o + 8], T.OB[:], cx[:, 0:8], False, True)]
        mm(ranks(464, 0, 16), 256, ["TB", "OB", "BE0", "CP", "CX", "ONEd"], ["ptA"])
        uL, uk = T["U%d" % v][:, lc], "U%d_%d" % (v, tp)
        tt(uL, PT[:, 464:472], T.TL[:], ALU.max, 8, ["TL"], ["ptA", uk])
        if v == NV - 1:
            lin(T.UF[:, lc], uL, 1.0, 0.0, 8, [uk], ["UF_%d" % tp])
        send_list(v, tp, 1)
        tt(T.YY[:], Iwin.indirect(uL), T.MB[:], ALU.mult, 128, IDK + [uk, "MB"], ["YY"], GAT)
        tt(Fwin.indirect(T.IX1[:, 0:8]), T.YY[:], T.FS[:], ALU.max, 128, ["IXs", "YY", "FS"], FK, SCA)
        mm(ranks(472, 1, 24) + [(PT[:, 480:488], T.OB[:], T.ONE[:, 32:40], True, False), (PT[:, 480:488], T.BE[:, 128:256], cpv, False, True)], 384,
           ["TB", "OB", "BE1", "CP", "CX", "ONEe", "ONEf"], ["ptC"])
        tt(T.IX2[:, 0:16], PT[:, 472:488], T.DUM[:], ALU.min, 16, ["DUM", "DUMb"], ["ptC", "IXd"])
        cp(Fwin.indirect(T.IX2[:, 0:8]), T.WDN[:], 128, ["IXd", "WDN"], FK, SCA)
        tt(T.IX2[:, 16:24], T.IX2[:, 8:16], T.TL[:], ALU.max, 8, ["IXd", "TL"], ["IXu"])
        lin(T.H0[:], T.GT[:], 0.5, -0.25, 128, ["GT"], ["H0"])
        ts(T.HF[:], T.H0[:], MAGIC, MAGIC, ALU.add, ALU.subtract, 128, ["H0"], ["HF"])
        cp(Cwin.indirect(T.IX2[:, 0:8]), T.HF[:], 128, ["IXd", "HF"], CK, SCA)
        tt(Cwin.indirect(T.IX2[:, 16:24]), T.GT[:], T.HF[:], ALU.subtract, 128, ["IXu", "GT", "HF"], CK, SCA)

    for v in range(NV):
        for ch in chunks(v):
            for step in range(3):
                tag[0] = ch[0] + str(v)
                if ch[0] == "T" and step == 2:
                    stage1(v)
                walk(v, ch, step)
        tag[0] = "t" + str(v)
        train(v)
    tag[0] = "o"
    dma("S", [(T.yp[r:128:16, 0:V0], T.F[r:128:16, 0:V0]) for r in (12, 13)] +
        [(T.yp[16 * g:16 * g + 14, V0:DUMMY], T.F[16 * g:16 * g + 14, V0:DUMMY]) for g in range(4)], "outs", FK, ["ypb"], 2.5)
    dma("A", [(T.yp[16 * g:16 * g + 14, V0:DUMMY], T.F[16 * g:16 * g + 14, V0:DUMMY]) for g in range(4, 8)], "outs", FK, ["ypd"], 2.5)
    dma("S", [(T.yp[r:128:16, 0:DUMMY], T.CN[r:128:16, 0:DUMMY]) for r in (14, 15)], "outs", CK, ["ypc"], 2.5)
    bl = blocks(NV - 1)
    for (pos, n) in [q for ch in chunks(NV - 1) for p in ch[4] for q in halves(p[0], p[1])]:
        lin(T.XS[:, cs(pos, n)], T["X%d" % NV][:, cs(pos, n)], 1.0, C(XM), 128 * n, bk("X%d" % NV, pos, n) + k_(XM), bk("XF", pos, n), 1.0, 0.5)
        dma("S", [(T.yx[:, cs(b, k)], T.XS[:, cs(a, k)]) for (a, b, k) in runs(pos, n, bl)], "outs", bk("XF", pos, n), ["yx%d" % pos], 2.3 + 0.125 * n)
    for ch in chunks(NV - 1):
        dma("A", [(T.ys[:, ls(b, k)], T.YS[:, ls(a, k)]) for (a, b, k) in runs(ch[2], ch[3], bl)], "outs", bk("YS", ch[2], ch[3]), ["ys" + ch[0]], 2.4)
    return ops, neng


def depend(ops):
    lastw, readers, deps = {}, {}, []
    for i, o in enumerate(ops):
        d = set()
        for k in o["rd"]:
            if k in lastw:
                d.add(lastw[k])
        for k in o["wr"]:
            if k in lastw:
                d.add(lastw[k])
            d.update(readers.get(k, []))
        d.discard(i)
        deps.append(sorted(d))
        for k in o["rd"]:
            readers.setdefault(k, []).append(i)
        for k in o["wr"]:
            lastw[k] = i
            readers[k] = []
    return deps


def plan(ops):
    deps = depend(ops)
    nums = [int(x) for x in ORDER.split()]
    order, asg = [abs(x) for x in nums], [0] * len(ops)
    for x in nums:
        asg[abs(x)] = 1 if x < 0 else 0
    assert sorted(order) == list(range(len(ops)))
    last = {}
    for i in order:
        b = ops[i]["bank"]
        if b:
            if b in last and ops[last[b]]["opts"][asg[last[b]]][0] != ops[i]["opts"][asg[i]][0]:
                deps[i] = sorted(set(deps[i] + [last[b]]))
            last[b] = i
    return order, deps, asg


def rank_program(g, core, T, topo):
    rank = T.rank_of(core)
    if rank is None:
        return
    nxt = T.cores[(rank + 1) % len(T.cores)]
    assert topo.may_write(core, nxt)
    ops, neng = build(T, topo, core, nxt)
    order, deps, asg = plan(ops)
    spot = {i: k for k, i in enumerate(order)}
    eng = {"V": g.vector, "A": g.scalar, "P": g.tensor, "G": g, "S": g.sync}
    count, token, clock = {}, {}, {}
    known = {q: {} for q in eng}
    nsent = 0
    for i in order:
        o = ops[i]
        q, fn = o["opts"][asg[i]][0], o["opts"][asg[i]][2]
        if fn is None:
            token[i] = ("qG", 0)
            continue
        kn = known[q]
        need = {}
        for j in deps[i]:
            s, val = token[j]
            if j != o["cont"] and kn.get(s, 0) < val and need.get(s, (0, 0))[0] < val:
                need[s] = (val, j)
        for s, (val, j) in sorted(need.items(), key=lambda e: -spot[e[1][1]]):
            if kn.get(s, 0) < val:
                eng[q].wait_ge(T.sem[s], val)
                kn[s] = val
                for s2, v2 in clock[j].items():
                    if kn.get(s2, 0) < v2:
                        kn[s2] = v2
        r = fn(g)
        s = o["sem"] or "q" + q
        count[s] = count.get(s, 0) + o["n"]
        if o["sem"] is None:
            r.then_inc(T.sem[s], 1)
        token[i] = (s, count[s])
        remote = o["sem"] is not None and q == "G"
        nsent += 1 if remote else 0
        clock[i] = {} if remote else dict(kn)
    for s in sorted(count):
        if max(known[q].get(s, 0) for q in known) < count[s]:
            g.wait_ge(T.sem[s], count[s])
    g.wait_ge(T.sem.sent, nsent * neng)
